import numpy as np
import ml_dtypes


def mxq(x, axis, fmt="e4m3"):
    dtype, down = {"e4m3": (ml_dtypes.float8_e4m3fn, 7), "e5m2": (ml_dtypes.float8_e5m2, 14)}[fmt]
    v = np.moveaxis(np.asarray(x, np.float32).astype(ml_dtypes.bfloat16).astype(np.float64), axis, -1)
    blocks = v.reshape(v.shape[:-1] + (-1, 32))
    amax = np.abs(blocks).max(-1, keepdims=True)
    byte = np.maximum(np.where(amax > 0, np.frexp(amax)[1] - 1 + 127, 0) - down, 1)
    scale = np.exp2(byte - 127.0)
    codes = (blocks / scale).astype(np.float32).astype(dtype).astype(np.float64)
    return np.moveaxis((codes * scale).reshape(v.shape), -1, axis)


WIDE = False


def mx_kscale(k):
    if not WIDE:
        return np.ones(k)
    levels = np.array([10, -10, 5, -5, 0])
    if k % 512:
        return np.exp2(np.random.permutation(np.resize(levels, k // 32))).repeat(32)
    a = np.empty((k // 512, 16))
    for p in range(k // 512):
        a[p, :8] = np.random.permutation(np.resize(levels, 8))
        for g in range(8):
            far = levels[np.abs(levels - a[p, g]) >= 10]
            a[p, g + 8] = far[np.random.randint(len(far))]
    return np.exp2(a.ravel()).repeat(32)


def f64(x):
    return np.asarray(x).astype(np.float64)


def striped(idx):
    return np.tile(idx.reshape(-1, 16).T, (8, 1)).astype(np.uint16)


def unstriped(offs):
    return offs[:16].T.reshape(-1).astype(np.int64)


E2M1 = np.array([0.0, 0.5, 1.0, 1.5, 2.0, 3.0, 4.0, 6.0, -0.0, -0.5, -1.0, -1.5, -2.0, -3.0, -4.0, -6.0])


def pack_weight(w, fmt):
    k, n = w.shape
    w = f64(np.asarray(w, np.float32).astype(ml_dtypes.bfloat16)).reshape(k // 32, 32, n)
    amax = np.abs(w).max(1)
    if fmt == "e4m3":
        byte = np.frexp(amax)[1] - 1 + 127 - 7
    else:
        mant, ex = np.frexp(amax / 6.0)
        byte = np.where(mant > 0.5, ex, ex - 1) + 127
    byte = np.clip(np.where(amax > 0, byte, 1), 1, 254)
    scaled = (w * np.exp2(127.0 - byte)[:, None, :]).reshape(k, n).astype(np.float32)
    by_word = np.ascontiguousarray(scaled.reshape(k // 512, 128, 4, n).transpose(0, 1, 3, 2))
    if fmt == "e4m3":
        words = by_word.astype(ml_dtypes.float8_e4m3fn).view(np.uint8)
    else:
        c = by_word.astype(ml_dtypes.float4_e2m1fn).view(np.uint8) & 0xF
        words = (c[..., 0::2] | (c[..., 1::2] << 4)).reshape(k // 512, 128, 2 * n)
    return np.ascontiguousarray(words), np.ascontiguousarray(byte.astype(np.uint8).reshape(k // 512, 16, n))


def unpack_weight(words, scales, fmt):
    g, _, n = scales.shape
    words = np.ascontiguousarray(words).reshape(g, 128, n, -1)
    if fmt == "e4m3":
        vals = words.view(ml_dtypes.float8_e4m3fn).astype(np.float64)
    else:
        nib = np.empty((g, 128, n, 4), np.uint8)
        nib[..., 0::2] = words & 0xF
        nib[..., 1::2] = words >> 4
        vals = E2M1[nib]
    vals = vals * np.repeat(np.exp2(scales.astype(np.float64) - 127.0), 8, axis=1)[..., None]
    return vals.transpose(0, 1, 3, 2).reshape(g * 512, n)


def gelu(v):
    return 0.5 * v * (1.0 + np.tanh(np.sqrt(2.0 / np.pi) * (v + 0.044715 * v**3)))


K, K1, K2, H, N, T, S, P = 1536, 1024, 512, 1024, 512, 4096, 1024, 512

def setup_inputs():
    n = np.random.standard_normal
    s = mx_kscale(K)[:, None]
    u = mx_kscale(H)[:, None]
    tab_words, tab_scales = pack_weight(n((K, T)) * s, "e4m3")
    w1 = (0.7 * n((K1, H)) / np.sqrt(K1) / s[:K1]).astype(np.float32)
    w2_words, w2_scales = pack_weight(0.7 * n((K2, H)) / np.sqrt(K2) / s[K1:], "e2m1")
    bias = (0.5 * n(H)).astype(np.float32)
    gain = (np.exp(0.3 * n(H)) * u[:, 0]).astype(np.float32)
    w3_words, w3_scales = pack_weight(n((H, N)) / np.sqrt(H) / u, "e4m3")
    return {"tab_words": tab_words, "tab_scales": tab_scales,
            "offs": striped(np.random.permutation(T)[:S]),
            "pos1": striped(np.random.permutation(S)[:P]),
            "pos2": striped(np.random.permutation(S)[:P]),
            "pos3": striped(np.random.permutation(S)[:P]),
            "w1": w1, "w2_words": w2_words, "w2_scales": w2_scales,
            "bias": bias, "gain": gain,
            "w3_words": w3_words, "w3_scales": w3_scales}

def reference(tab_words, tab_scales, offs, pos1, pos2, pos3, w1, w2_words, w2_scales,
              bias, gain, w3_words, w3_scales):
    v = unpack_weight(tab_words, tab_scales, "e4m3")[:, unstriped(offs)]
    w1q = mxq(f64(w1), 0, "e4m3")
    w2q = unpack_weight(w2_words, w2_scales, "e2m1")
    d = w1q.T @ v[:K1] + w2q.T @ v[K1:]
    h = np.tanh(d + f64(bias)[:, None])
    lower = h[:, unstriped(pos1)]
    hearth = h[:, unstriped(pos2)]
    upper = h[:, unstriped(pos3)]
    z = (np.square(lower) * hearth + upper) * f64(gain)[:, None]
    w3q = unpack_weight(w3_words, w3_scales, "e4m3")
    return w3q.T @ mxq(z, 0, "e4m3")

@@ -1,0 +1,289 @@
+from contextlib import ExitStack
+
+import concourse.mybir as mybir
+
+K1, K2, H, N, T, S, M = 1024, 512, 1024, 512, 4096, 1024, 512
+FLOPS = 2 * (K1 + K2) * H * S + 2 * H * N * M
+
+F32 = mybir.dt.float32
+BF16 = mybir.dt.bfloat16
+I32 = mybir.dt.int32
+U32 = mybir.dt.uint32
+U16 = mybir.dt.uint16
+U8 = mybir.dt.uint8
+FP8X4 = mybir.dt.float8_e4m3fn_x4
+FP4X4 = mybir.dt.float4_e2m1fn_x4
+ACT = mybir.ActivationFunctionType
+ALU = mybir.AluOpType
+
+P = 128
+PACK = 4
+KP = P * PACK
+BANK = 512
+
+
+def tile_list_site_phasing_kernel(tc, tab_words, tab_scales, offs, pos1, pos2, pos3, w1, w2_words,
+                                            w2_scales, bias, gain, w3_words, w3_scales, out):
+    nc = tc.nc
+    with ExitStack() as ctx:
+        keep = ctx.enter_context(tc.tile_pool(name="keep", bufs=1))
+        work = ctx.enter_context(tc.tile_pool(name="work", bufs=2))
+        psum = ctx.enter_context(tc.psum_pool(name="psum", bufs=1))
+
+        def load_list(src, name):
+            tile = keep.tile(list(src.shape), U16, name=name)
+            nc.sync.dma_start(tile[:], src)
+            return tile
+
+        def load_table(a):
+            tile = keep.tile([P, T], U32, name="table%d" % a, align_bytes=64)
+            nc.sync.dma_start(tile[:].bitcast(I32), tab_words[a].rearrange("p t i -> p (t i)").bitcast(I32))
+            return tile
+
+        def load_w1(a, b, c0, c1):
+            tile = keep.tile([P, PACK, c1 - c0], F32, name="w1_raw%d%d_%d" % (a, b, c0))
+            rows = w1[b * KP:(b + 1) * KP, a * KP + c0:a * KP + c1]
+            nc.sync.dma_start(tile[:], rows.rearrange("(p j) c -> p j c", j=PACK))
+            return tile
+
+        tab_planes = keep.tile([P, T], U8, name="tab_planes", tag="first_window", align_bytes=64)
+        w2_plane_raw = keep.tile([P, H], U8, name="w2_plane_raw", align_bytes=64)
+        w3_planes = keep.tile([P, N], U8, name="w3_planes", align_bytes=64)
+        v2_plane = keep.tile([P, S], U8, name="v2_plane", align_bytes=64)
+        for plane in (tab_planes, w2_plane_raw, w3_planes, v2_plane):
+            nc.vector.memset(plane[:].bitcast(I32), 0)
+        for q in range(4):
+            nc.gpsimd.dma_start(tab_planes[32 * q:32 * q + 12, :].bitcast(I32),
+                                tab_scales[:, 4 * q:4 * q + 4, :].bitcast(I32))
+        for q in range(4):
+            nc.gpsimd.dma_start(w2_plane_raw[32 * q:32 * q + 4, :].bitcast(I32),
+                                w2_scales[0, 4 * q:4 * q + 4, :].bitcast(I32))
+
+        warm = keep.tile([P, 2], F32, name="warm")
+        nc.vector.memset(warm[:], 0.0)
+        nc.scalar.activation(warm[:, 1:2], warm[:, 0:1], ACT.Tanh)
+
+        offs_t = load_list(offs, "offs_t")
+        table = [load_table(0)]
+        w2_raw = keep.tile([P, 2 * H], U8, name="w2_raw", align_bytes=64)
+        nc.sync.dma_start(w2_raw[:].bitcast(I32), w2_words[0].bitcast(I32))
+        w1_raw = {(0, 0): load_w1(0, 0, 0, KP)}
+        table.append(load_table(1))
+        table.append(load_table(2))
+        w1_last = [load_w1(0, 1, 0, KP // 2), load_w1(0, 1, KP // 2, KP)]
+        bias_t = keep.tile([P, 2, PACK], F32, name="bias_t")
+        gain_t = keep.tile([P, 2, PACK], F32, name="gain_t")
+        nc.sync.dma_start(bias_t[:], bias.rearrange("(a p t) -> p a t", p=P, t=PACK))
+        p1 = load_list(pos1, "p1")
+        p2 = load_list(pos2, "p2")
+        p3 = load_list(pos3, "p3")
+        nc.sync.dma_start(gain_t[:], gain.rearrange("(a p t) -> p a t", p=P, t=PACK))
+        w1_raw[1, 0] = load_w1(1, 0, 0, KP)
+        w1_raw[1, 1] = load_w1(1, 1, 0, KP)
+        w3_codes = keep.tile([P, 2, N], U32, name="w3_codes", align_bytes=64)
+        nc.sync.dma_start(w3_codes[:].bitcast(I32), w3_words.rearrange("a p c i -> p a (c i)").bitcast(I32))
+
+        w2_codes = keep.tile([P, 2 * H], U8, name="w2_codes", align_bytes=64)
+        w2_plane = keep.tile([P, H], U8, name="w2_plane", align_bytes=64)
+        nc.vector.tensor_copy(w2_codes[:].bitcast(U16).rearrange("p (a t m) -> p a t m", a=2, t=PACK),
+                              w2_raw[:].bitcast(U16).rearrange("p (a m t) -> p a t m", a=2, t=PACK))
+
+        v_planes = keep.tile([P, S], U8, name="v_planes", align_bytes=64)
+        nc.vector.tensor_copy(v_planes[:], tab_planes[:].indirect(offs_t[:]))
+        nc.gpsimd.dma_start(v2_plane[0:120, :].bitcast(I32), v_planes[8:128, :].bitcast(I32))
+        for q in range(4):
+            nc.gpsimd.dma_start(w3_planes[32 * q:32 * q + 8, :].bitcast(I32),
+                                w3_scales[:, 4 * q:4 * q + 4, :].bitcast(I32))
+
+        def gather_table(a):
+            tile = keep.tile([P, S], U32, name="v_codes%d" % a, align_bytes=64,
+                             tag="first_window" if a == 0 else "v_codes%d" % a)
+            nc.vector.tensor_copy(tile[:], table[a][:].indirect(offs_t[:]))
+            return tile
+
+        w1_q = {}
+
+        def new_rounded(a, b):
+            return keep.tile([P, PACK, P, PACK], BF16, name="w1_rounded%d%d" % (a, b), align_bytes=64,
+                             tag="shared%d" % b if a == 1 else "w1_rounded%d" % b)
+
+        def round_w1(copy, rounded, m0, raw):
+            src = raw.rearrange("p j (m t) -> p m t j", t=PACK)
+            copy(rounded[:].rearrange("p t m j -> p m t j")[:, m0:m0 + src.shape[1]], src)
+
+        def quantize_w1(a, b, rounded, pieces):
+            codes = keep.tile([P, KP], U32, name="w1_codes%d%d" % (a, b), align_bytes=64)
+            plane = keep.tile([P, KP], U8, name="w1_plane%d%d" % (a, b), align_bytes=64)
+            flat = rounded[:].rearrange("p t m j -> p (t m j)")
+            w = KP // pieces
+            for i in range(pieces):
+                nc.vector.quantize_mx(out=codes[:, i * w:(i + 1) * w].bitcast(FP8X4), scales=plane[:, i * w:(i + 1) * w],
+                                      in_=flat[:, PACK * i * w:PACK * (i + 1) * w])
+            w1_q[a, b] = (codes, plane)
+
+        rounded = {(0, b): new_rounded(0, b) for b in range(2)}
+        v_codes = [gather_table(0)]
+        nc.vector.tensor_copy(w2_plane[:].rearrange("p (a t m) -> p a t m", a=2, t=PACK),
+                              w2_plane_raw[:].rearrange("p (a m t) -> p a t m", a=2, t=PACK))
+        round_w1(nc.scalar.copy, rounded[0, 0], 0, w1_raw[0, 0][:])
+        v_codes.append(gather_table(1))
+        quantize_w1(0, 0, rounded[0, 0], 1)
+        v_codes.append(gather_table(2))
+        round_w1(nc.scalar.copy, rounded[0, 1], 0, w1_last[0][:])
+        round_w1(nc.vector.tensor_copy, rounded[0, 1], P // 2, w1_last[1][:])
+        quantize_w1(0, 1, rounded[0, 1], PACK)
+
+        def bank(i):
+            return psum.tile([P, BANK], F32, name="bank%d" % i)
+
+        def first_pass(acc, a, t, half, which, start, stop):
+            cols = slice(half * BANK, (half + 1) * BANK)
+            if which == 2:
+                c0 = a * KP + t * P
+                nc.tensor.matmul_mx(out=acc[:], lhsT=w2_codes[:, 2 * c0:2 * (c0 + P)].bitcast(FP4X4),
+                                    lhsT_scale=w2_plane[:, c0:c0 + P], rhs=v_codes[2][:, cols].bitcast(FP8X4),
+                                    rhs_scale=v2_plane[:, cols], start=start, stop=stop)
+            else:
+                codes, plane = w1_q[a, which]
+                nc.tensor.matmul_mx(out=acc[:], lhsT=codes[:, t * P:(t + 1) * P].bitcast(FP8X4),
+                                    lhsT_scale=plane[:, t * P:(t + 1) * P], rhs=v_codes[which][:, cols].bitcast(FP8X4),
+                                    rhs_scale=v_planes[4 * which:P, cols], start=start, stop=stop)
+
+        order = (0, 2, 1)
+        accs = {}
+        for t in range(PACK):
+            for half in range(2):
+                accs[0, t, half] = bank(2 * t + half)
+        for i, which in enumerate(order):
+            for t in range(PACK):
+                for half in range(2):
+                    first_pass(accs[0, t, half], 0, t, half, which, i == 0, i == 2)
+
+        def multiply(s):
+            a, t = divmod(s, PACK)
+            for half in range(2):
+                accs[a, t, half] = bank(2 * (t % 2) + half)
+                for i, which in enumerate(order):
+                    first_pass(accs[a, t, half], a, t, half, which, i == 0, i == 2)
+
+        h = {}
+        lower = {}
+        sq = {}
+        total = {}
+        zb = [keep.tile([P, PACK, M], BF16, name="zb%d" % a, align_bytes=64) for a in range(2)]
+        HALF = M // 2
+        halves = [(slice(u * HALF, (u + 1) * HALF), slice(u * HALF // 16, (u + 1) * HALF // 16)) for u in range(2)]
+
+        def activate(s):
+            a, t = divmod(s, PACK)
+            if a == 1:
+                multiply(s)
+            h[s] = work.tile([P, S], F32, name="h", bufs=4)
+            for half in range(2):
+                nc.scalar.activation(h[s][:, half * BANK:(half + 1) * BANK], accs[a, t, half][:], ACT.Tanh,
+                                     bias=bias_t[:, a, t:t + 1])
+            if s < 2:
+                lower[s] = keep.tile([P, M], F32, name="lower%d" % s, tag="shared%d" % s, align_bytes=64)
+            else:
+                lower[s] = work.tile([P, M], F32, name="lower", bufs=4)
+            nc.vector.tensor_copy(lower[s][:], h[s][:].indirect(p1[:]))
+
+        def combine(s):
+            sq = work.tile([P, M], F32, name="sq", bufs=3)
+            nc.scalar.activation(sq[:], lower[s][:], ACT.Square)
+            prod = work.tile([P, M], F32, name="prod", bufs=3)
+            for cols, entries in halves:
+                nc.vector.tensor_tensor(prod[:, cols], h[s][:].indirect(p2[:, entries]), sq[:, cols], ALU.mult)
+            total[s] = work.tile([P, M], F32, name="total", bufs=4)
+            for cols, entries in halves:
+                nc.vector.tensor_tensor(total[s][:, cols], h[s][:].indirect(p3[:, entries]), prod[:, cols], ALU.add)
+
+        def scale(s, cols):
+            a, t = divmod(s, PACK)
+            nc.scalar.activation(zb[a][:, t, cols], total[s][:, cols], ACT.Copy, scale=gain_t[:, a, t:t + 1])
+
+        woven = [keep.tile([P, M, PACK], BF16, name="woven%d" % a, align_bytes=64) for a in range(2)]
+        z_codes = [keep.tile([P, M], U32, name="z_codes%d" % a, align_bytes=64) for a in range(2)]
+        z_plane = [keep.tile([P, M], U8, name="z_plane%d" % a, align_bytes=64) for a in range(2)]
+
+        def weave(copy, a, cols):
+            copy(woven[a][:, cols, :].rearrange("p (c i) t -> p c t i", i=4),
+                 zb[a][:, :, cols].rearrange("p t (c i) -> p c t i", i=4))
+
+        def quantize_z(a, cols):
+            nc.vector.quantize_mx(out=z_codes[a][:, cols].bitcast(FP8X4), scales=z_plane[a][:, cols],
+                                  in_=woven[a][:, cols, :].rearrange("p m t -> p (m t)"))
+
+        outs = {}
+
+        def second(a, u):
+            cols = halves[u][0]
+            for n in range(4):
+                if a == 0:
+                    outs[u, n] = psum.tile([P, HALF], F32, name="bank%d" % (4 * (1 - u) + n))
+                nc.tensor.matmul_mx(out=outs[u, n][:], lhsT=w3_codes[:, a, n * P:(n + 1) * P].bitcast(FP8X4),
+                                    lhsT_scale=w3_planes[4 * a:P, n * P:(n + 1) * P],
+                                    rhs=z_codes[a][:, cols].bitcast(FP8X4), rhs_scale=z_plane[a][:, cols],
+                                    start=(a == 0), stop=(a == 1))
+
+        def store(u):
+            cols = halves[u][0]
+            for pair, copy in enumerate((nc.scalar.copy, nc.vector.tensor_copy)):
+                result = keep.tile([P, 2, HALF], F32, name="result%d%d" % (u, pair))
+                for i in range(2):
+                    copy(result[:, i, :], outs[u, 2 * pair + i][:])
+                rows = out[2 * pair * P:(2 * pair + 2) * P, cols]
+                nc.sync.dma_start(rows.rearrange("(n p) m -> p n m", p=P), result[:])
+
+        def round_half(b, u):
+            if u == 0:
+                rounded[1, b] = new_rounded(1, b)
+            round_w1(nc.scalar.copy, rounded[1, b], u * P // 2, w1_raw[1, b][:, :, u * KP // 2:(u + 1) * KP // 2])
+
+        whole = slice(0, M)
+        activate(0)
+        activate(1)
+        combine(0)
+        round_half(0, 0)
+        activate(2)
+        combine(1)
+        round_half(0, 1)
+        quantize_w1(1, 0, rounded[1, 0], 1)
+        activate(3)
+        round_half(1, 0)
+        combine(2)
+        round_half(1, 1)
+        quantize_w1(1, 1, rounded[1, 1], 1)
+        combine(3)
+        scale(0, whole)
+        scale(1, whole)
+        activate(4)
+        activate(5)
+        scale(2, whole)
+        combine(4)
+        scale(3, whole)
+        activate(6)
+        weave(nc.scalar.copy, 0, halves[0][0])
+        combine(5)
+        activate(7)
+        weave(nc.scalar.copy, 0, halves[1][0])
+        combine(6)
+        quantize_z(0, whole)
+        second(0, 0)
+        second(0, 1)
+        scale(4, whole)
+        scale(5, whole)
+        combine(7)
+        scale(6, whole)
+        scale(7, halves[0][0])
+        weave(nc.scalar.copy, 1, slice(0, 96))
+        weave(nc.vector.tensor_copy, 1, slice(96, HALF))
+        scale(7, halves[1][0])
+        quantize_z(1, halves[0][0])
+        second(1, 0)
+        weave(nc.scalar.copy, 1, slice(HALF, HALF + 96))
+        weave(nc.vector.tensor_copy, 1, slice(HALF + 96, M))
+        quantize_z(1, halves[1][0])
+        second(1, 1)
+        store(0)
+        store(1)

@@ -27,6 +27,7 @@ def tile_list_site_phasing_kernel(tc, tab_words, tab_scales, offs, pos1, pos2, p
     nc = tc.nc
     with ExitStack() as ctx:
         keep = ctx.enter_context(tc.tile_pool(name="keep", bufs=1))
+        reuse = ctx.enter_context(tc.tile_pool(name="reuse", bufs=1))
         work = ctx.enter_context(tc.tile_pool(name="work", bufs=2))
         psum = ctx.enter_context(tc.psum_pool(name="psum", bufs=1))
 
@@ -36,7 +37,7 @@ def tile_list_site_phasing_kernel(tc, tab_words, tab_scales, offs, pos1, pos2, p
             return tile
 
         def load_table(a):
-            tile = keep.tile([P, T], U32, name="table%d" % a, align_bytes=64)
+            tile = reuse.tile([P, T], U32, name="table%d" % a, align_bytes=64, offset=4 * T * a)
             nc.sync.dma_start(tile[:].bitcast(I32), tab_words[a].rearrange("p t i -> p (t i)").bitcast(I32))
             return tile
 
@@ -46,8 +47,8 @@ def tile_list_site_phasing_kernel(tc, tab_words, tab_scales, offs, pos1, pos2, p
             nc.sync.dma_start(tile[:], rows.rearrange("(p j) c -> p j c", j=PACK))
             return tile
 
-        tab_planes = keep.tile([P, T], U8, name="tab_planes", tag="first_window", align_bytes=64)
-        w2_plane_raw = keep.tile([P, H], U8, name="w2_plane_raw", align_bytes=64)
+        tab_planes = reuse.tile([P, T], U8, name="tab_planes", align_bytes=64, offset=12 * T)
+        w2_plane_raw = reuse.tile([P, H], U8, name="w2_plane_raw", align_bytes=64, offset=13 * T)
         w3_planes = keep.tile([P, N], U8, name="w3_planes", align_bytes=64)
         v2_plane = keep.tile([P, S], U8, name="v2_plane", align_bytes=64)
         for plane in (tab_planes, w2_plane_raw, w3_planes, v2_plane):
@@ -64,22 +65,22 @@ def tile_list_site_phasing_kernel(tc, tab_words, tab_scales, offs, pos1, pos2, p
         nc.scalar.activation(warm[:, 1:2], warm[:, 0:1], ACT.Tanh)
 
         offs_t = load_list(offs, "offs_t")
-        table = [load_table(0)]
         w2_raw = keep.tile([P, 2 * H], U8, name="w2_raw", align_bytes=64)
         nc.sync.dma_start(w2_raw[:].bitcast(I32), w2_words[0].bitcast(I32))
+        table = {0: load_table(0)}
         w1_raw = {(0, 0): load_w1(0, 0, 0, KP)}
-        table.append(load_table(1))
-        table.append(load_table(2))
-        w1_last = [load_w1(0, 1, 0, KP // 2), load_w1(0, 1, KP // 2, KP)]
+        table[2] = load_table(2)
+        table[1] = load_table(1)
+        w1_raw[0, 1] = load_w1(0, 1, 0, KP)
         bias_t = keep.tile([P, 2, PACK], F32, name="bias_t")
         gain_t = keep.tile([P, 2, PACK], F32, name="gain_t")
         nc.sync.dma_start(bias_t[:], bias.rearrange("(a p t) -> p a t", p=P, t=PACK))
         p1 = load_list(pos1, "p1")
         p2 = load_list(pos2, "p2")
         p3 = load_list(pos3, "p3")
-        nc.sync.dma_start(gain_t[:], gain.rearrange("(a p t) -> p a t", p=P, t=PACK))
         w1_raw[1, 0] = load_w1(1, 0, 0, KP)
         w1_raw[1, 1] = load_w1(1, 1, 0, KP)
+        nc.sync.dma_start(gain_t[:], gain.rearrange("(a p t) -> p a t", p=P, t=PACK))
         w3_codes = keep.tile([P, 2, N], U32, name="w3_codes", align_bytes=64)
         nc.sync.dma_start(w3_codes[:].bitcast(I32), w3_words.rearrange("a p c i -> p a (c i)").bitcast(I32))
 
@@ -88,31 +89,28 @@ def tile_list_site_phasing_kernel(tc, tab_words, tab_scales, offs, pos1, pos2, p
         nc.vector.tensor_copy(w2_codes[:].bitcast(U16).rearrange("p (a t m) -> p a t m", a=2, t=PACK),
                               w2_raw[:].bitcast(U16).rearrange("p (a m t) -> p a t m", a=2, t=PACK))
 
-        v_planes = keep.tile([P, S], U8, name="v_planes", align_bytes=64)
-        nc.vector.tensor_copy(v_planes[:], tab_planes[:].indirect(offs_t[:]))
-        nc.gpsimd.dma_start(v2_plane[0:120, :].bitcast(I32), v_planes[8:128, :].bitcast(I32))
-        for q in range(4):
-            nc.gpsimd.dma_start(w3_planes[32 * q:32 * q + 8, :].bitcast(I32),
-                                w3_scales[:, 4 * q:4 * q + 4, :].bitcast(I32))
-
         def gather_table(a):
-            tile = keep.tile([P, S], U32, name="v_codes%d" % a, align_bytes=64,
-                             tag="first_window" if a == 0 else "v_codes%d" % a)
+            tile = reuse.tile([P, S], U32, name="v_codes%d" % a, align_bytes=64, offset=(12 * T, 13 * T, 0)[a])
             nc.vector.tensor_copy(tile[:], table[a][:].indirect(offs_t[:]))
             return tile
 
         w1_q = {}
 
         def new_rounded(a, b):
+            if (a, b) == (0, 1):
+                return reuse.tile([P, PACK, P, PACK], BF16, name="w1_rounded01", align_bytes=64, offset=4 * T)
             return keep.tile([P, PACK, P, PACK], BF16, name="w1_rounded%d%d" % (a, b), align_bytes=64,
                              tag="shared%d" % b if a == 1 else "w1_rounded%d" % b)
 
         def round_w1(copy, rounded, m0, raw):
-            src = raw.rearrange("p j (m t) -> p m t j", t=PACK)
-            copy(rounded[:].rearrange("p t m j -> p m t j")[:, m0:m0 + src.shape[1]], src)
+            src = raw.rearrange("p j (m t) -> p m j t", t=PACK)
+            copy(rounded[:].rearrange("p t m j -> p m j t")[:, m0:m0 + src.shape[1]], src)
 
         def quantize_w1(a, b, rounded, pieces):
-            codes = keep.tile([P, KP], U32, name="w1_codes%d%d" % (a, b), align_bytes=64)
+            if (a, b) == (0, 0):
+                codes = reuse.tile([P, KP], U32, name="w1_codes00", align_bytes=64, offset=T)
+            else:
+                codes = keep.tile([P, KP], U32, name="w1_codes%d%d" % (a, b), align_bytes=64)
             plane = keep.tile([P, KP], U8, name="w1_plane%d%d" % (a, b), align_bytes=64)
             flat = rounded[:].rearrange("p t m j -> p (t m j)")
             w = KP // pieces
@@ -121,16 +119,24 @@ def tile_list_site_phasing_kernel(tc, tab_words, tab_scales, offs, pos1, pos2, p
                                       in_=flat[:, PACK * i * w:PACK * (i + 1) * w])
             w1_q[a, b] = (codes, plane)
 
-        rounded = {(0, b): new_rounded(0, b) for b in range(2)}
-        v_codes = [gather_table(0)]
+        rounded = {(0, 0): new_rounded(0, 0)}
+        v_planes = keep.tile([P, S], U8, name="v_planes", align_bytes=64)
+        nc.vector.tensor_copy(v_planes[:], tab_planes[:].indirect(offs_t[:]))
+        nc.gpsimd.dma_start(v2_plane[0:120, :].bitcast(I32), v_planes[8:128, :].bitcast(I32))
+        for q in range(4):
+            nc.gpsimd.dma_start(w3_planes[32 * q:32 * q + 8, :].bitcast(I32),
+                                w3_scales[:, 4 * q:4 * q + 4, :].bitcast(I32))
+        v_codes = {0: gather_table(0)}
+
+        round_w1(nc.scalar.copy, rounded[0, 0], 0, w1_raw[0, 0][:])
+        quantize_w1(0, 0, rounded[0, 0], 1)
+        v_codes[2] = gather_table(2)
         nc.vector.tensor_copy(w2_plane[:].rearrange("p (a t m) -> p a t m", a=2, t=PACK),
                               w2_plane_raw[:].rearrange("p (a m t) -> p a t m", a=2, t=PACK))
-        round_w1(nc.scalar.copy, rounded[0, 0], 0, w1_raw[0, 0][:])
-        v_codes.append(gather_table(1))
-        quantize_w1(0, 0, rounded[0, 0], 1)
-        v_codes.append(gather_table(2))
-        round_w1(nc.scalar.copy, rounded[0, 1], 0, w1_last[0][:])
-        round_w1(nc.vector.tensor_copy, rounded[0, 1], P // 2, w1_last[1][:])
+        v_codes[1] = gather_table(1)
+        rounded[0, 1] = new_rounded(0, 1)
+        round_w1(nc.scalar.copy, rounded[0, 1], 0, w1_raw[0, 1][:, :, :PACK * 44])
+        round_w1(nc.vector.tensor_copy, rounded[0, 1], 44, w1_raw[0, 1][:, :, PACK * 44:])
         quantize_w1(0, 1, rounded[0, 1], PACK)
 
         def bank(i):

@@ -20,6 +20,23 @@ P = 128
 PACK = 4
 KP = P * PACK
 BANK = 512
+QUADRANTS = 4
+SLICES = H // P
+HALF = M // 2
+LANES = 16
+W2_PASS = 2
+PASS_ORDER = (0, W2_PASS, 1)
+
+ROUND_ON_SCALAR = 44
+WEAVE_ON_SCALAR = 80
+
+TABLE_BYTES = 4 * T
+AT_TABLE = (0, TABLE_BYTES, 2 * TABLE_BYTES)
+AT_TABLE_PLANES = 3 * TABLE_BYTES
+AT_W2_PLANE = AT_TABLE_PLANES + T
+AT_PICKED = (AT_TABLE_PLANES, AT_W2_PLANE, AT_TABLE[0])
+AT_FIRST_W1_CODES = AT_TABLE[0] + 4 * S
+AT_ROUNDED = (AT_TABLE[1], AT_TABLE[1] + 2 * PACK * KP)
 
 
 def tile_list_site_phasing_kernel(tc, tab_words, tab_scales, offs, pos1, pos2, pos3, w1, w2_words,
@@ -27,7 +44,7 @@ def tile_list_site_phasing_kernel(tc, tab_words, tab_scales, offs, pos1, pos2, p
     nc = tc.nc
     with ExitStack() as ctx:
         keep = ctx.enter_context(tc.tile_pool(name="keep", bufs=1))
-        reuse = ctx.enter_context(tc.tile_pool(name="reuse", bufs=1))
+        shared = ctx.enter_context(tc.tile_pool(name="shared", bufs=1))
         work = ctx.enter_context(tc.tile_pool(name="work", bufs=2))
         psum = ctx.enter_context(tc.psum_pool(name="psum", bufs=1))
 
@@ -37,259 +54,252 @@ def tile_list_site_phasing_kernel(tc, tab_words, tab_scales, offs, pos1, pos2, p
             return tile
 
         def load_table(a):
-            tile = reuse.tile([P, T], U32, name="table%d" % a, align_bytes=64, offset=4 * T * a)
+            tile = shared.tile([P, T], U32, name="table%d" % a, align_bytes=64, offset=AT_TABLE[a])
             nc.sync.dma_start(tile[:].bitcast(I32), tab_words[a].rearrange("p t i -> p (t i)").bitcast(I32))
             return tile
 
-        def load_w1(a, b, c0, c1):
-            tile = keep.tile([P, PACK, c1 - c0], F32, name="w1_raw%d%d_%d" % (a, b, c0))
-            rows = w1[b * KP:(b + 1) * KP, a * KP + c0:a * KP + c1]
+        def load_w1(a, b):
+            tile = keep.tile([P, PACK, KP], F32, name="w1_raw%d%d" % (a, b))
+            rows = w1[b * KP:(b + 1) * KP, a * KP:(a + 1) * KP]
             nc.sync.dma_start(tile[:], rows.rearrange("(p j) c -> p j c", j=PACK))
             return tile
 
-        tab_planes = reuse.tile([P, T], U8, name="tab_planes", align_bytes=64, offset=12 * T)
-        w2_plane_raw = reuse.tile([P, H], U8, name="w2_plane_raw", align_bytes=64, offset=13 * T)
+        def load_planes(queue, planes, scales):
+            rows = 4 * scales.shape[0]
+            for q in range(QUADRANTS):
+                queue.dma_start(planes[32 * q:32 * q + rows, :].bitcast(I32),
+                                scales[:, 4 * q:4 * q + 4, :].bitcast(I32))
+
+        table_planes = shared.tile([P, T], U8, name="table_planes", align_bytes=64, offset=AT_TABLE_PLANES)
+        w2_plane_raw = shared.tile([P, H], U8, name="w2_plane_raw", align_bytes=64, offset=AT_W2_PLANE)
         w3_planes = keep.tile([P, N], U8, name="w3_planes", align_bytes=64)
-        v2_plane = keep.tile([P, S], U8, name="v2_plane", align_bytes=64)
-        for plane in (tab_planes, w2_plane_raw, w3_planes, v2_plane):
+        picked_plane2 = keep.tile([P, S], U8, name="picked_plane2", align_bytes=64)
+        for plane in (table_planes, w2_plane_raw, w3_planes, picked_plane2):
             nc.vector.memset(plane[:].bitcast(I32), 0)
-        for q in range(4):
-            nc.gpsimd.dma_start(tab_planes[32 * q:32 * q + 12, :].bitcast(I32),
-                                tab_scales[:, 4 * q:4 * q + 4, :].bitcast(I32))
-        for q in range(4):
-            nc.gpsimd.dma_start(w2_plane_raw[32 * q:32 * q + 4, :].bitcast(I32),
-                                w2_scales[0, 4 * q:4 * q + 4, :].bitcast(I32))
+        load_planes(nc.gpsimd, table_planes, tab_scales)
+        load_planes(nc.gpsimd, w2_plane_raw, w2_scales)
 
         warm = keep.tile([P, 2], F32, name="warm")
         nc.vector.memset(warm[:], 0.0)
-        nc.scalar.activation(warm[:, 1:2], warm[:, 0:1], ACT.Tanh)
+        nc.scalar.activation(warm[:, 1:2], warm[:, 0:1], ACT.Sigmoid)
 
         offs_t = load_list(offs, "offs_t")
         w2_raw = keep.tile([P, 2 * H], U8, name="w2_raw", align_bytes=64)
         nc.sync.dma_start(w2_raw[:].bitcast(I32), w2_words[0].bitcast(I32))
         table = {0: load_table(0)}
-        w1_raw = {(0, 0): load_w1(0, 0, 0, KP)}
-        table[2] = load_table(2)
+        w1_raw = {(0, 0): load_w1(0, 0)}
+        table[W2_PASS] = load_table(W2_PASS)
         table[1] = load_table(1)
-        w1_raw[0, 1] = load_w1(0, 1, 0, KP)
+        w1_raw[0, 1] = load_w1(0, 1)
         bias_t = keep.tile([P, 2, PACK], F32, name="bias_t")
         gain_t = keep.tile([P, 2, PACK], F32, name="gain_t")
         nc.sync.dma_start(bias_t[:], bias.rearrange("(a p t) -> p a t", p=P, t=PACK))
         p1 = load_list(pos1, "p1")
         p2 = load_list(pos2, "p2")
         p3 = load_list(pos3, "p3")
-        w1_raw[1, 0] = load_w1(1, 0, 0, KP)
-        w1_raw[1, 1] = load_w1(1, 1, 0, KP)
+        w1_raw[1, 0] = load_w1(1, 0)
+        w1_raw[1, 1] = load_w1(1, 1)
         nc.sync.dma_start(gain_t[:], gain.rearrange("(a p t) -> p a t", p=P, t=PACK))
         w3_codes = keep.tile([P, 2, N], U32, name="w3_codes", align_bytes=64)
         nc.sync.dma_start(w3_codes[:].bitcast(I32), w3_words.rearrange("a p c i -> p a (c i)").bitcast(I32))
+        load_planes(nc.sync, w3_planes, w3_scales)
 
-        w2_codes = keep.tile([P, 2 * H], U8, name="w2_codes", align_bytes=64)
-        w2_plane = keep.tile([P, H], U8, name="w2_plane", align_bytes=64)
-        nc.vector.tensor_copy(w2_codes[:].bitcast(U16).rearrange("p (a t m) -> p a t m", a=2, t=PACK),
-                              w2_raw[:].bitcast(U16).rearrange("p (a m t) -> p a t m", a=2, t=PACK))
+        def in_slice_order(dst, src):
+            nc.vector.tensor_copy(dst.rearrange("p (a t m) -> p a t m", a=2, t=PACK),
+                                  src.rearrange("p (a m t) -> p a t m", a=2, t=PACK))
 
         def gather_table(a):
-            tile = reuse.tile([P, S], U32, name="v_codes%d" % a, align_bytes=64, offset=(12 * T, 13 * T, 0)[a])
+            tile = shared.tile([P, S], U32, name="picked_codes%d" % a, align_bytes=64, offset=AT_PICKED[a])
             nc.vector.tensor_copy(tile[:], table[a][:].indirect(offs_t[:]))
             return tile
 
-        w1_q = {}
+        def round_w1(copy, rounded, raw, m0, m1):
+            src = raw[:, :, PACK * m0:PACK * m1].rearrange("p j (m t) -> p m j t", t=PACK)
+            copy(rounded[:].rearrange("p t m j -> p m j t")[:, m0:m1], src)
 
-        def new_rounded(a, b):
-            if (a, b) == (0, 1):
-                return reuse.tile([P, PACK, P, PACK], BF16, name="w1_rounded01", align_bytes=64, offset=4 * T)
-            return keep.tile([P, PACK, P, PACK], BF16, name="w1_rounded%d%d" % (a, b), align_bytes=64,
-                             tag="shared%d" % b if a == 1 else "w1_rounded%d" % b)
-
-        def round_w1(copy, rounded, m0, raw):
-            src = raw.rearrange("p j (m t) -> p m j t", t=PACK)
-            copy(rounded[:].rearrange("p t m j -> p m j t")[:, m0:m0 + src.shape[1]], src)
-
-        def quantize_w1(a, b, rounded, pieces):
-            if (a, b) == (0, 0):
-                codes = reuse.tile([P, KP], U32, name="w1_codes00", align_bytes=64, offset=T)
-            else:
-                codes = keep.tile([P, KP], U32, name="w1_codes%d%d" % (a, b), align_bytes=64)
-            plane = keep.tile([P, KP], U8, name="w1_plane%d%d" % (a, b), align_bytes=64)
+        def quantize_w1(rounded, codes, name, pieces):
+            plane = keep.tile([P, KP], U8, name=name, align_bytes=64)
             flat = rounded[:].rearrange("p t m j -> p (t m j)")
-            w = KP // pieces
+            width = KP // pieces
             for i in range(pieces):
-                nc.vector.quantize_mx(out=codes[:, i * w:(i + 1) * w].bitcast(FP8X4), scales=plane[:, i * w:(i + 1) * w],
-                                      in_=flat[:, PACK * i * w:PACK * (i + 1) * w])
-            w1_q[a, b] = (codes, plane)
+                cols = slice(i * width, (i + 1) * width)
+                nc.vector.quantize_mx(out=codes[:, cols].bitcast(FP8X4), scales=plane[:, cols],
+                                      in_=flat[:, PACK * i * width:PACK * (i + 1) * width])
+            return codes, plane
 
-        rounded = {(0, 0): new_rounded(0, 0)}
-        v_planes = keep.tile([P, S], U8, name="v_planes", align_bytes=64)
-        nc.vector.tensor_copy(v_planes[:], tab_planes[:].indirect(offs_t[:]))
-        nc.gpsimd.dma_start(v2_plane[0:120, :].bitcast(I32), v_planes[8:128, :].bitcast(I32))
-        for q in range(4):
-            nc.gpsimd.dma_start(w3_planes[32 * q:32 * q + 8, :].bitcast(I32),
-                                w3_scales[:, 4 * q:4 * q + 4, :].bitcast(I32))
-        v_codes = {0: gather_table(0)}
+        w2_codes = keep.tile([P, 2 * H], U8, name="w2_codes", align_bytes=64)
+        w2_plane = keep.tile([P, H], U8, name="w2_plane", align_bytes=64)
+        in_slice_order(w2_codes[:].bitcast(U16), w2_raw[:].bitcast(U16))
 
-        round_w1(nc.scalar.copy, rounded[0, 0], 0, w1_raw[0, 0][:])
-        quantize_w1(0, 0, rounded[0, 0], 1)
-        v_codes[2] = gather_table(2)
-        nc.vector.tensor_copy(w2_plane[:].rearrange("p (a t m) -> p a t m", a=2, t=PACK),
-                              w2_plane_raw[:].rearrange("p (a m t) -> p a t m", a=2, t=PACK))
-        v_codes[1] = gather_table(1)
-        rounded[0, 1] = new_rounded(0, 1)
-        round_w1(nc.scalar.copy, rounded[0, 1], 0, w1_raw[0, 1][:, :, :PACK * 44])
-        round_w1(nc.vector.tensor_copy, rounded[0, 1], 44, w1_raw[0, 1][:, :, PACK * 44:])
-        quantize_w1(0, 1, rounded[0, 1], PACK)
+        rounded = keep.tile([P, PACK, P, PACK], BF16, name="w1_rounded00", align_bytes=64)
+        picked_planes = keep.tile([P, S], U8, name="picked_planes", align_bytes=64)
+        nc.vector.tensor_copy(picked_planes[:], table_planes[:].indirect(offs_t[:]))
+        down = 4 * W2_PASS
+        nc.gpsimd.dma_start(picked_plane2[0:P - down, :].bitcast(I32), picked_planes[down:P, :].bitcast(I32))
 
-        def bank(i):
-            return psum.tile([P, BANK], F32, name="bank%d" % i)
+        picked = {0: gather_table(0)}
+        round_w1(nc.scalar.copy, rounded, w1_raw[0, 0], 0, P)
+        codes = shared.tile([P, KP], U32, name="w1_codes00", align_bytes=64, offset=AT_FIRST_W1_CODES)
+        w1_mx = {(0, 0): quantize_w1(rounded, codes, "w1_plane00", 1)}
+        picked[W2_PASS] = gather_table(W2_PASS)
+        in_slice_order(w2_plane[:], w2_plane_raw[:])
+        picked[1] = gather_table(1)
+        rounded = shared.tile([P, PACK, P, PACK], BF16, name="w1_rounded01", align_bytes=64, offset=AT_ROUNDED[0])
+        round_w1(nc.scalar.copy, rounded, w1_raw[0, 1], 0, ROUND_ON_SCALAR)
+        round_w1(nc.vector.tensor_copy, rounded, w1_raw[0, 1], ROUND_ON_SCALAR, P)
+        codes = keep.tile([P, KP], U32, name="w1_codes01", align_bytes=64)
+        w1_mx[0, 1] = quantize_w1(rounded, codes, "w1_plane01", PACK)
 
-        def first_pass(acc, a, t, half, which, start, stop):
-            cols = slice(half * BANK, (half + 1) * BANK)
-            if which == 2:
+        sums = {}
+
+        def open_sums(a, t, u):
+            sums[a, t, u] = psum.tile([P, BANK], F32, name="bank%d" % (2 * t + u))
+
+        def first_stage_pass(a, t, u, b):
+            cols = slice(u * BANK, (u + 1) * BANK)
+            if b == W2_PASS:
                 c0 = a * KP + t * P
-                nc.tensor.matmul_mx(out=acc[:], lhsT=w2_codes[:, 2 * c0:2 * (c0 + P)].bitcast(FP4X4),
-                                    lhsT_scale=w2_plane[:, c0:c0 + P], rhs=v_codes[2][:, cols].bitcast(FP8X4),
-                                    rhs_scale=v2_plane[:, cols], start=start, stop=stop)
+                lhs, lhs_plane = w2_codes[:, 2 * c0:2 * (c0 + P)].bitcast(FP4X4), w2_plane[:, c0:c0 + P]
+                rhs_plane = picked_plane2[:, cols]
             else:
-                codes, plane = w1_q[a, which]
-                nc.tensor.matmul_mx(out=acc[:], lhsT=codes[:, t * P:(t + 1) * P].bitcast(FP8X4),
-                                    lhsT_scale=plane[:, t * P:(t + 1) * P], rhs=v_codes[which][:, cols].bitcast(FP8X4),
-                                    rhs_scale=v_planes[4 * which:P, cols], start=start, stop=stop)
+                w_codes, w_plane = w1_mx[a, b]
+                lhs, lhs_plane = w_codes[:, t * P:(t + 1) * P].bitcast(FP8X4), w_plane[:, t * P:(t + 1) * P]
+                rhs_plane = picked_planes[4 * b:P, cols]
+            nc.tensor.matmul_mx(out=sums[a, t, u][:], lhsT=lhs, lhsT_scale=lhs_plane,
+                                rhs=picked[b][:, cols].bitcast(FP8X4), rhs_scale=rhs_plane,
+                                start=b == PASS_ORDER[0], stop=b == PASS_ORDER[-1])
 
-        order = (0, 2, 1)
-        accs = {}
         for t in range(PACK):
-            for half in range(2):
-                accs[0, t, half] = bank(2 * t + half)
-        for i, which in enumerate(order):
+            for u in range(2):
+                open_sums(0, t, u)
+        for b in PASS_ORDER:
             for t in range(PACK):
-                for half in range(2):
-                    first_pass(accs[0, t, half], 0, t, half, which, i == 0, i == 2)
+                for u in range(2):
+                    first_stage_pass(0, t, u, b)
 
-        def multiply(s):
-            a, t = divmod(s, PACK)
-            for half in range(2):
-                accs[a, t, half] = bank(2 * (t % 2) + half)
-                for i, which in enumerate(order):
-                    first_pass(accs[a, t, half], a, t, half, which, i == 0, i == 2)
-
-        h = {}
+        window = {}
         lower = {}
-        sq = {}
-        total = {}
-        zb = [keep.tile([P, PACK, M], BF16, name="zb%d" % a, align_bytes=64) for a in range(2)]
-        HALF = M // 2
-        halves = [(slice(u * HALF, (u + 1) * HALF), slice(u * HALF // 16, (u + 1) * HALF // 16)) for u in range(2)]
+        z = [keep.tile([P, PACK, M], BF16, name="z%d" % a, align_bytes=64) for a in range(2)]
+        whole = [(slice(0, M), slice(0, M // LANES))]
+        halves = [(slice(u * HALF, (u + 1) * HALF), slice(u * HALF // LANES, (u + 1) * HALF // LANES))
+                  for u in range(2)]
 
         def activate(s):
             a, t = divmod(s, PACK)
             if a == 1:
-                multiply(s)
-            h[s] = work.tile([P, S], F32, name="h", bufs=4)
-            for half in range(2):
-                nc.scalar.activation(h[s][:, half * BANK:(half + 1) * BANK], accs[a, t, half][:], ACT.Tanh,
-                                     bias=bias_t[:, a, t:t + 1])
-            if s < 2:
-                lower[s] = keep.tile([P, M], F32, name="lower%d" % s, tag="shared%d" % s, align_bytes=64)
-            else:
-                lower[s] = work.tile([P, M], F32, name="lower", bufs=4)
-            nc.vector.tensor_copy(lower[s][:], h[s][:].indirect(p1[:]))
+                for u in range(2):
+                    open_sums(a, t, u)
+                    for b in PASS_ORDER:
+                        first_stage_pass(a, t, u, b)
+            window[s] = work.tile([P, S], F32, name="window", bufs=6)
+            for u in range(2):
+                nc.scalar.activation(window[s][:, u * BANK:(u + 1) * BANK], sums[a, t, u][:],
+                                     ACT.Identity if s % 2 else ACT.Tanh, bias=bias_t[:, a, t:t + 1])
+            if s % 2 == 0:
+                lower[s] = work.tile([P, M], F32, name="lower", bufs=3)
+                nc.vector.tensor_copy(lower[s][:], window[s][:].indirect(p1[:]))
 
-        def combine(s):
-            sq = work.tile([P, M], F32, name="sq", bufs=3)
-            nc.scalar.activation(sq[:], lower[s][:], ACT.Square)
-            prod = work.tile([P, M], F32, name="prod", bufs=3)
-            for cols, entries in halves:
-                nc.vector.tensor_tensor(prod[:, cols], h[s][:].indirect(p2[:, entries]), sq[:, cols], ALU.mult)
-            total[s] = work.tile([P, M], F32, name="total", bufs=4)
-            for cols, entries in halves:
-                nc.vector.tensor_tensor(total[s][:, cols], h[s][:].indirect(p3[:, entries]), prod[:, cols], ALU.add)
-
-        def scale(s, cols):
+        def combine_even(s):
             a, t = divmod(s, PACK)
-            nc.scalar.activation(zb[a][:, t, cols], total[s][:, cols], ACT.Copy, scale=gain_t[:, a, t:t + 1])
+            square = work.tile([P, M], F32, name="square")
+            nc.scalar.activation(square[:], lower[s][:], ACT.Square)
+            product = work.tile([P, M], F32, name="product")
+            for cols, entries in halves:
+                nc.vector.tensor_tensor(product[:, cols], window[s][:].indirect(p2[:, entries]), square[:, cols],
+                                        ALU.mult)
+            total = work.tile([P, M], F32, name="total")
+            for cols, entries in halves:
+                nc.vector.tensor_tensor(total[:, cols], window[s][:].indirect(p3[:, entries]), product[:, cols],
+                                        ALU.add)
+            nc.vector.tensor_scalar(z[a][:, t, :], total[:], gain_t[:, a, t:t + 1], None, ALU.mult)
+
+        def pick_sigmoid(s, places, name, parts):
+            sigmoid = work.tile([P, M], F32, name=name)
+            for cols, entries in parts:
+                nc.scalar.activation(sigmoid[:, cols], window[s][:].indirect(places[:, entries]), ACT.Sigmoid,
+                                     scale=2.0)
+            return sigmoid
+
+        def half_product(sig_lower, sig_hearth):
+            square = work.tile([P, M], F32, name="odd_square")
+            nc.scalar.activation(square[:], sig_lower[:], ACT.Square, scale=2.0, bias=-1.0)
+            product = work.tile([P, M], F32, name="odd_product")
+            nc.vector.scalar_tensor_tensor(product[:], sig_hearth[:], 0.5, square[:], ALU.subtract, ALU.mult)
+            return product
+
+        def finish_odd(s, product, sig_upper):
+            a, t = divmod(s, PACK)
+            total = work.tile([P, M], F32, name="odd_total")
+            for cols, entries in halves:
+                nc.vector.scalar_tensor_tensor(total[:, cols], sig_upper[:, cols], 0.5, product[:, cols],
+                                               ALU.subtract, ALU.add)
+            for cols, entries in halves:
+                nc.vector.tensor_scalar(z[a][:, t, cols], total[:, cols], gain_t[:, a, t:t + 1], 2.0,
+                                        ALU.mult, ALU.mult)
 
         woven = [keep.tile([P, M, PACK], BF16, name="woven%d" % a, align_bytes=64) for a in range(2)]
         z_codes = [keep.tile([P, M], U32, name="z_codes%d" % a, align_bytes=64) for a in range(2)]
         z_plane = [keep.tile([P, M], U8, name="z_plane%d" % a, align_bytes=64) for a in range(2)]
+        results = {}
 
         def weave(copy, a, cols):
             copy(woven[a][:, cols, :].rearrange("p (c i) t -> p c t i", i=4),
-                 zb[a][:, :, cols].rearrange("p t (c i) -> p c t i", i=4))
+                 z[a][:, :, cols].rearrange("p t (c i) -> p c t i", i=4))
 
         def quantize_z(a, cols):
             nc.vector.quantize_mx(out=z_codes[a][:, cols].bitcast(FP8X4), scales=z_plane[a][:, cols],
                                   in_=woven[a][:, cols, :].rearrange("p m t -> p (m t)"))
 
-        outs = {}
-
-        def second(a, u):
+        def second_stage_pass(a, u):
             cols = halves[u][0]
-            for n in range(4):
+            for n in range(N // P):
                 if a == 0:
-                    outs[u, n] = psum.tile([P, HALF], F32, name="bank%d" % (4 * (1 - u) + n))
-                nc.tensor.matmul_mx(out=outs[u, n][:], lhsT=w3_codes[:, a, n * P:(n + 1) * P].bitcast(FP8X4),
+                    results[u, n] = psum.tile([P, HALF], F32, name="bank%d" % (4 * u + n))
+                nc.tensor.matmul_mx(out=results[u, n][:], lhsT=w3_codes[:, a, n * P:(n + 1) * P].bitcast(FP8X4),
                                     lhsT_scale=w3_planes[4 * a:P, n * P:(n + 1) * P],
                                     rhs=z_codes[a][:, cols].bitcast(FP8X4), rhs_scale=z_plane[a][:, cols],
-                                    start=(a == 0), stop=(a == 1))
+                                    start=a == 0, stop=a == 1)
 
         def store(u):
             cols = halves[u][0]
             for pair, copy in enumerate((nc.scalar.copy, nc.vector.tensor_copy)):
-                result = keep.tile([P, 2, HALF], F32, name="result%d%d" % (u, pair))
+                staged = keep.tile([P, 2, HALF], F32, name="staged%d%d" % (u, pair))
                 for i in range(2):
-                    copy(result[:, i, :], outs[u, 2 * pair + i][:])
+                    copy(staged[:, i, :], results[u, 2 * pair + i][:])
                 rows = out[2 * pair * P:(2 * pair + 2) * P, cols]
-                nc.sync.dma_start(rows.rearrange("(n p) m -> p n m", p=P), result[:])
+                nc.sync.dma_start(rows.rearrange("(n p) m -> p n m", p=P), staged[:])
 
-        def round_half(b, u):
-            if u == 0:
-                rounded[1, b] = new_rounded(1, b)
-            round_w1(nc.scalar.copy, rounded[1, b], u * P // 2, w1_raw[1, b][:, :, u * KP // 2:(u + 1) * KP // 2])
-
-        whole = slice(0, M)
-        activate(0)
-        activate(1)
-        combine(0)
-        round_half(0, 0)
+        for b in range(2):
+            activate(b)
+            rounded = shared.tile([P, PACK, P, PACK], BF16, name="w1_rounded1%d" % b, align_bytes=64,
+                                  offset=AT_ROUNDED[1])
+            round_w1(nc.vector.tensor_copy, rounded, w1_raw[1, b], 0, P)
+            codes = keep.tile([P, KP], U32, name="w1_codes1%d" % b, align_bytes=64)
+            w1_mx[1, b] = quantize_w1(rounded, codes, "w1_plane1%d" % b, 1)
         activate(2)
-        combine(1)
-        round_half(0, 1)
-        quantize_w1(1, 0, rounded[1, 0], 1)
-        activate(3)
-        round_half(1, 0)
-        combine(2)
-        round_half(1, 1)
-        quantize_w1(1, 1, rounded[1, 1], 1)
-        combine(3)
-        scale(0, whole)
-        scale(1, whole)
-        activate(4)
-        activate(5)
-        scale(2, whole)
-        combine(4)
-        scale(3, whole)
-        activate(6)
-        weave(nc.scalar.copy, 0, halves[0][0])
-        combine(5)
-        activate(7)
-        weave(nc.scalar.copy, 0, halves[1][0])
-        combine(6)
-        quantize_z(0, whole)
-        second(0, 0)
-        second(0, 1)
-        scale(4, whole)
-        scale(5, whole)
-        combine(7)
-        scale(6, whole)
-        scale(7, halves[0][0])
-        weave(nc.scalar.copy, 1, slice(0, 96))
-        weave(nc.vector.tensor_copy, 1, slice(96, HALF))
-        scale(7, halves[1][0])
-        quantize_z(1, halves[0][0])
-        second(1, 0)
-        weave(nc.scalar.copy, 1, slice(HALF, HALF + 96))
-        weave(nc.vector.tensor_copy, 1, slice(HALF + 96, M))
-        quantize_z(1, halves[1][0])
-        second(1, 1)
+        for s in range(1, SLICES, 2):
+            last = s + 1 == SLICES
+            sig_lower = pick_sigmoid(s, p1, "sig_lower", whole)
+            combine_even(s - 1)
+            sig_hearth = pick_sigmoid(s, p2, "sig_hearth", whole)
+            product = half_product(sig_lower, sig_hearth)
+            if s + 3 < SLICES:
+                activate(s + 3)
+            sig_upper = pick_sigmoid(s, p3, "sig_upper", halves if last else whole)
+            if not last:
+                activate(s + 2)
+            finish_odd(s, product, sig_upper)
+            if s + 1 == PACK:
+                weave(nc.vector.tensor_copy, 0, whole[0][0])
+                quantize_z(0, whole[0][0])
+            if s + 2 == SLICES - 1:
+                second_stage_pass(0, 0)
+                second_stage_pass(0, 1)
+        for u in range(2):
+            split = u * HALF + WEAVE_ON_SCALAR
+            weave(nc.scalar.copy, 1, slice(u * HALF, split))
+            weave(nc.vector.tensor_copy, 1, slice(split, (u + 1) * HALF))
+            quantize_z(1, halves[u][0])
+            second_stage_pass(1, u)
         store(0)
         store(1)

@@ -31,12 +31,21 @@ ROUND_ON_SCALAR = 44
 WEAVE_ON_SCALAR = 80
 
 TABLE_BYTES = 4 * T
-AT_TABLE = (0, TABLE_BYTES, 2 * TABLE_BYTES)
-AT_TABLE_PLANES = 3 * TABLE_BYTES
-AT_W2_PLANE = AT_TABLE_PLANES + T
-AT_PICKED = (AT_TABLE_PLANES, AT_W2_PLANE, AT_TABLE[0])
+W1_BYTES = 4 * PACK * KP
+ROUNDED_BYTES = 2 * PACK * KP
+AT_TABLE = (0, TABLE_BYTES, 2 * TABLE_BYTES + 4 * S)
+AT_TABLE_PLANES = AT_TABLE[1] + TABLE_BYTES - T // 2
+AT_W2_RAW = AT_TABLE[2] + TABLE_BYTES - H
+AT_FIRST_ROUNDED = AT_TABLE[2] + TABLE_BYTES + W1_BYTES
+AT_W1_RAW = {(0, 0): AT_TABLE[2] + TABLE_BYTES, (0, 1): AT_TABLE[2] + TABLE_BYTES,
+             (1, 0): AT_FIRST_ROUNDED, (1, 1): AT_TABLE[2]}
+AT_W2_PLANE = AT_FIRST_ROUNDED + W1_BYTES
+AT_PICKED = (AT_TABLE[1] + TABLE_BYTES, AT_W2_PLANE, AT_TABLE[0])
 AT_FIRST_W1_CODES = AT_TABLE[0] + 4 * S
-AT_ROUNDED = (AT_TABLE[1], AT_TABLE[1] + 2 * PACK * KP)
+AT_BIAS = AT_FIRST_W1_CODES + 4 * KP
+AT_GAIN = AT_BIAS + 64
+AT_ROUNDED = (AT_TABLE[1], AT_TABLE[1] + ROUNDED_BYTES)
+AT_W3_CODES = AT_TABLE[1] + 2 * ROUNDED_BYTES
 
 
 def tile_list_site_phasing_kernel(tc, tab_words, tab_scales, offs, pos1, pos2, pos3, w1, w2_words,
@@ -53,20 +62,22 @@ def tile_list_site_phasing_kernel(tc, tab_words, tab_scales, offs, pos1, pos2, p
             nc.sync.dma_start(tile[:], src)
             return tile
 
-        def load_table(a):
-            tile = shared.tile([P, T], U32, name="table%d" % a, align_bytes=64, offset=AT_TABLE[a])
-            nc.sync.dma_start(tile[:].bitcast(I32), tab_words[a].rearrange("p t i -> p (t i)").bitcast(I32))
-            return tile
+        def new_table(a):
+            return shared.tile([P, T], U32, name="table%d" % a, align_bytes=64, offset=AT_TABLE[a])
+
+        def load_table(tile, a, cols):
+            words = tab_words[a].rearrange("p t i -> p (t i)").bitcast(I32)
+            nc.sync.dma_start(tile[:].bitcast(I32)[:, cols], words[:, cols])
 
         def load_w1(a, b):
-            tile = keep.tile([P, PACK, KP], F32, name="w1_raw%d%d" % (a, b))
+            tile = shared.tile([P, PACK, KP], F32, name="w1_raw%d%d" % (a, b), align_bytes=64, offset=AT_W1_RAW[a, b])
             rows = w1[b * KP:(b + 1) * KP, a * KP:(a + 1) * KP]
             nc.sync.dma_start(tile[:], rows.rearrange("(p j) c -> p j c", j=PACK))
             return tile
 
-        def load_planes(queue, planes, scales):
+        def load_planes(queues, planes, scales):
             rows = 4 * scales.shape[0]
-            for q in range(QUADRANTS):
+            for q, queue in enumerate(queues):
                 queue.dma_start(planes[32 * q:32 * q + rows, :].bitcast(I32),
                                 scales[:, 4 * q:4 * q + 4, :].bitcast(I32))
 
@@ -76,33 +87,22 @@ def tile_list_site_phasing_kernel(tc, tab_words, tab_scales, offs, pos1, pos2, p
         picked_plane2 = keep.tile([P, S], U8, name="picked_plane2", align_bytes=64)
         for plane in (table_planes, w2_plane_raw, w3_planes, picked_plane2):
             nc.vector.memset(plane[:].bitcast(I32), 0)
-        load_planes(nc.gpsimd, table_planes, tab_scales)
-        load_planes(nc.gpsimd, w2_plane_raw, w2_scales)
+        load_planes((nc.gpsimd, nc.gpsimd, nc.scalar, nc.scalar), table_planes, tab_scales)
+        load_planes([nc.gpsimd] * QUADRANTS, w2_plane_raw, w2_scales)
 
         warm = keep.tile([P, 2], F32, name="warm")
         nc.vector.memset(warm[:], 0.0)
         nc.scalar.activation(warm[:, 1:2], warm[:, 0:1], ACT.Sigmoid)
 
         offs_t = load_list(offs, "offs_t")
-        w2_raw = keep.tile([P, 2 * H], U8, name="w2_raw", align_bytes=64)
+        w2_raw = shared.tile([P, 2 * H], U8, name="w2_raw", align_bytes=64, offset=AT_W2_RAW)
+        table = {0: new_table(0)}
+        load_table(table[0], 0, slice(0, T // 2))
         nc.sync.dma_start(w2_raw[:].bitcast(I32), w2_words[0].bitcast(I32))
-        table = {0: load_table(0)}
-        w1_raw = {(0, 0): load_w1(0, 0)}
-        table[W2_PASS] = load_table(W2_PASS)
-        table[1] = load_table(1)
-        w1_raw[0, 1] = load_w1(0, 1)
-        bias_t = keep.tile([P, 2, PACK], F32, name="bias_t")
-        gain_t = keep.tile([P, 2, PACK], F32, name="gain_t")
-        nc.sync.dma_start(bias_t[:], bias.rearrange("(a p t) -> p a t", p=P, t=PACK))
+        load_table(table[0], 0, slice(T // 2, T))
         p1 = load_list(pos1, "p1")
         p2 = load_list(pos2, "p2")
         p3 = load_list(pos3, "p3")
-        w1_raw[1, 0] = load_w1(1, 0)
-        w1_raw[1, 1] = load_w1(1, 1)
-        nc.sync.dma_start(gain_t[:], gain.rearrange("(a p t) -> p a t", p=P, t=PACK))
-        w3_codes = keep.tile([P, 2, N], U32, name="w3_codes", align_bytes=64)
-        nc.sync.dma_start(w3_codes[:].bitcast(I32), w3_words.rearrange("a p c i -> p a (c i)").bitcast(I32))
-        load_planes(nc.sync, w3_planes, w3_scales)
 
         def in_slice_order(dst, src):
             nc.vector.tensor_copy(dst.rearrange("p (a t m) -> p a t m", a=2, t=PACK),
@@ -130,20 +130,35 @@ def tile_list_site_phasing_kernel(tc, tab_words, tab_scales, offs, pos1, pos2, p
         w2_codes = keep.tile([P, 2 * H], U8, name="w2_codes", align_bytes=64)
         w2_plane = keep.tile([P, H], U8, name="w2_plane", align_bytes=64)
         in_slice_order(w2_codes[:].bitcast(U16), w2_raw[:].bitcast(U16))
+        w1_raw = {(0, 0): load_w1(0, 0)}
+        table[W2_PASS] = new_table(W2_PASS)
+        load_table(table[W2_PASS], W2_PASS, slice(0, T))
 
-        rounded = keep.tile([P, PACK, P, PACK], BF16, name="w1_rounded00", align_bytes=64)
+        rounded = shared.tile([P, PACK, P, PACK], BF16, name="w1_rounded00", align_bytes=64, offset=AT_FIRST_ROUNDED)
         picked_planes = keep.tile([P, S], U8, name="picked_planes", align_bytes=64)
         nc.vector.tensor_copy(picked_planes[:], table_planes[:].indirect(offs_t[:]))
         down = 4 * W2_PASS
-        nc.gpsimd.dma_start(picked_plane2[0:P - down, :].bitcast(I32), picked_planes[down:P, :].bitcast(I32))
+        nc.sync.dma_start(picked_plane2[0:P - down, :].bitcast(I32), picked_planes[down:P, :].bitcast(I32))
+        table[1] = new_table(1)
+        load_table(table[1], 1, slice(0, T))
 
         picked = {0: gather_table(0)}
+        bias_t = shared.tile([P, 2, PACK], F32, name="bias_t", align_bytes=64, offset=AT_BIAS)
+        gain_t = shared.tile([P, 2, PACK], F32, name="gain_t", align_bytes=64, offset=AT_GAIN)
+        nc.sync.dma_start(bias_t[:], bias.rearrange("(a p t) -> p a t", p=P, t=PACK))
+        nc.sync.dma_start(gain_t[:], gain.rearrange("(a p t) -> p a t", p=P, t=PACK))
         round_w1(nc.scalar.copy, rounded, w1_raw[0, 0], 0, P)
+        w1_raw[0, 1] = load_w1(0, 1)
         codes = shared.tile([P, KP], U32, name="w1_codes00", align_bytes=64, offset=AT_FIRST_W1_CODES)
         w1_mx = {(0, 0): quantize_w1(rounded, codes, "w1_plane00", 1)}
+        w1_raw[1, 0] = load_w1(1, 0)
         picked[W2_PASS] = gather_table(W2_PASS)
+        w1_raw[1, 1] = load_w1(1, 1)
         in_slice_order(w2_plane[:], w2_plane_raw[:])
         picked[1] = gather_table(1)
+        w3_codes = shared.tile([P, 2, N], U32, name="w3_codes", align_bytes=64, offset=AT_W3_CODES)
+        nc.sync.dma_start(w3_codes[:].bitcast(I32), w3_words.rearrange("a p c i -> p a (c i)").bitcast(I32))
+        load_planes([nc.gpsimd] * QUADRANTS, w3_planes, w3_scales)
         rounded = shared.tile([P, PACK, P, PACK], BF16, name="w1_rounded01", align_bytes=64, offset=AT_ROUNDED[0])
         round_w1(nc.scalar.copy, rounded, w1_raw[0, 1], 0, ROUND_ON_SCALAR)
         round_w1(nc.vector.tensor_copy, rounded, w1_raw[0, 1], ROUND_ON_SCALAR, P)

@@ -21,40 +21,31 @@ PACK = 4
 KP = P * PACK
 BANK = 512
 QUADRANTS = 4
-SLICES = H // P
-HALF = M // 2
 LANES = 16
 W2_PASS = 2
-PASS_ORDER = (0, W2_PASS, 1)
+PIECES = ((0, 256), (256, 384), (384, 512))
 
-ROUND_ON_SCALAR = 44
-WEAVE_ON_SCALAR = 80
 
-TABLE_BYTES = 4 * T
-W1_BYTES = 4 * PACK * KP
-ROUNDED_BYTES = 2 * PACK * KP
-AT_TABLE = (0, TABLE_BYTES, 2 * TABLE_BYTES + 4 * S)
-AT_TABLE_PLANES = AT_TABLE[1] + TABLE_BYTES - T // 2
-AT_W2_RAW = AT_TABLE[2] + TABLE_BYTES - H
-AT_FIRST_ROUNDED = AT_TABLE[2] + TABLE_BYTES + W1_BYTES
-AT_W1_RAW = {(0, 0): AT_TABLE[2] + TABLE_BYTES, (0, 1): AT_TABLE[2] + TABLE_BYTES,
-             (1, 0): AT_FIRST_ROUNDED, (1, 1): AT_TABLE[2]}
-AT_W2_PLANE = AT_FIRST_ROUNDED + W1_BYTES
-AT_PICKED = (AT_TABLE[1] + TABLE_BYTES, AT_W2_PLANE, AT_TABLE[0])
-AT_FIRST_W1_CODES = AT_TABLE[0] + 4 * S
-AT_BIAS = AT_FIRST_W1_CODES + 4 * KP
-AT_GAIN = AT_BIAS + 64
-AT_ROUNDED = (AT_TABLE[1], AT_TABLE[1] + ROUNDED_BYTES)
-AT_W3_CODES = AT_TABLE[1] + 2 * ROUNDED_BYTES
+KB = 1024
+AT_TABLE = (0, 37 * KB, 3 * KB)
+AT_PICKED_PLANES = 0
+AT_TABLE_PLANES = 16 * KB
+AT_BIAS, AT_GAIN = 36 * KB + 512, 36 * KB + 576
+AT_W1_EARLY = 20 * KB + 512
+AT_W2_RAW = 36 * KB
+AT_W1_LATE = (37 * KB, 50 * KB + 512)
+AT_W3_PLANES = 45 * KB
+AT_W2_PLANE = 45 * KB + 512
+AT_W3_CODES = 46 * KB + 512
 
 
 def tile_list_site_phasing_kernel(tc, tab_words, tab_scales, offs, pos1, pos2, pos3, w1, w2_words,
-                                            w2_scales, bias, gain, w3_words, w3_scales, out):
+                                                w2_scales, bias, gain, w3_words, w3_scales, out):
     nc = tc.nc
     with ExitStack() as ctx:
         keep = ctx.enter_context(tc.tile_pool(name="keep", bufs=1))
         shared = ctx.enter_context(tc.tile_pool(name="shared", bufs=1))
-        work = ctx.enter_context(tc.tile_pool(name="work", bufs=2))
+        work = ctx.enter_context(tc.tile_pool(name="work", bufs=1))
         psum = ctx.enter_context(tc.psum_pool(name="psum", bufs=1))
 
         def load_list(src, name):
@@ -69,11 +60,11 @@ def tile_list_site_phasing_kernel(tc, tab_words, tab_scales, offs, pos1, pos2, p
             words = tab_words[a].rearrange("p t i -> p (t i)").bitcast(I32)
             nc.sync.dma_start(tile[:].bitcast(I32)[:, cols], words[:, cols])
 
-        def load_w1(a, b):
-            tile = shared.tile([P, PACK, KP], F32, name="w1_raw%d%d" % (a, b), align_bytes=64, offset=AT_W1_RAW[a, b])
+        def load_w1(dst, a, b):
             rows = w1[b * KP:(b + 1) * KP, a * KP:(a + 1) * KP]
-            nc.sync.dma_start(tile[:], rows.rearrange("(p j) c -> p j c", j=PACK))
-            return tile
+            raw = dst.rearrange("p (j c) -> p j c", j=PACK)
+            nc.sync.dma_start(raw, rows.rearrange("(p j) c -> p j c", j=PACK))
+            return raw
 
         def load_planes(queues, planes, scales):
             rows = 4 * scales.shape[0]
@@ -82,18 +73,10 @@ def tile_list_site_phasing_kernel(tc, tab_words, tab_scales, offs, pos1, pos2, p
                                 scales[:, 4 * q:4 * q + 4, :].bitcast(I32))
 
         table_planes = shared.tile([P, T], U8, name="table_planes", align_bytes=64, offset=AT_TABLE_PLANES)
-        w2_plane_raw = shared.tile([P, H], U8, name="w2_plane_raw", align_bytes=64, offset=AT_W2_PLANE)
-        w3_planes = keep.tile([P, N], U8, name="w3_planes", align_bytes=64)
+        w2_plane_raw = keep.tile([P, H], U8, name="w2_plane_raw", align_bytes=64)
         picked_plane2 = keep.tile([P, S], U8, name="picked_plane2", align_bytes=64)
-        for plane in (table_planes, w2_plane_raw, w3_planes, picked_plane2):
+        for plane in (table_planes, w2_plane_raw, picked_plane2):
             nc.vector.memset(plane[:].bitcast(I32), 0)
-        load_planes((nc.gpsimd, nc.gpsimd, nc.scalar, nc.scalar), table_planes, tab_scales)
-        load_planes([nc.gpsimd] * QUADRANTS, w2_plane_raw, w2_scales)
-
-        warm = keep.tile([P, 2], F32, name="warm")
-        nc.vector.memset(warm[:], 0.0)
-        nc.scalar.activation(warm[:, 1:2], warm[:, 0:1], ACT.Sigmoid)
-
         offs_t = load_list(offs, "offs_t")
         w2_raw = shared.tile([P, 2 * H], U8, name="w2_raw", align_bytes=64, offset=AT_W2_RAW)
         table = {0: new_table(0)}
@@ -103,67 +86,75 @@ def tile_list_site_phasing_kernel(tc, tab_words, tab_scales, offs, pos1, pos2, p
         p1 = load_list(pos1, "p1")
         p2 = load_list(pos2, "p2")
         p3 = load_list(pos3, "p3")
+        load_planes((nc.gpsimd, nc.gpsimd, nc.scalar, nc.scalar), table_planes, tab_scales)
+        load_planes([nc.gpsimd] * QUADRANTS, w2_plane_raw, w2_scales)
+
+        warm = keep.tile([P, 2], F32, name="warm")
+        nc.vector.memset(warm[:], 0.0)
+        nc.scalar.activation(warm[:, 1:2], warm[:, 0:1], ACT.Sigmoid)
 
         def in_slice_order(dst, src):
             nc.vector.tensor_copy(dst.rearrange("p (a t m) -> p a t m", a=2, t=PACK),
                                   src.rearrange("p (a m t) -> p a t m", a=2, t=PACK))
 
-        def gather_table(a):
-            tile = shared.tile([P, S], U32, name="picked_codes%d" % a, align_bytes=64, offset=AT_PICKED[a])
-            nc.vector.tensor_copy(tile[:], table[a][:].indirect(offs_t[:]))
-            return tile
-
         def round_w1(copy, rounded, raw, m0, m1):
             src = raw[:, :, PACK * m0:PACK * m1].rearrange("p j (m t) -> p m j t", t=PACK)
             copy(rounded[:].rearrange("p t m j -> p m j t")[:, m0:m1], src)
 
-        def quantize_w1(rounded, codes, name, pieces):
-            plane = keep.tile([P, KP], U8, name=name, align_bytes=64)
-            flat = rounded[:].rearrange("p t m j -> p (t m j)")
-            width = KP // pieces
-            for i in range(pieces):
-                cols = slice(i * width, (i + 1) * width)
-                nc.vector.quantize_mx(out=codes[:, cols].bitcast(FP8X4), scales=plane[:, cols],
-                                      in_=flat[:, PACK * i * width:PACK * (i + 1) * width])
-            return codes, plane
+        def new_rounded():
+            return work.tile([P, PACK, P, PACK], BF16, name="w1_rounded", align_bytes=64, bufs=2)
+
+        w1_mx = {}
+
+        def quantize_w1(rounded, a, b):
+            codes = keep.tile([P, KP], U32, name="w1_codes%d%d" % (a, b), align_bytes=64)
+            plane = keep.tile([P, KP], U8, name="w1_plane%d%d" % (a, b), align_bytes=64)
+            nc.vector.quantize_mx(out=codes[:].bitcast(FP8X4), scales=plane[:],
+                                  in_=rounded[:].rearrange("p t m j -> p (t m j)"))
+            w1_mx[a, b] = codes, plane
 
         w2_codes = keep.tile([P, 2 * H], U8, name="w2_codes", align_bytes=64)
-        w2_plane = keep.tile([P, H], U8, name="w2_plane", align_bytes=64)
         in_slice_order(w2_codes[:].bitcast(U16), w2_raw[:].bitcast(U16))
-        w1_raw = {(0, 0): load_w1(0, 0)}
-        table[W2_PASS] = new_table(W2_PASS)
-        load_table(table[W2_PASS], W2_PASS, slice(0, T))
-
-        rounded = shared.tile([P, PACK, P, PACK], BF16, name="w1_rounded00", align_bytes=64, offset=AT_FIRST_ROUNDED)
-        picked_planes = keep.tile([P, S], U8, name="picked_planes", align_bytes=64)
+        w1_early = shared.tile([P, 2 * PACK * KP], F32, name="w1_early", align_bytes=64, offset=AT_W1_EARLY)
+        w1_raw = {(0, b): load_w1(w1_early[:, b * PACK * KP:(b + 1) * PACK * KP], 0, b) for b in range(2)}
+        bias_t = shared.tile([P, 2, PACK], F32, name="bias_t", align_bytes=64, offset=AT_BIAS)
+        gain_t = shared.tile([P, 2, PACK], F32, name="gain_t", align_bytes=64, offset=AT_GAIN)
+        nc.sync.dma_start(gain_t[:], gain.rearrange("(a p t) -> p a t", p=P, t=PACK))
+        nc.sync.dma_start(bias_t[:], bias.rearrange("(a p t) -> p a t", p=P, t=PACK))
+        table[1] = new_table(1)
+        load_table(table[1], 1, slice(0, T))
+        picked = {0: keep.tile([P, S], U32, name="picked_codes0", align_bytes=64)}
+        nc.vector.tensor_copy(picked[0][:], table[0][:].indirect(offs_t[:]))
+        picked_planes = shared.tile([P, S], U8, name="picked_planes", align_bytes=64, offset=AT_PICKED_PLANES)
         nc.vector.tensor_copy(picked_planes[:], table_planes[:].indirect(offs_t[:]))
         down = 4 * W2_PASS
         nc.sync.dma_start(picked_plane2[0:P - down, :].bitcast(I32), picked_planes[down:P, :].bitcast(I32))
-        table[1] = new_table(1)
-        load_table(table[1], 1, slice(0, T))
+        table[W2_PASS] = new_table(W2_PASS)
+        load_table(table[W2_PASS], W2_PASS, slice(0, T))
+        for b in range(2):
+            rounded = new_rounded()
+            round_w1(nc.scalar.copy, rounded, w1_raw[0, b], 0, P)
+            quantize_w1(rounded, 0, b)
 
-        picked = {0: gather_table(0)}
-        bias_t = shared.tile([P, 2, PACK], F32, name="bias_t", align_bytes=64, offset=AT_BIAS)
-        gain_t = shared.tile([P, 2, PACK], F32, name="gain_t", align_bytes=64, offset=AT_GAIN)
-        nc.sync.dma_start(bias_t[:], bias.rearrange("(a p t) -> p a t", p=P, t=PACK))
-        nc.sync.dma_start(gain_t[:], gain.rearrange("(a p t) -> p a t", p=P, t=PACK))
-        round_w1(nc.scalar.copy, rounded, w1_raw[0, 0], 0, P)
-        w1_raw[0, 1] = load_w1(0, 1)
-        codes = shared.tile([P, KP], U32, name="w1_codes00", align_bytes=64, offset=AT_FIRST_W1_CODES)
-        w1_mx = {(0, 0): quantize_w1(rounded, codes, "w1_plane00", 1)}
-        w1_raw[1, 0] = load_w1(1, 0)
-        picked[W2_PASS] = gather_table(W2_PASS)
-        w1_raw[1, 1] = load_w1(1, 1)
-        in_slice_order(w2_plane[:], w2_plane_raw[:])
-        picked[1] = gather_table(1)
-        w3_codes = shared.tile([P, 2, N], U32, name="w3_codes", align_bytes=64, offset=AT_W3_CODES)
-        nc.sync.dma_start(w3_codes[:].bitcast(I32), w3_words.rearrange("a p c i -> p a (c i)").bitcast(I32))
-        load_planes([nc.gpsimd] * QUADRANTS, w3_planes, w3_scales)
-        rounded = shared.tile([P, PACK, P, PACK], BF16, name="w1_rounded01", align_bytes=64, offset=AT_ROUNDED[0])
-        round_w1(nc.scalar.copy, rounded, w1_raw[0, 1], 0, ROUND_ON_SCALAR)
-        round_w1(nc.vector.tensor_copy, rounded, w1_raw[0, 1], ROUND_ON_SCALAR, P)
-        codes = keep.tile([P, KP], U32, name="w1_codes01", align_bytes=64)
-        w1_mx[0, 1] = quantize_w1(rounded, codes, "w1_plane01", PACK)
+        def per_row(name):
+            return keep.tile([P, 2, PACK], F32, name=name)
+
+        sign, signed_bias, factor, half = per_row("sign"), per_row("signed_bias"), per_row("factor"), per_row("half")
+        root, root2, minus_root = per_row("root"), per_row("root2"), per_row("minus_root")
+        nc.gpsimd.memset(half[:], 0.5)
+        nc.gpsimd.tensor_scalar(sign[:], gain_t[:], 0.0, 2.0, ALU.is_ge, ALU.mult)
+        nc.gpsimd.tensor_scalar(sign[:], sign[:], -1.0, 1.0, ALU.add, ALU.mult)
+        nc.gpsimd.tensor_tensor(factor[:], gain_t[:], sign[:], ALU.mult)
+        nc.gpsimd.tensor_scalar(factor[:, :, 1::2], factor[:, :, 1::2], 2.0, 0.0, ALU.mult, ALU.add)
+        nc.gpsimd.tensor_tensor(signed_bias[:], bias_t[:], sign[:], ALU.mult)
+        nc.gpsimd.tensor_tensor(root[:], factor[:], half[:], ALU.pow)
+        nc.gpsimd.tensor_scalar(root2[:], root[:], 2.0, 0.0, ALU.mult, ALU.add)
+        nc.gpsimd.tensor_scalar(minus_root[:], root[:], -1.0, 0.0, ALU.mult, ALU.add)
+        spread = {}
+        for a in range(2):
+            for t in range(0, PACK, 2):
+                spread[a, t] = keep.tile([P, M], F32, name="spread%d%d" % (a, t))
+                nc.scalar.copy(spread[a, t][:], factor[:, a, t:t + 1].to_broadcast([P, M]))
 
         sums = {}
 
@@ -182,139 +173,209 @@ def tile_list_site_phasing_kernel(tc, tab_words, tab_scales, offs, pos1, pos2, p
                 rhs_plane = picked_planes[4 * b:P, cols]
             nc.tensor.matmul_mx(out=sums[a, t, u][:], lhsT=lhs, lhsT_scale=lhs_plane,
                                 rhs=picked[b][:, cols].bitcast(FP8X4), rhs_scale=rhs_plane,
-                                start=b == PASS_ORDER[0], stop=b == PASS_ORDER[-1])
+                                start=b == 0, stop=b == W2_PASS)
 
         for t in range(PACK):
             for u in range(2):
                 open_sums(0, t, u)
-        for b in PASS_ORDER:
-            for t in range(PACK):
-                for u in range(2):
-                    first_stage_pass(0, t, u, b)
-
-        window = {}
-        lower = {}
-        z = [keep.tile([P, PACK, M], BF16, name="z%d" % a, align_bytes=64) for a in range(2)]
-        whole = [(slice(0, M), slice(0, M // LANES))]
-        halves = [(slice(u * HALF, (u + 1) * HALF), slice(u * HALF // LANES, (u + 1) * HALF // LANES))
-                  for u in range(2)]
-
-        def activate(s):
-            a, t = divmod(s, PACK)
-            if a == 1:
-                for u in range(2):
-                    open_sums(a, t, u)
-                    for b in PASS_ORDER:
-                        first_stage_pass(a, t, u, b)
-            window[s] = work.tile([P, S], F32, name="window", bufs=6)
+        for t in range(PACK):
             for u in range(2):
-                nc.scalar.activation(window[s][:, u * BANK:(u + 1) * BANK], sums[a, t, u][:],
-                                     ACT.Identity if s % 2 else ACT.Tanh, bias=bias_t[:, a, t:t + 1])
-            if s % 2 == 0:
-                lower[s] = work.tile([P, M], F32, name="lower", bufs=3)
-                nc.vector.tensor_copy(lower[s][:], window[s][:].indirect(p1[:]))
+                first_stage_pass(0, t, u, 0)
 
-        def combine_even(s):
-            a, t = divmod(s, PACK)
-            square = work.tile([P, M], F32, name="square")
-            nc.scalar.activation(square[:], lower[s][:], ACT.Square)
-            product = work.tile([P, M], F32, name="product")
-            for cols, entries in halves:
-                nc.vector.tensor_tensor(product[:, cols], window[s][:].indirect(p2[:, entries]), square[:, cols],
-                                        ALU.mult)
-            total = work.tile([P, M], F32, name="total")
-            for cols, entries in halves:
-                nc.vector.tensor_tensor(total[:, cols], window[s][:].indirect(p3[:, entries]), product[:, cols],
-                                        ALU.add)
-            nc.vector.tensor_scalar(z[a][:, t, :], total[:], gain_t[:, a, t:t + 1], None, ALU.mult)
+        def gather_half(b, u):
+            nc.vector.tensor_copy(picked[b][:, u * BANK:(u + 1) * BANK],
+                                  table[b][:].indirect(offs_t[:, u * BANK // LANES:(u + 1) * BANK // LANES]))
 
-        def pick_sigmoid(s, places, name, parts):
-            sigmoid = work.tile([P, M], F32, name=name)
-            for cols, entries in parts:
-                nc.scalar.activation(sigmoid[:, cols], window[s][:].indirect(places[:, entries]), ACT.Sigmoid,
-                                     scale=2.0)
-            return sigmoid
+        picked[1] = keep.tile([P, S], U32, name="picked_codes1", align_bytes=64)
+        picked[W2_PASS] = keep.tile([P, S], U32, name="picked_codes2", align_bytes=64)
+        for u in range(2):
+            gather_half(1, u)
+            for t in range(PACK):
+                first_stage_pass(0, t, u, 1)
+        w2_plane = shared.tile([P, H], U8, name="w2_plane", align_bytes=64, offset=AT_W2_PLANE)
+        in_slice_order(w2_plane[:], w2_plane_raw[:])
+        for b in range(2):
+            late = shared.tile([P, PACK * KP], F32, name="w1_late%d" % b, align_bytes=64, offset=AT_W1_LATE[b])
+            w1_raw[1, b] = load_w1(late[:], 1, b)
+        w3_codes = shared.tile([P, 2, N], U32, name="w3_codes", align_bytes=64, offset=AT_W3_CODES)
+        nc.sync.dma_start(w3_codes[:].bitcast(I32), w3_words.rearrange("a p c i -> p a (c i)").bitcast(I32))
+        w3_planes = shared.tile([P, N], U8, name="w3_planes", align_bytes=64, offset=AT_W3_PLANES)
+        nc.vector.memset(w3_planes[:].bitcast(I32), 0)
+        load_planes([nc.sync] * QUADRANTS, w3_planes, w3_scales)
+        for u in range(2):
+            gather_half(W2_PASS, u)
+            for t in range(2):
+                first_stage_pass(0, t, u, W2_PASS)
+        for t in range(2, PACK):
+            for u in range(2):
+                first_stage_pass(0, t, u, W2_PASS)
 
-        def half_product(sig_lower, sig_hearth):
-            square = work.tile([P, M], F32, name="odd_square")
-            nc.scalar.activation(square[:], sig_lower[:], ACT.Square, scale=2.0, bias=-1.0)
-            product = work.tile([P, M], F32, name="odd_product")
-            nc.vector.scalar_tensor_tensor(product[:], sig_hearth[:], 0.5, square[:], ALU.subtract, ALU.mult)
-            return product
+        window, lower, square, hearth, upper = {}, {}, {}, {}, {}
+        first_term = [keep.tile([P, PACK, M], F32, name="first_term%d" % a) for a in range(2)]
+        second_term = [keep.tile([P, PACK, M], F32, name="second_term%d" % a) for a in range(2)]
 
-        def finish_odd(s, product, sig_upper):
-            a, t = divmod(s, PACK)
-            total = work.tile([P, M], F32, name="odd_total")
-            for cols, entries in halves:
-                nc.vector.scalar_tensor_tensor(total[:, cols], sig_upper[:, cols], 0.5, product[:, cols],
-                                               ALU.subtract, ALU.add)
-            for cols, entries in halves:
-                nc.vector.tensor_scalar(z[a][:, t, cols], total[:, cols], gain_t[:, a, t:t + 1], 2.0,
-                                        ALU.mult, ALU.mult)
+        def entries(c0, c1):
+            return slice(c0 // LANES, c1 // LANES)
+
+        def temp(name, t):
+            return work.tile([P, M], F32, name="%s%d" % (name, t), bufs=2)
+
+        def multiply(a, t):
+            for u in range(2):
+                open_sums(a, t, u)
+                for b in range(3):
+                    first_stage_pass(a, t, u, b)
+
+        def leave(a, t, u, on_vector=False):
+            if u == 0:
+                window[a, t] = work.tile([P, S], F32, name="window%d" % t, bufs=2)
+            dst = window[a, t][:, u * BANK:(u + 1) * BANK]
+            if on_vector:
+                nc.vector.tensor_scalar(dst, sums[a, t, u][:], sign[:, a, t:t + 1], signed_bias[:, a, t:t + 1],
+                                        ALU.mult, ALU.add)
+            else:
+                nc.scalar.activation(dst, sums[a, t, u][:], ACT.Identity if t % 2 else ACT.Tanh,
+                                     scale=sign[:, a, t:t + 1], bias=signed_bias[:, a, t:t + 1])
+
+        def sigmoid(dst, a, t, places):
+            nc.scalar.activation(dst, window[a, t][:].indirect(places), ACT.Sigmoid, scale=2.0)
+
+        def pick_lower(a, t, c0, c1):
+            if c0 == 0:
+                lower[a, t] = temp("lower", t)
+            if t % 2:
+                sigmoid(lower[a, t][:, c0:c1], a, t, p1[:, entries(c0, c1)])
+            else:
+                nc.vector.tensor_copy(lower[a, t][:, c0:c1], window[a, t][:].indirect(p1[:, entries(c0, c1)]))
+
+        def square_lower(a, t, c0, c1):
+            if c0 == 0:
+                square[a, t] = temp("square", t)
+            if t % 2:
+                nc.scalar.activation(square[a, t][:, c0:c1], lower[a, t][:, c0:c1], ACT.Square,
+                                     scale=root2[:, a, t:t + 1], bias=minus_root[:, a, t:t + 1])
+            elif (a, t) == (1, 2):
+                nc.vector.scalar_tensor_tensor(square[a, t][:, c0:c1], lower[a, t][:, c0:c1], factor[:, a, t:t + 1],
+                                               lower[a, t][:, c0:c1], ALU.mult, ALU.mult)
+            else:
+                nc.scalar.activation(square[a, t][:, c0:c1], lower[a, t][:, c0:c1], ACT.Square,
+                                     scale=root[:, a, t:t + 1])
+
+        def pick_hearth(a, t, c0, c1):
+            if t % 2:
+                if c0 == 0:
+                    hearth[a, t] = temp("hearth", t)
+                sigmoid(hearth[a, t][:, c0:c1], a, t, p2[:, entries(c0, c1)])
+            else:
+                nc.vector.tensor_tensor(first_term[a][:, t, c0:c1], window[a, t][:].indirect(p2[:, entries(c0, c1)]),
+                                        square[a, t][:, c0:c1], ALU.mult)
+
+        def half_product(a, t, c0, c1):
+            nc.vector.scalar_tensor_tensor(first_term[a][:, t, c0:c1], hearth[a, t][:, c0:c1], 0.5,
+                                           square[a, t][:, c0:c1], ALU.subtract, ALU.mult)
+
+        def pick_upper(a, t, c0, c1):
+            if t % 2:
+                if c0 == 0:
+                    upper[a, t] = temp("upper", t)
+                sigmoid(upper[a, t][:, c0:c1], a, t, p3[:, entries(c0, c1)])
+            else:
+                nc.vector.tensor_tensor(second_term[a][:, t, c0:c1],
+                                        window[a, t][:].indirect(p3[:, entries(c0, c1)]),
+                                        spread[a, t][:, c0:c1], ALU.mult)
+
+        def scale_upper(a, t, c0, c1):
+            nc.vector.tensor_scalar(second_term[a][:, t, c0:c1], upper[a, t][:, c0:c1], 0.5, factor[:, a, t:t + 1],
+                                    ALU.subtract, ALU.mult)
 
         woven = [keep.tile([P, M, PACK], BF16, name="woven%d" % a, align_bytes=64) for a in range(2)]
         z_codes = [keep.tile([P, M], U32, name="z_codes%d" % a, align_bytes=64) for a in range(2)]
         z_plane = [keep.tile([P, M], U8, name="z_plane%d" % a, align_bytes=64) for a in range(2)]
         results = {}
 
-        def weave(copy, a, cols):
-            copy(woven[a][:, cols, :].rearrange("p (c i) t -> p c t i", i=4),
-                 z[a][:, :, cols].rearrange("p t (c i) -> p c t i", i=4))
+        def weave(a, c0, c1):
+            nc.vector.tensor_tensor(woven[a][:, c0:c1, :].rearrange("p (c i) t -> p c t i", i=4),
+                                    first_term[a][:, :, c0:c1].rearrange("p t (c i) -> p c t i", i=4),
+                                    second_term[a][:, :, c0:c1].rearrange("p t (c i) -> p c t i", i=4), ALU.add)
 
-        def quantize_z(a, cols):
-            nc.vector.quantize_mx(out=z_codes[a][:, cols].bitcast(FP8X4), scales=z_plane[a][:, cols],
-                                  in_=woven[a][:, cols, :].rearrange("p m t -> p (m t)"))
+        def quantize_z(a, c0, c1):
+            nc.vector.quantize_mx(out=z_codes[a][:, c0:c1].bitcast(FP8X4), scales=z_plane[a][:, c0:c1],
+                                  in_=woven[a][:, c0:c1, :].rearrange("p m t -> p (m t)"))
 
-        def second_stage_pass(a, u):
-            cols = halves[u][0]
+        def second_stage_pass(a, i):
+            c0, c1 = PIECES[i]
             for n in range(N // P):
-                if a == 0:
-                    results[u, n] = psum.tile([P, HALF], F32, name="bank%d" % (4 * u + n))
-                nc.tensor.matmul_mx(out=results[u, n][:], lhsT=w3_codes[:, a, n * P:(n + 1) * P].bitcast(FP8X4),
+                k, side = divmod(n, 2)
+                if a == 0 and side == 0:
+                    results[i, k] = psum.tile([P, 2, c1 - c0], F32, name="bank%d" % (2 * i + k))
+                nc.tensor.matmul_mx(out=results[i, k][:, side, :],
+                                    lhsT=w3_codes[:, a, n * P:(n + 1) * P].bitcast(FP8X4),
                                     lhsT_scale=w3_planes[4 * a:P, n * P:(n + 1) * P],
-                                    rhs=z_codes[a][:, cols].bitcast(FP8X4), rhs_scale=z_plane[a][:, cols],
-                                    start=a == 0, stop=a == 1)
+                                    rhs=z_codes[a][:, c0:c1].bitcast(FP8X4), rhs_scale=z_plane[a][:, c0:c1],
+                                    start=a == 0 and side == 0, stop=a == 1 and side == 1)
 
-        def store(u):
-            cols = halves[u][0]
-            for pair, copy in enumerate((nc.scalar.copy, nc.vector.tensor_copy)):
-                staged = keep.tile([P, 2, HALF], F32, name="staged%d%d" % (u, pair))
-                for i in range(2):
-                    copy(staged[:, i, :], results[u, 2 * pair + i][:])
-                rows = out[2 * pair * P:(2 * pair + 2) * P, cols]
-                nc.sync.dma_start(rows.rearrange("(n p) m -> p n m", p=P), staged[:])
+        def store(i, copies):
+            c0, c1 = PIECES[i]
+            staged = keep.tile([P, N // P, c1 - c0], F32, name="staged%d" % i)
+            for k, copy in enumerate(copies):
+                copy(staged[:, 2 * k:2 * k + 2, :], results[i, k][:])
+            nc.sync.dma_start(out[:, c0:c1].rearrange("(n p) m -> p n m", p=P), staged[:])
 
-        for b in range(2):
-            activate(b)
-            rounded = shared.tile([P, PACK, P, PACK], BF16, name="w1_rounded1%d" % b, align_bytes=64,
-                                  offset=AT_ROUNDED[1])
+        def prepare_w1(b):
+            rounded = new_rounded()
             round_w1(nc.vector.tensor_copy, rounded, w1_raw[1, b], 0, P)
-            codes = keep.tile([P, KP], U32, name="w1_codes1%d" % b, align_bytes=64)
-            w1_mx[1, b] = quantize_w1(rounded, codes, "w1_plane1%d" % b, 1)
-        activate(2)
-        for s in range(1, SLICES, 2):
-            last = s + 1 == SLICES
-            sig_lower = pick_sigmoid(s, p1, "sig_lower", whole)
-            combine_even(s - 1)
-            sig_hearth = pick_sigmoid(s, p2, "sig_hearth", whole)
-            product = half_product(sig_lower, sig_hearth)
-            if s + 3 < SLICES:
-                activate(s + 3)
-            sig_upper = pick_sigmoid(s, p3, "sig_upper", halves if last else whole)
-            if not last:
-                activate(s + 2)
-            finish_odd(s, product, sig_upper)
-            if s + 1 == PACK:
-                weave(nc.vector.tensor_copy, 0, whole[0][0])
-                quantize_z(0, whole[0][0])
-            if s + 2 == SLICES - 1:
-                second_stage_pass(0, 0)
-                second_stage_pass(0, 1)
-        for u in range(2):
-            split = u * HALF + WEAVE_ON_SCALAR
-            weave(nc.scalar.copy, 1, slice(u * HALF, split))
-            weave(nc.vector.tensor_copy, 1, slice(split, (u + 1) * HALF))
-            quantize_z(1, halves[u][0])
-            second_stage_pass(1, u)
-        store(0)
-        store(1)
+            quantize_w1(rounded, 1, b)
+
+        leave(0, 0, 0)
+        leave(0, 1, 0)
+        leave(0, 0, 1)
+        leave(0, 1, 1, True)
+        for a in range(2):
+            leave(a, 2, 0)
+            leave(a, 2, 1)
+            pick_lower(a, 0, 0, M)
+            if a == 0:
+                prepare_w1(0)
+            pick_lower(a, 1, 0, M)
+            pick_lower(a, 2, 0, M)
+            if a == 0:
+                prepare_w1(1)
+            else:
+                weave(0, 0, M)
+                quantize_z(0, 0, M)
+            square_lower(a, 0, 0, M)
+            square_lower(a, 1, 0, M)
+            pick_hearth(a, 1, 0, M)
+            pick_upper(a, 0, 0, M)
+            pick_hearth(a, 0, 0, M)
+            square_lower(a, 2, 0, M)
+            pick_upper(a, 1, 0, M)
+            leave(a, 3, 0)
+            leave(a, 3, 1)
+            if a == 0:
+                for t in range(PACK):
+                    multiply(1, t)
+            else:
+                for i in range(len(PIECES)):
+                    second_stage_pass(0, i)
+            half_product(a, 1, 0, M)
+            scale_upper(a, 1, 0, M)
+            pick_hearth(a, 2, 0, M)
+            pick_upper(a, 2, 0, M)
+            for i, (c0, c1) in enumerate(PIECES if a == 1 else [(0, M)]):
+                pick_lower(a, 3, c0, c1)
+                pick_hearth(a, 3, c0, c1)
+                square_lower(a, 3, c0, c1)
+                pick_upper(a, 3, c0, c1)
+                half_product(a, 3, c0, c1)
+                scale_upper(a, 3, c0, c1)
+                if a == 1:
+                    weave(1, c0, c1)
+                    quantize_z(1, c0, c1)
+                    second_stage_pass(1, i)
+            if a == 0:
+                for t in range(2):
+                    leave(1, t, 0)
+                    leave(1, t, 1)
+        for i in range(len(PIECES)):
+            store(i, (nc.scalar.copy, nc.vector.tensor_copy if i + 1 == len(PIECES) else nc.scalar.copy))

@@ -27,11 +27,12 @@ PIECES = ((0, 256), (256, 384), (384, 512))
 
 
 KB = 1024
-AT_TABLE = (0, 37 * KB, 3 * KB)
+ROUND_ON_SCALAR = 20
+AT_TABLE = (0, 37 * KB, 2 * KB)
 AT_PICKED_PLANES = 0
 AT_TABLE_PLANES = 16 * KB
 AT_BIAS, AT_GAIN = 36 * KB + 512, 36 * KB + 576
-AT_W1_EARLY = 20 * KB + 512
+AT_W1_EARLY = (28 * KB + 512, 18 * KB)
 AT_W2_RAW = 36 * KB
 AT_W1_LATE = (37 * KB, 50 * KB + 512)
 AT_W3_PLANES = 45 * KB
@@ -60,8 +61,8 @@ def tile_list_site_phasing_kernel(tc, tab_words, tab_scales, offs, pos1, pos2, p
             words = tab_words[a].rearrange("p t i -> p (t i)").bitcast(I32)
             nc.sync.dma_start(tile[:].bitcast(I32)[:, cols], words[:, cols])
 
-        def load_w1(dst, a, b):
-            rows = w1[b * KP:(b + 1) * KP, a * KP:(a + 1) * KP]
+        def load_w1(dst, b, c0, c1):
+            rows = w1[b * KP:(b + 1) * KP, c0:c1]
             raw = dst.rearrange("p (j c) -> p j c", j=PACK)
             nc.sync.dma_start(raw, rows.rearrange("(p j) c -> p j c", j=PACK))
             return raw
@@ -97,8 +98,8 @@ def tile_list_site_phasing_kernel(tc, tab_words, tab_scales, offs, pos1, pos2, p
             nc.vector.tensor_copy(dst.rearrange("p (a t m) -> p a t m", a=2, t=PACK),
                                   src.rearrange("p (a m t) -> p a t m", a=2, t=PACK))
 
-        def round_w1(copy, rounded, raw, m0, m1):
-            src = raw[:, :, PACK * m0:PACK * m1].rearrange("p j (m t) -> p m j t", t=PACK)
+        def round_w1(copy, rounded, raw, m0, m1, first=0):
+            src = raw[:, :, PACK * (m0 - first):PACK * (m1 - first)].rearrange("p j (m t) -> p m j t", t=PACK)
             copy(rounded[:].rearrange("p t m j -> p m j t")[:, m0:m1], src)
 
         def new_rounded():
@@ -106,17 +107,21 @@ def tile_list_site_phasing_kernel(tc, tab_words, tab_scales, offs, pos1, pos2, p
 
         w1_mx = {}
 
-        def quantize_w1(rounded, a, b):
+        def quantize_w1(rounded, a, b, pieces=1):
             codes = keep.tile([P, KP], U32, name="w1_codes%d%d" % (a, b), align_bytes=64)
             plane = keep.tile([P, KP], U8, name="w1_plane%d%d" % (a, b), align_bytes=64)
-            nc.vector.quantize_mx(out=codes[:].bitcast(FP8X4), scales=plane[:],
-                                  in_=rounded[:].rearrange("p t m j -> p (t m j)"))
+            flat = rounded[:].rearrange("p t m j -> p (t m j)")
+            width = KP // pieces
+            for i in range(pieces):
+                cols = slice(i * width, (i + 1) * width)
+                nc.vector.quantize_mx(out=codes[:, cols].bitcast(FP8X4), scales=plane[:, cols],
+                                      in_=flat[:, PACK * i * width:PACK * (i + 1) * width])
             w1_mx[a, b] = codes, plane
 
         w2_codes = keep.tile([P, 2 * H], U8, name="w2_codes", align_bytes=64)
         in_slice_order(w2_codes[:].bitcast(U16), w2_raw[:].bitcast(U16))
-        w1_early = shared.tile([P, 2 * PACK * KP], F32, name="w1_early", align_bytes=64, offset=AT_W1_EARLY)
-        w1_raw = {(0, b): load_w1(w1_early[:, b * PACK * KP:(b + 1) * PACK * KP], 0, b) for b in range(2)}
+        early = shared.tile([P, PACK * KP], F32, name="w1_early0", align_bytes=64, offset=AT_W1_EARLY[0])
+        w1_raw = {(0, 0): load_w1(early[:], 0, 0, KP)}
         bias_t = shared.tile([P, 2, PACK], F32, name="bias_t", align_bytes=64, offset=AT_BIAS)
         gain_t = shared.tile([P, 2, PACK], F32, name="gain_t", align_bytes=64, offset=AT_GAIN)
         nc.sync.dma_start(gain_t[:], gain.rearrange("(a p t) -> p a t", p=P, t=PACK))
@@ -131,10 +136,11 @@ def tile_list_site_phasing_kernel(tc, tab_words, tab_scales, offs, pos1, pos2, p
         nc.sync.dma_start(picked_plane2[0:P - down, :].bitcast(I32), picked_planes[down:P, :].bitcast(I32))
         table[W2_PASS] = new_table(W2_PASS)
         load_table(table[W2_PASS], W2_PASS, slice(0, T))
-        for b in range(2):
-            rounded = new_rounded()
-            round_w1(nc.scalar.copy, rounded, w1_raw[0, b], 0, P)
-            quantize_w1(rounded, 0, b)
+        early = shared.tile([P, PACK * KP], F32, name="w1_early1", align_bytes=64, offset=AT_W1_EARLY[1])
+        last_raw = [load_w1(early[:, h * 2 * KP:(h + 1) * 2 * KP], 1, h * KP // 2, (h + 1) * KP // 2) for h in range(2)]
+        rounded = new_rounded()
+        round_w1(nc.scalar.copy, rounded, w1_raw[0, 0], 0, P)
+        quantize_w1(rounded, 0, 0)
 
         def per_row(name):
             return keep.tile([P, 2, PACK], F32, name=name)
@@ -173,7 +179,7 @@ def tile_list_site_phasing_kernel(tc, tab_words, tab_scales, offs, pos1, pos2, p
                 rhs_plane = picked_planes[4 * b:P, cols]
             nc.tensor.matmul_mx(out=sums[a, t, u][:], lhsT=lhs, lhsT_scale=lhs_plane,
                                 rhs=picked[b][:, cols].bitcast(FP8X4), rhs_scale=rhs_plane,
-                                start=b == 0, stop=b == W2_PASS)
+                                start=b == 0, stop=b == (1 if (a, t // 2) == (0, 0) else W2_PASS))
 
         for t in range(PACK):
             for u in range(2):
@@ -188,15 +194,12 @@ def tile_list_site_phasing_kernel(tc, tab_words, tab_scales, offs, pos1, pos2, p
 
         picked[1] = keep.tile([P, S], U32, name="picked_codes1", align_bytes=64)
         picked[W2_PASS] = keep.tile([P, S], U32, name="picked_codes2", align_bytes=64)
-        for u in range(2):
-            gather_half(1, u)
-            for t in range(PACK):
-                first_stage_pass(0, t, u, 1)
+        nc.vector.tensor_copy(picked[1][:], table[1][:].indirect(offs_t[:]))
         w2_plane = shared.tile([P, H], U8, name="w2_plane", align_bytes=64, offset=AT_W2_PLANE)
         in_slice_order(w2_plane[:], w2_plane_raw[:])
         for b in range(2):
             late = shared.tile([P, PACK * KP], F32, name="w1_late%d" % b, align_bytes=64, offset=AT_W1_LATE[b])
-            w1_raw[1, b] = load_w1(late[:], 1, b)
+            w1_raw[1, b] = load_w1(late[:], b, KP, 2 * KP)
         w3_codes = shared.tile([P, 2, N], U32, name="w3_codes", align_bytes=64, offset=AT_W3_CODES)
         nc.sync.dma_start(w3_codes[:].bitcast(I32), w3_words.rearrange("a p c i -> p a (c i)").bitcast(I32))
         w3_planes = shared.tile([P, N], U8, name="w3_planes", align_bytes=64, offset=AT_W3_PLANES)
@@ -206,9 +209,16 @@ def tile_list_site_phasing_kernel(tc, tab_words, tab_scales, offs, pos1, pos2, p
             gather_half(W2_PASS, u)
             for t in range(2):
                 first_stage_pass(0, t, u, W2_PASS)
-        for t in range(2, PACK):
+        rounded = new_rounded()
+        round_w1(nc.scalar.copy, rounded, last_raw[0], 0, P // 2)
+        round_w1(nc.scalar.copy, rounded, last_raw[1], P // 2, P // 2 + ROUND_ON_SCALAR, P // 2)
+        round_w1(nc.vector.tensor_copy, rounded, last_raw[1], P // 2 + ROUND_ON_SCALAR, P, P // 2)
+        quantize_w1(rounded, 0, 1, 2)
+        for t in range(PACK):
             for u in range(2):
-                first_stage_pass(0, t, u, W2_PASS)
+                first_stage_pass(0, t, u, 1)
+                if t >= 2:
+                    first_stage_pass(0, t, u, W2_PASS)
 
         window, lower, square, hearth, upper = {}, {}, {}, {}, {}
         first_term = [keep.tile([P, PACK, M], F32, name="first_term%d" % a) for a in range(2)]
@@ -294,9 +304,9 @@ def tile_list_site_phasing_kernel(tc, tab_words, tab_scales, offs, pos1, pos2, p
         results = {}
 
         def weave(a, c0, c1):
-            nc.vector.tensor_tensor(woven[a][:, c0:c1, :].rearrange("p (c i) t -> p c t i", i=4),
-                                    first_term[a][:, :, c0:c1].rearrange("p t (c i) -> p c t i", i=4),
-                                    second_term[a][:, :, c0:c1].rearrange("p t (c i) -> p c t i", i=4), ALU.add)
+            nc.vector.tensor_tensor(woven[a][:, c0:c1, :].rearrange("p (c i) t -> p c t i", i=2),
+                                    first_term[a][:, :, c0:c1].rearrange("p t (c i) -> p c t i", i=2),
+                                    second_term[a][:, :, c0:c1].rearrange("p t (c i) -> p c t i", i=2), ALU.add)
 
         def quantize_z(a, c0, c1):
             nc.vector.quantize_mx(out=z_codes[a][:, c0:c1].bitcast(FP8X4), scales=z_plane[a][:, c0:c1],
@@ -317,9 +327,11 @@ def tile_list_site_phasing_kernel(tc, tab_words, tab_scales, offs, pos1, pos2, p
         def store(i, copies):
             c0, c1 = PIECES[i]
             staged = keep.tile([P, N // P, c1 - c0], F32, name="staged%d" % i)
+            rows = out[:, c0:c1].rearrange("(n p) m -> p n m", p=P)
             for k, copy in enumerate(copies):
                 copy(staged[:, 2 * k:2 * k + 2, :], results[i, k][:])
-            nc.sync.dma_start(out[:, c0:c1].rearrange("(n p) m -> p n m", p=P), staged[:])
+                queue = nc.scalar if (i + 1, k) == (len(PIECES), 0) else nc.sync
+                queue.dma_start(rows[:, 2 * k:2 * k + 2, :], staged[:, 2 * k:2 * k + 2, :])
 
         def prepare_w1(b):
             rounded = new_rounded()
@@ -327,8 +339,8 @@ def tile_list_site_phasing_kernel(tc, tab_words, tab_scales, offs, pos1, pos2, p
             quantize_w1(rounded, 1, b)
 
         leave(0, 0, 0)
-        leave(0, 1, 0)
         leave(0, 0, 1)
+        leave(0, 1, 0, True)
         leave(0, 1, 1, True)
         for a in range(2):
             leave(a, 2, 0)

@@ -27,12 +27,11 @@ PIECES = ((0, 256), (256, 384), (384, 512))
 
 
 KB = 1024
-ROUND_ON_SCALAR = 20
 AT_TABLE = (0, 37 * KB, 2 * KB)
 AT_PICKED_PLANES = 0
 AT_TABLE_PLANES = 16 * KB
-AT_BIAS, AT_GAIN = 36 * KB + 512, 36 * KB + 576
-AT_W1_EARLY = (28 * KB + 512, 18 * KB)
+AT_BIAS, AT_GAIN = 18 * KB, 36 * KB + 576
+AT_W1_EARLY = (28 * KB + 512, 18 * KB + 64)
 AT_W2_RAW = 36 * KB
 AT_W1_LATE = (37 * KB, 50 * KB + 512)
 AT_W3_PLANES = 45 * KB
@@ -98,9 +97,9 @@ def tile_list_site_phasing_kernel(tc, tab_words, tab_scales, offs, pos1, pos2, p
             nc.vector.tensor_copy(dst.rearrange("p (a t m) -> p a t m", a=2, t=PACK),
                                   src.rearrange("p (a m t) -> p a t m", a=2, t=PACK))
 
-        def round_w1(copy, rounded, raw, m0, m1, first=0):
+        def round_w1(copy, rounded, raw, m0, m1, first=0, slices=slice(0, PACK)):
             src = raw[:, :, PACK * (m0 - first):PACK * (m1 - first)].rearrange("p j (m t) -> p m j t", t=PACK)
-            copy(rounded[:].rearrange("p t m j -> p m j t")[:, m0:m1], src)
+            copy(rounded[:].rearrange("p t m j -> p m j t")[:, m0:m1, :, slices], src[:, :, :, slices])
 
         def new_rounded():
             return work.tile([P, PACK, P, PACK], BF16, name="w1_rounded", align_bytes=64, bufs=2)
@@ -122,10 +121,8 @@ def tile_list_site_phasing_kernel(tc, tab_words, tab_scales, offs, pos1, pos2, p
         in_slice_order(w2_codes[:].bitcast(U16), w2_raw[:].bitcast(U16))
         early = shared.tile([P, PACK * KP], F32, name="w1_early0", align_bytes=64, offset=AT_W1_EARLY[0])
         w1_raw = {(0, 0): load_w1(early[:], 0, 0, KP)}
-        bias_t = shared.tile([P, 2, PACK], F32, name="bias_t", align_bytes=64, offset=AT_BIAS)
         gain_t = shared.tile([P, 2, PACK], F32, name="gain_t", align_bytes=64, offset=AT_GAIN)
         nc.sync.dma_start(gain_t[:], gain.rearrange("(a p t) -> p a t", p=P, t=PACK))
-        nc.sync.dma_start(bias_t[:], bias.rearrange("(a p t) -> p a t", p=P, t=PACK))
         table[1] = new_table(1)
         load_table(table[1], 1, slice(0, T))
         picked = {0: keep.tile([P, S], U32, name="picked_codes0", align_bytes=64)}
@@ -133,11 +130,15 @@ def tile_list_site_phasing_kernel(tc, tab_words, tab_scales, offs, pos1, pos2, p
         picked_planes = shared.tile([P, S], U8, name="picked_planes", align_bytes=64, offset=AT_PICKED_PLANES)
         nc.vector.tensor_copy(picked_planes[:], table_planes[:].indirect(offs_t[:]))
         down = 4 * W2_PASS
-        nc.sync.dma_start(picked_plane2[0:P - down, :].bitcast(I32), picked_planes[down:P, :].bitcast(I32))
+        for q in range(QUADRANTS):
+            nc.scalar.dma_start(picked_plane2[32 * q:32 * q + 4, :].bitcast(I32),
+                                picked_planes[32 * q + down:32 * q + down + 4, :].bitcast(I32))
         table[W2_PASS] = new_table(W2_PASS)
         load_table(table[W2_PASS], W2_PASS, slice(0, T))
         early = shared.tile([P, PACK * KP], F32, name="w1_early1", align_bytes=64, offset=AT_W1_EARLY[1])
         last_raw = [load_w1(early[:, h * 2 * KP:(h + 1) * 2 * KP], 1, h * KP // 2, (h + 1) * KP // 2) for h in range(2)]
+        bias_t = shared.tile([P, 2, PACK], F32, name="bias_t", align_bytes=64, offset=AT_BIAS)
+        nc.sync.dma_start(bias_t[:], bias.rearrange("(a p t) -> p a t", p=P, t=PACK))
         rounded = new_rounded()
         round_w1(nc.scalar.copy, rounded, w1_raw[0, 0], 0, P)
         quantize_w1(rounded, 0, 0)
@@ -152,10 +153,10 @@ def tile_list_site_phasing_kernel(tc, tab_words, tab_scales, offs, pos1, pos2, p
         nc.gpsimd.tensor_scalar(sign[:], sign[:], -1.0, 1.0, ALU.add, ALU.mult)
         nc.gpsimd.tensor_tensor(factor[:], gain_t[:], sign[:], ALU.mult)
         nc.gpsimd.tensor_scalar(factor[:, :, 1::2], factor[:, :, 1::2], 2.0, 0.0, ALU.mult, ALU.add)
-        nc.gpsimd.tensor_tensor(signed_bias[:], bias_t[:], sign[:], ALU.mult)
         nc.gpsimd.tensor_tensor(root[:], factor[:], half[:], ALU.pow)
         nc.gpsimd.tensor_scalar(root2[:], root[:], 2.0, 0.0, ALU.mult, ALU.add)
         nc.gpsimd.tensor_scalar(minus_root[:], root[:], -1.0, 0.0, ALU.mult, ALU.add)
+        nc.gpsimd.tensor_tensor(signed_bias[:], bias_t[:], sign[:], ALU.mult)
         spread = {}
         for a in range(2):
             for t in range(0, PACK, 2):
@@ -211,8 +212,8 @@ def tile_list_site_phasing_kernel(tc, tab_words, tab_scales, offs, pos1, pos2, p
                 first_stage_pass(0, t, u, W2_PASS)
         rounded = new_rounded()
         round_w1(nc.scalar.copy, rounded, last_raw[0], 0, P // 2)
-        round_w1(nc.scalar.copy, rounded, last_raw[1], P // 2, P // 2 + ROUND_ON_SCALAR, P // 2)
-        round_w1(nc.vector.tensor_copy, rounded, last_raw[1], P // 2 + ROUND_ON_SCALAR, P, P // 2)
+        round_w1(nc.vector.tensor_copy, rounded, last_raw[1], P // 2, P, P // 2, slice(0, 2))
+        round_w1(nc.scalar.copy, rounded, last_raw[1], P // 2, P, P // 2, slice(2, PACK))
         quantize_w1(rounded, 0, 1, 2)
         for t in range(PACK):
             for u in range(2):
@@ -221,8 +222,10 @@ def tile_list_site_phasing_kernel(tc, tab_words, tab_scales, offs, pos1, pos2, p
                     first_stage_pass(0, t, u, W2_PASS)
 
         window, lower, square, hearth, upper = {}, {}, {}, {}, {}
-        first_term = [keep.tile([P, PACK, M], F32, name="first_term%d" % a) for a in range(2)]
-        second_term = [keep.tile([P, PACK, M], F32, name="second_term%d" % a) for a in range(2)]
+        first_term, second_term = {}, {}
+
+        def new_term(name, at):
+            return shared.tile([P, PACK, M], F32, name=name, align_bytes=64, offset=at)
 
         def entries(c0, c1):
             return slice(c0 // LANES, c1 // LANES)
@@ -333,10 +336,6 @@ def tile_list_site_phasing_kernel(tc, tab_words, tab_scales, offs, pos1, pos2, p
                 queue = nc.scalar if (i + 1, k) == (len(PIECES), 0) else nc.sync
                 queue.dma_start(rows[:, 2 * k:2 * k + 2, :], staged[:, 2 * k:2 * k + 2, :])
 
-        def prepare_w1(b):
-            rounded = new_rounded()
-            round_w1(nc.vector.tensor_copy, rounded, w1_raw[1, b], 0, P)
-            quantize_w1(rounded, 1, b)
 
         leave(0, 0, 0)
         leave(0, 0, 1)
@@ -346,24 +345,32 @@ def tile_list_site_phasing_kernel(tc, tab_words, tab_scales, offs, pos1, pos2, p
             leave(a, 2, 0)
             leave(a, 2, 1)
             pick_lower(a, 0, 0, M)
-            if a == 0:
-                prepare_w1(0)
             pick_lower(a, 1, 0, M)
             pick_lower(a, 2, 0, M)
-            if a == 0:
-                prepare_w1(1)
-            else:
-                weave(0, 0, M)
-                quantize_z(0, 0, M)
             square_lower(a, 0, 0, M)
             square_lower(a, 1, 0, M)
             pick_hearth(a, 1, 0, M)
+            if a == 0:
+                rounded = new_rounded()
+                round_w1(nc.vector.tensor_copy, rounded, w1_raw[1, 0], 0, P)
+            else:
+                weave(0, 0, M)
+            second_term[a] = new_term("second_term%d" % a, AT_W1_LATE[0])
             pick_upper(a, 0, 0, M)
+            if a == 0:
+                quantize_w1(rounded, 1, 0)
+                rounded = new_rounded()
+                round_w1(nc.vector.tensor_copy, rounded, w1_raw[1, 1], 0, P)
+            else:
+                quantize_z(0, 0, M)
+            first_term[a] = new_term("first_term%d" % a, AT_W1_LATE[1])
             pick_hearth(a, 0, 0, M)
+            if a == 0:
+                quantize_w1(rounded, 1, 1)
             square_lower(a, 2, 0, M)
-            pick_upper(a, 1, 0, M)
             leave(a, 3, 0)
             leave(a, 3, 1)
+            pick_upper(a, 1, 0, M)
             if a == 0:
                 for t in range(PACK):
                     multiply(1, t)
@@ -382,12 +389,15 @@ def tile_list_site_phasing_kernel(tc, tab_words, tab_scales, offs, pos1, pos2, p
                 half_product(a, 3, c0, c1)
                 scale_upper(a, 3, c0, c1)
                 if a == 1:
+                    if i:
+                        quantize_z(1, *PIECES[i - 1])
+                        second_stage_pass(1, i - 1)
                     weave(1, c0, c1)
-                    quantize_z(1, c0, c1)
-                    second_stage_pass(1, i)
             if a == 0:
                 for t in range(2):
                     leave(1, t, 0)
                     leave(1, t, 1)
+        quantize_z(1, *PIECES[-1])
+        second_stage_pass(1, len(PIECES) - 1)
         for i in range(len(PIECES)):
             store(i, (nc.scalar.copy, nc.vector.tensor_copy if i + 1 == len(PIECES) else nc.scalar.copy))

@@ -156,6 +156,8 @@ def tile_list_site_phasing_kernel(tc, tab_words, tab_scales, offs, pos1, pos2, p
         nc.gpsimd.tensor_tensor(root[:], factor[:], half[:], ALU.pow)
         nc.gpsimd.tensor_scalar(root2[:], root[:], 2.0, 0.0, ALU.mult, ALU.add)
         nc.gpsimd.tensor_scalar(minus_root[:], root[:], -1.0, 0.0, ALU.mult, ALU.add)
+        minus_half_factor = per_row("minus_half_factor")
+        nc.gpsimd.tensor_scalar(minus_half_factor[:], factor[:], -0.5, 0.0, ALU.mult, ALU.add)
         nc.gpsimd.tensor_tensor(signed_bias[:], bias_t[:], sign[:], ALU.mult)
         spread = {}
         for a in range(2):
@@ -167,6 +169,11 @@ def tile_list_site_phasing_kernel(tc, tab_words, tab_scales, offs, pos1, pos2, p
 
         def open_sums(a, t, u):
             sums[a, t, u] = psum.tile([P, BANK], F32, name="bank%d" % (2 * t + u))
+
+        def pass_order(a, t):
+            if a == 1:
+                return W2_PASS, 0, 1
+            return (0, W2_PASS, 1) if t < 2 else (0, 1, W2_PASS)
 
         def first_stage_pass(a, t, u, b):
             cols = slice(u * BANK, (u + 1) * BANK)
@@ -180,7 +187,7 @@ def tile_list_site_phasing_kernel(tc, tab_words, tab_scales, offs, pos1, pos2, p
                 rhs_plane = picked_planes[4 * b:P, cols]
             nc.tensor.matmul_mx(out=sums[a, t, u][:], lhsT=lhs, lhsT_scale=lhs_plane,
                                 rhs=picked[b][:, cols].bitcast(FP8X4), rhs_scale=rhs_plane,
-                                start=b == 0, stop=b == (1 if (a, t // 2) == (0, 0) else W2_PASS))
+                                start=b == pass_order(a, t)[0], stop=b == pass_order(a, t)[-1])
 
         for t in range(PACK):
             for u in range(2):
@@ -236,7 +243,8 @@ def tile_list_site_phasing_kernel(tc, tab_words, tab_scales, offs, pos1, pos2, p
         def multiply(a, t):
             for u in range(2):
                 open_sums(a, t, u)
-                for b in range(3):
+            for b in pass_order(a, t):
+                for u in range(2):
                     first_stage_pass(a, t, u, b)
 
         def leave(a, t, u, on_vector=False):
@@ -298,6 +306,10 @@ def tile_list_site_phasing_kernel(tc, tab_words, tab_scales, offs, pos1, pos2, p
                                         spread[a, t][:, c0:c1], ALU.mult)
 
         def scale_upper(a, t, c0, c1):
+            if (a, t) == (1, 3):
+                nc.scalar.activation(second_term[a][:, t, c0:c1], upper[a, t][:, c0:c1], ACT.Identity,
+                                     scale=factor[:, a, t:t + 1], bias=minus_half_factor[:, a, t:t + 1])
+                return
             nc.vector.tensor_scalar(second_term[a][:, t, c0:c1], upper[a, t][:, c0:c1], 0.5, factor[:, a, t:t + 1],
                                     ALU.subtract, ALU.mult)
 

@@ -205,9 +205,11 @@ def tile_list_site_phasing_kernel(tc, tab_words, tab_scales, offs, pos1, pos2, p
         nc.vector.tensor_copy(picked[1][:], table[1][:].indirect(offs_t[:]))
         w2_plane = shared.tile([P, H], U8, name="w2_plane", align_bytes=64, offset=AT_W2_PLANE)
         in_slice_order(w2_plane[:], w2_plane_raw[:])
-        for b in range(2):
-            late = shared.tile([P, PACK * KP], F32, name="w1_late%d" % b, align_bytes=64, offset=AT_W1_LATE[b])
-            w1_raw[1, b] = load_w1(late[:], b, KP, 2 * KP)
+        late = shared.tile([P, PACK * KP], F32, name="w1_late0", align_bytes=64, offset=AT_W1_LATE[0])
+        late_raw = [load_w1(late[:, h * 2 * KP:(h + 1) * 2 * KP], 0, KP + h * KP // 2, KP + (h + 1) * KP // 2)
+                    for h in range(2)]
+        late = shared.tile([P, PACK * KP], F32, name="w1_late1", align_bytes=64, offset=AT_W1_LATE[1])
+        w1_raw[1, 1] = load_w1(late[:], 1, KP, 2 * KP)
         w3_codes = shared.tile([P, 2, N], U32, name="w3_codes", align_bytes=64, offset=AT_W3_CODES)
         nc.sync.dma_start(w3_codes[:].bitcast(I32), w3_words.rearrange("a p c i -> p a (c i)").bitcast(I32))
         w3_planes = shared.tile([P, N], U8, name="w3_planes", align_bytes=64, offset=AT_W3_PLANES)
@@ -349,6 +351,8 @@ def tile_list_site_phasing_kernel(tc, tab_words, tab_scales, offs, pos1, pos2, p
                 queue.dma_start(rows[:, 2 * k:2 * k + 2, :], staged[:, 2 * k:2 * k + 2, :])
 
 
+        rounded = shared.tile([P, PACK, P, PACK], BF16, name="w1_rounded10", align_bytes=64, offset=AT_W1_EARLY[1])
+        round_w1(nc.vector.tensor_copy, rounded, late_raw[0], 0, P // 2)
         leave(0, 0, 0)
         leave(0, 0, 1)
         leave(0, 1, 0, True)
@@ -363,8 +367,7 @@ def tile_list_site_phasing_kernel(tc, tab_words, tab_scales, offs, pos1, pos2, p
             square_lower(a, 1, 0, M)
             pick_hearth(a, 1, 0, M)
             if a == 0:
-                rounded = new_rounded()
-                round_w1(nc.vector.tensor_copy, rounded, w1_raw[1, 0], 0, P)
+                round_w1(nc.vector.tensor_copy, rounded, late_raw[1], P // 2, P, P // 2)
             else:
                 weave(0, 0, M)
             second_term[a] = new_term("second_term%d" % a, AT_W1_LATE[0])

@@ -277,7 +277,7 @@ def tile_list_site_phasing_kernel(tc, tab_words, tab_scales, offs, pos1, pos2, p
             if t % 2:
                 nc.scalar.activation(square[a, t][:, c0:c1], lower[a, t][:, c0:c1], ACT.Square,
                                      scale=root2[:, a, t:t + 1], bias=minus_root[:, a, t:t + 1])
-            elif (a, t) == (1, 2):
+            elif t == 2:
                 nc.vector.scalar_tensor_tensor(square[a, t][:, c0:c1], lower[a, t][:, c0:c1], factor[:, a, t:t + 1],
                                                lower[a, t][:, c0:c1], ALU.mult, ALU.mult)
             else:

@@ -23,7 +23,8 @@ BANK = 512
 QUADRANTS = 4
 LANES = 16
 W2_PASS = 2
-PIECES = ((0, 256), (256, 384), (384, 512))
+PIECES = ((0, 128), (128, 256), (256, 384), (384, 512))
+BLOCKS_IN_BANK = (4, 4, 2, 1)
 
 
 KB = 1024
@@ -331,25 +332,30 @@ def tile_list_site_phasing_kernel(tc, tab_words, tab_scales, offs, pos1, pos2, p
 
         def second_stage_pass(a, i):
             c0, c1 = PIECES[i]
+            share = BLOCKS_IN_BANK[i]
+            first_bank = sum(N // P // other for other in BLOCKS_IN_BANK[:i])
             for n in range(N // P):
-                k, side = divmod(n, 2)
+                k, side = divmod(n, share)
                 if a == 0 and side == 0:
-                    results[i, k] = psum.tile([P, 2, c1 - c0], F32, name="bank%d" % (2 * i + k))
+                    results[i, k] = psum.tile([P, share, c1 - c0], F32, name="bank%d" % (first_bank + k))
                 nc.tensor.matmul_mx(out=results[i, k][:, side, :],
                                     lhsT=w3_codes[:, a, n * P:(n + 1) * P].bitcast(FP8X4),
                                     lhsT_scale=w3_planes[4 * a:P, n * P:(n + 1) * P],
                                     rhs=z_codes[a][:, c0:c1].bitcast(FP8X4), rhs_scale=z_plane[a][:, c0:c1],
-                                    start=a == 0 and side == 0, stop=a == 1 and side == 1)
+                                    start=a == 0 and side == 0, stop=a == 1 and side == share - 1)
 
-        def store(i, copies):
+        def store(i):
             c0, c1 = PIECES[i]
+            share = BLOCKS_IN_BANK[i]
             staged = keep.tile([P, N // P, c1 - c0], F32, name="staged%d" % i)
             rows = out[:, c0:c1].rearrange("(n p) m -> p n m", p=P)
-            for k, copy in enumerate(copies):
-                copy(staged[:, 2 * k:2 * k + 2, :], results[i, k][:])
-                queue = nc.scalar if (i + 1, k) == (len(PIECES), 0) else nc.sync
-                queue.dma_start(rows[:, 2 * k:2 * k + 2, :], staged[:, 2 * k:2 * k + 2, :])
-
+            blocks = max(share, 2)
+            for n0 in range(0, N // P, blocks):
+                copy = nc.vector.tensor_copy if n0 + blocks < N // P else nc.scalar.copy
+                for n in range(n0, n0 + blocks, share):
+                    copy(staged[:, n:n + share, :], results[i, n // share][:])
+                queue = nc.scalar if i + 1 == len(PIECES) and n0 else nc.sync
+                queue.dma_start(rows[:, n0:n0 + blocks, :], staged[:, n0:n0 + blocks, :])
 
         rounded = shared.tile([P, PACK, P, PACK], BF16, name="w1_rounded10", align_bytes=64, offset=AT_W1_EARLY[1])
         round_w1(nc.vector.tensor_copy, rounded, late_raw[0], 0, P // 2)
@@ -415,4 +421,4 @@ def tile_list_site_phasing_kernel(tc, tab_words, tab_scales, offs, pos1, pos2, p
         quantize_z(1, *PIECES[-1])
         second_stage_pass(1, len(PIECES) - 1)
         for i in range(len(PIECES)):
-            store(i, (nc.scalar.copy, nc.vector.tensor_copy if i + 1 == len(PIECES) else nc.scalar.copy))
+            store(i)

@@ -150,16 +150,15 @@ def tile_list_site_phasing_kernel(tc, tab_words, tab_scales, offs, pos1, pos2, p
         sign, signed_bias, factor, half = per_row("sign"), per_row("signed_bias"), per_row("factor"), per_row("half")
         root, root2, minus_root = per_row("root"), per_row("root2"), per_row("minus_root")
         nc.gpsimd.memset(half[:], 0.5)
-        nc.gpsimd.tensor_scalar(sign[:], gain_t[:], 0.0, 2.0, ALU.is_ge, ALU.mult)
-        nc.gpsimd.tensor_scalar(sign[:], sign[:], -1.0, 1.0, ALU.add, ALU.mult)
-        nc.gpsimd.tensor_tensor(factor[:], gain_t[:], sign[:], ALU.mult)
-        nc.gpsimd.tensor_scalar(factor[:, :, 1::2], factor[:, :, 1::2], 2.0, 0.0, ALU.mult, ALU.add)
+        nc.vector.tensor_scalar(sign[:], gain_t[:], 0.0, 2.0, ALU.is_ge, ALU.mult)
+        nc.vector.tensor_scalar(sign[:], sign[:], -1.0, None, ALU.add)
+        nc.vector.tensor_tensor(factor[:], gain_t[:], sign[:], ALU.mult)
+        nc.vector.tensor_scalar(factor[:, :, 1::2], factor[:, :, 1::2], 2.0, None, ALU.mult)
         nc.gpsimd.tensor_tensor(root[:], factor[:], half[:], ALU.pow)
         nc.gpsimd.tensor_scalar(root2[:], root[:], 2.0, 0.0, ALU.mult, ALU.add)
         nc.gpsimd.tensor_scalar(minus_root[:], root[:], -1.0, 0.0, ALU.mult, ALU.add)
         minus_half_factor = per_row("minus_half_factor")
         nc.gpsimd.tensor_scalar(minus_half_factor[:], factor[:], -0.5, 0.0, ALU.mult, ALU.add)
-        nc.gpsimd.tensor_tensor(signed_bias[:], bias_t[:], sign[:], ALU.mult)
         spread = {}
         for a in range(2):
             for t in range(0, PACK, 2):
@@ -224,6 +223,7 @@ def tile_list_site_phasing_kernel(tc, tab_words, tab_scales, offs, pos1, pos2, p
         round_w1(nc.scalar.copy, rounded, last_raw[0], 0, P // 2)
         round_w1(nc.vector.tensor_copy, rounded, last_raw[1], P // 2, P, P // 2, slice(0, 2))
         round_w1(nc.scalar.copy, rounded, last_raw[1], P // 2, P, P // 2, slice(2, PACK))
+        nc.vector.tensor_tensor(signed_bias[:], bias_t[:], sign[:], ALU.mult)
         quantize_w1(rounded, 0, 1, 2)
         for t in range(PACK):
             for u in range(2):

@@ -28,16 +28,20 @@ BLOCKS_IN_BANK = (4, 4, 2, 1)
 
 
 KB = 1024
-AT_TABLE = (0, 37 * KB, 2 * KB)
+AT_TABLE = (0, 39 * KB, 2 * KB)
 AT_PICKED_PLANES = 0
 AT_TABLE_PLANES = 16 * KB
-AT_BIAS, AT_GAIN = 18 * KB, 36 * KB + 576
-AT_W1_EARLY = (28 * KB + 512, 18 * KB + 64)
-AT_W2_RAW = 36 * KB
-AT_W1_LATE = (37 * KB, 50 * KB + 512)
-AT_W3_PLANES = 45 * KB
-AT_W2_PLANE = 45 * KB + 512
-AT_W3_CODES = 46 * KB + 512
+FIRST_PLANE = 4
+PLANES_TILE = 6 * KB + 256
+AT_BIAS, AT_GAIN = 18 * KB, 38 * KB + 576
+AT_ROUNDED = 18 * KB + 64
+AT_W1_EARLY = (30 * KB + 512, 22 * KB + 64)
+AT_W2_RAW = 38 * KB
+AT_W1_LATE = (39 * KB, 52 * KB + 512)
+AT_W3_PLANES = 47 * KB
+AT_W2_PLANE = (47 * KB + 512, 2 * KB)
+AT_W1_PLANE = 48 * KB
+AT_W3_CODES = 48 * KB + 512
 
 
 def tile_list_site_phasing_kernel(tc, tab_words, tab_scales, offs, pos1, pos2, pos3, w1, w2_words,
@@ -67,17 +71,18 @@ def tile_list_site_phasing_kernel(tc, tab_words, tab_scales, offs, pos1, pos2, p
             nc.sync.dma_start(raw, rows.rearrange("(p j) c -> p j c", j=PACK))
             return raw
 
-        def load_planes(queues, planes, scales):
+        def load_planes(queues, planes, scales, first=0):
             rows = 4 * scales.shape[0]
             for q, queue in enumerate(queues):
-                queue.dma_start(planes[32 * q:32 * q + rows, :].bitcast(I32),
+                queue.dma_start(planes[32 * q + first:32 * q + first + rows, :].bitcast(I32),
                                 scales[:, 4 * q:4 * q + 4, :].bitcast(I32))
 
-        table_planes = shared.tile([P, T], U8, name="table_planes", align_bytes=64, offset=AT_TABLE_PLANES)
+        table_planes = shared.tile([P, PLANES_TILE], U8, name="table_planes", align_bytes=64,
+                                   offset=AT_TABLE_PLANES)[:, 0:T]
         w2_plane_raw = keep.tile([P, H], U8, name="w2_plane_raw", align_bytes=64)
         picked_plane2 = keep.tile([P, S], U8, name="picked_plane2", align_bytes=64)
-        for plane in (table_planes, w2_plane_raw, picked_plane2):
-            nc.vector.memset(plane[:].bitcast(I32), 0)
+        for plane in (table_planes, w2_plane_raw[:], picked_plane2[:]):
+            nc.vector.memset(plane.bitcast(I32), 0)
         offs_t = load_list(offs, "offs_t")
         w2_raw = shared.tile([P, 2 * H], U8, name="w2_raw", align_bytes=64, offset=AT_W2_RAW)
         table = {0: new_table(0)}
@@ -87,7 +92,7 @@ def tile_list_site_phasing_kernel(tc, tab_words, tab_scales, offs, pos1, pos2, p
         p1 = load_list(pos1, "p1")
         p2 = load_list(pos2, "p2")
         p3 = load_list(pos3, "p3")
-        load_planes((nc.gpsimd, nc.gpsimd, nc.scalar, nc.scalar), table_planes, tab_scales)
+        load_planes((nc.gpsimd, nc.gpsimd, nc.scalar, nc.scalar), table_planes, tab_scales, FIRST_PLANE)
         load_planes([nc.gpsimd] * QUADRANTS, w2_plane_raw, w2_scales)
 
         warm = keep.tile([P, 2], F32, name="warm")
@@ -95,28 +100,30 @@ def tile_list_site_phasing_kernel(tc, tab_words, tab_scales, offs, pos1, pos2, p
         nc.scalar.activation(warm[:, 1:2], warm[:, 0:1], ACT.Sigmoid)
 
         def in_slice_order(dst, src):
-            nc.vector.tensor_copy(dst.rearrange("p (a t m) -> p a t m", a=2, t=PACK),
-                                  src.rearrange("p (a m t) -> p a t m", a=2, t=PACK))
+            nc.vector.tensor_copy(dst.rearrange("p (a t m) -> p a t m", m=P, t=PACK),
+                                  src.rearrange("p (a m t) -> p a t m", m=P, t=PACK))
 
         def round_w1(copy, rounded, raw, m0, m1, first=0, slices=slice(0, PACK)):
             src = raw[:, :, PACK * (m0 - first):PACK * (m1 - first)].rearrange("p j (m t) -> p m j t", t=PACK)
-            copy(rounded[:].rearrange("p t m j -> p m j t")[:, m0:m1, :, slices], src[:, :, :, slices])
+            copy(rounded[:].rearrange("p t m j -> p m j t")[:, m0:m1, :, :], src[:, :, :, slices])
 
         def new_rounded():
             return work.tile([P, PACK, P, PACK], BF16, name="w1_rounded", align_bytes=64, bufs=2)
 
         w1_mx = {}
 
-        def quantize_w1(rounded, a, b, pieces=1):
-            codes = keep.tile([P, KP], U32, name="w1_codes%d%d" % (a, b), align_bytes=64)
-            plane = keep.tile([P, KP], U8, name="w1_plane%d%d" % (a, b), align_bytes=64)
-            flat = rounded[:].rearrange("p t m j -> p (t m j)")
-            width = KP // pieces
-            for i in range(pieces):
-                cols = slice(i * width, (i + 1) * width)
-                nc.vector.quantize_mx(out=codes[:, cols].bitcast(FP8X4), scales=plane[:, cols],
-                                      in_=flat[:, PACK * i * width:PACK * (i + 1) * width])
-            w1_mx[a, b] = codes, plane
+        def quantize_w1(a, b, piece, first=0, at=None):
+            count = piece.shape[1]
+            codes = keep.tile([P, count * P], U32, name="w1_codes%d%d%d" % (a, b, first), align_bytes=64)
+            name = "w1_plane%d%d%d" % (a, b, first)
+            if at is None:
+                plane = keep.tile([P, count * P], U8, name=name, align_bytes=64)
+            else:
+                plane = shared.tile([P, count * P], U8, name=name, align_bytes=64, offset=at)
+            nc.vector.quantize_mx(out=codes[:].bitcast(FP8X4), scales=plane[:],
+                                  in_=piece.rearrange("p t m j -> p (t m j)"))
+            for t in range(count):
+                w1_mx[a, b, first + t] = codes[:, t * P:(t + 1) * P], plane[:, t * P:(t + 1) * P]
 
         w2_codes = keep.tile([P, 2 * H], U8, name="w2_codes", align_bytes=64)
         in_slice_order(w2_codes[:].bitcast(U16), w2_raw[:].bitcast(U16))
@@ -129,8 +136,8 @@ def tile_list_site_phasing_kernel(tc, tab_words, tab_scales, offs, pos1, pos2, p
         picked = {0: keep.tile([P, S], U32, name="picked_codes0", align_bytes=64)}
         nc.vector.tensor_copy(picked[0][:], table[0][:].indirect(offs_t[:]))
         picked_planes = shared.tile([P, S], U8, name="picked_planes", align_bytes=64, offset=AT_PICKED_PLANES)
-        nc.vector.tensor_copy(picked_planes[:], table_planes[:].indirect(offs_t[:]))
-        down = 4 * W2_PASS
+        nc.vector.tensor_copy(picked_planes[:], table_planes.indirect(offs_t[:]))
+        down = FIRST_PLANE + 4 * W2_PASS
         for q in range(QUADRANTS):
             nc.scalar.dma_start(picked_plane2[32 * q:32 * q + 4, :].bitcast(I32),
                                 picked_planes[32 * q + down:32 * q + down + 4, :].bitcast(I32))
@@ -140,9 +147,9 @@ def tile_list_site_phasing_kernel(tc, tab_words, tab_scales, offs, pos1, pos2, p
         last_raw = [load_w1(early[:, h * 2 * KP:(h + 1) * 2 * KP], 1, h * KP // 2, (h + 1) * KP // 2) for h in range(2)]
         bias_t = shared.tile([P, 2, PACK], F32, name="bias_t", align_bytes=64, offset=AT_BIAS)
         nc.sync.dma_start(bias_t[:], bias.rearrange("(a p t) -> p a t", p=P, t=PACK))
-        rounded = new_rounded()
-        round_w1(nc.scalar.copy, rounded, w1_raw[0, 0], 0, P)
-        quantize_w1(rounded, 0, 0)
+        rounded = shared.tile([P, PACK, P, PACK], BF16, name="w1_rounded00", align_bytes=64, offset=AT_ROUNDED)
+        round_w1(nc.vector.tensor_copy, rounded, w1_raw[0, 0], 0, P)
+        quantize_w1(0, 0, rounded[:, 0:2])
 
         def per_row(name):
             return keep.tile([P, 2, PACK], F32, name=name)
@@ -170,7 +177,7 @@ def tile_list_site_phasing_kernel(tc, tab_words, tab_scales, offs, pos1, pos2, p
         def open_sums(a, t, u):
             sums[a, t, u] = psum.tile([P, BANK], F32, name="bank%d" % (2 * t + u))
 
-        def pass_order(a, t):
+        def pass_order(a, t, u):
             if a == 1:
                 return W2_PASS, 0, 1
             return (0, W2_PASS, 1) if t < 2 else (0, 1, W2_PASS)
@@ -179,20 +186,20 @@ def tile_list_site_phasing_kernel(tc, tab_words, tab_scales, offs, pos1, pos2, p
             cols = slice(u * BANK, (u + 1) * BANK)
             if b == W2_PASS:
                 c0 = a * KP + t * P
-                lhs, lhs_plane = w2_codes[:, 2 * c0:2 * (c0 + P)].bitcast(FP4X4), w2_plane[:, c0:c0 + P]
+                lhs, lhs_plane = w2_codes[:, 2 * c0:2 * (c0 + P)].bitcast(FP4X4), w2_plane[a][:, t * P:(t + 1) * P]
                 rhs_plane = picked_plane2[:, cols]
             else:
-                w_codes, w_plane = w1_mx[a, b]
-                lhs, lhs_plane = w_codes[:, t * P:(t + 1) * P].bitcast(FP8X4), w_plane[:, t * P:(t + 1) * P]
-                rhs_plane = picked_planes[4 * b:P, cols]
+                w_codes, lhs_plane = w1_mx[a, b, t]
+                lhs = w_codes.bitcast(FP8X4)
+                rhs_plane = picked_planes[FIRST_PLANE + 4 * b:P, cols]
             nc.tensor.matmul_mx(out=sums[a, t, u][:], lhsT=lhs, lhsT_scale=lhs_plane,
                                 rhs=picked[b][:, cols].bitcast(FP8X4), rhs_scale=rhs_plane,
-                                start=b == pass_order(a, t)[0], stop=b == pass_order(a, t)[-1])
+                                start=b == pass_order(a, t, u)[0], stop=b == pass_order(a, t, u)[-1])
 
         for t in range(PACK):
             for u in range(2):
                 open_sums(0, t, u)
-        for t in range(PACK):
+        for t in range(2):
             for u in range(2):
                 first_stage_pass(0, t, u, 0)
 
@@ -203,8 +210,17 @@ def tile_list_site_phasing_kernel(tc, tab_words, tab_scales, offs, pos1, pos2, p
         picked[1] = keep.tile([P, S], U32, name="picked_codes1", align_bytes=64)
         picked[W2_PASS] = keep.tile([P, S], U32, name="picked_codes2", align_bytes=64)
         nc.vector.tensor_copy(picked[1][:], table[1][:].indirect(offs_t[:]))
-        w2_plane = shared.tile([P, H], U8, name="w2_plane", align_bytes=64, offset=AT_W2_PLANE)
-        in_slice_order(w2_plane[:], w2_plane_raw[:])
+        w2_plane = {}
+
+        def order_w2_plane(a):
+            w2_plane[a] = shared.tile([P, KP], U8, name="w2_plane%d" % a, align_bytes=64, offset=AT_W2_PLANE[a])
+            in_slice_order(w2_plane[a][:], w2_plane_raw[:, a * KP:(a + 1) * KP])
+
+        order_w2_plane(0)
+        quantize_w1(0, 0, rounded[:, 2:PACK], 2, AT_W1_PLANE)
+        for t in range(2, PACK):
+            for u in range(2):
+                first_stage_pass(0, t, u, 0)
         late = shared.tile([P, PACK * KP], F32, name="w1_late0", align_bytes=64, offset=AT_W1_LATE[0])
         late_raw = [load_w1(late[:, h * 2 * KP:(h + 1) * 2 * KP], 0, KP + h * KP // 2, KP + (h + 1) * KP // 2)
                     for h in range(2)]
@@ -219,12 +235,14 @@ def tile_list_site_phasing_kernel(tc, tab_words, tab_scales, offs, pos1, pos2, p
             gather_half(W2_PASS, u)
             for t in range(2):
                 first_stage_pass(0, t, u, W2_PASS)
-        rounded = new_rounded()
-        round_w1(nc.scalar.copy, rounded, last_raw[0], 0, P // 2)
-        round_w1(nc.vector.tensor_copy, rounded, last_raw[1], P // 2, P, P // 2, slice(0, 2))
-        round_w1(nc.scalar.copy, rounded, last_raw[1], P // 2, P, P // 2, slice(2, PACK))
+        pairs = [keep.tile([P, 2, P, PACK], BF16, name="w1_rounded_pair%d" % i, align_bytes=64) for i in range(2)]
+        round_w1(nc.scalar.copy, pairs[0], last_raw[0], 0, P // 2, 0, slice(0, 2))
+        round_w1(nc.scalar.copy, pairs[1], last_raw[0], 0, P // 2, 0, slice(2, PACK))
+        round_w1(nc.vector.tensor_copy, pairs[0], last_raw[1], P // 2, P, P // 2, slice(0, 2))
+        round_w1(nc.scalar.copy, pairs[1], last_raw[1], P // 2, P, P // 2, slice(2, PACK))
         nc.vector.tensor_tensor(signed_bias[:], bias_t[:], sign[:], ALU.mult)
-        quantize_w1(rounded, 0, 1, 2)
+        quantize_w1(0, 1, pairs[0][:])
+        quantize_w1(0, 1, pairs[1][:], 2)
         for t in range(PACK):
             for u in range(2):
                 first_stage_pass(0, t, u, 1)
@@ -246,7 +264,7 @@ def tile_list_site_phasing_kernel(tc, tab_words, tab_scales, offs, pos1, pos2, p
         def multiply(a, t):
             for u in range(2):
                 open_sums(a, t, u)
-            for b in pass_order(a, t):
+            for b in pass_order(a, t, 0):
                 for u in range(2):
                     first_stage_pass(a, t, u, b)
 
@@ -359,6 +377,7 @@ def tile_list_site_phasing_kernel(tc, tab_words, tab_scales, offs, pos1, pos2, p
 
         rounded = shared.tile([P, PACK, P, PACK], BF16, name="w1_rounded10", align_bytes=64, offset=AT_W1_EARLY[1])
         round_w1(nc.vector.tensor_copy, rounded, late_raw[0], 0, P // 2)
+        order_w2_plane(1)
         leave(0, 0, 0)
         leave(0, 0, 1)
         leave(0, 1, 0, True)
@@ -379,7 +398,7 @@ def tile_list_site_phasing_kernel(tc, tab_words, tab_scales, offs, pos1, pos2, p
             second_term[a] = new_term("second_term%d" % a, AT_W1_LATE[0])
             pick_upper(a, 0, 0, M)
             if a == 0:
-                quantize_w1(rounded, 1, 0)
+                quantize_w1(1, 0, rounded[:])
                 rounded = new_rounded()
                 round_w1(nc.vector.tensor_copy, rounded, w1_raw[1, 1], 0, P)
             else:
@@ -387,7 +406,7 @@ def tile_list_site_phasing_kernel(tc, tab_words, tab_scales, offs, pos1, pos2, p
             first_term[a] = new_term("first_term%d" % a, AT_W1_LATE[1])
             pick_hearth(a, 0, 0, M)
             if a == 0:
-                quantize_w1(rounded, 1, 1)
+                quantize_w1(1, 1, rounded[:])
             square_lower(a, 2, 0, M)
             leave(a, 3, 0)
             leave(a, 3, 1)

@@ -340,9 +340,9 @@ def tile_list_site_phasing_kernel(tc, tab_words, tab_scales, offs, pos1, pos2, p
         results = {}
 
         def weave(a, c0, c1):
-            nc.vector.tensor_tensor(woven[a][:, c0:c1, :].rearrange("p (c i) t -> p c t i", i=2),
-                                    first_term[a][:, :, c0:c1].rearrange("p t (c i) -> p c t i", i=2),
-                                    second_term[a][:, :, c0:c1].rearrange("p t (c i) -> p c t i", i=2), ALU.add)
+            nc.vector.tensor_tensor(woven[a][:, c0:c1, :].rearrange("p (c i) t -> p c t i", i=4),
+                                    first_term[a][:, :, c0:c1].rearrange("p t (c i) -> p c t i", i=4),
+                                    second_term[a][:, :, c0:c1].rearrange("p t (c i) -> p c t i", i=4), ALU.add)
 
         def quantize_z(a, c0, c1):
             nc.vector.quantize_mx(out=z_codes[a][:, c0:c1].bitcast(FP8X4), scales=z_plane[a][:, c0:c1],

@@ -32,6 +32,7 @@ AT_TABLE = (0, 39 * KB, 2 * KB)
 AT_PICKED_PLANES = 0
 AT_TABLE_PLANES = 16 * KB
 FIRST_PLANE = 4
+FIRST_COLUMNS = 1280
 PLANES_TILE = 6 * KB + 256
 AT_BIAS, AT_GAIN = 18 * KB, 38 * KB + 576
 AT_ROUNDED = 18 * KB + 64
@@ -86,9 +87,9 @@ def tile_list_site_phasing_kernel(tc, tab_words, tab_scales, offs, pos1, pos2, p
         offs_t = load_list(offs, "offs_t")
         w2_raw = shared.tile([P, 2 * H], U8, name="w2_raw", align_bytes=64, offset=AT_W2_RAW)
         table = {0: new_table(0)}
-        load_table(table[0], 0, slice(0, T // 2))
+        load_table(table[0], 0, slice(0, FIRST_COLUMNS))
         nc.sync.dma_start(w2_raw[:].bitcast(I32), w2_words[0].bitcast(I32))
-        load_table(table[0], 0, slice(T // 2, T))
+        load_table(table[0], 0, slice(FIRST_COLUMNS, T))
         p1 = load_list(pos1, "p1")
         p2 = load_list(pos2, "p2")
         p3 = load_list(pos3, "p3")
@@ -369,8 +370,9 @@ def tile_list_site_phasing_kernel(tc, tab_words, tab_scales, offs, pos1, pos2, p
             rows = out[:, c0:c1].rearrange("(n p) m -> p n m", p=P)
             blocks = max(share, 2)
             for n0 in range(0, N // P, blocks):
-                copy = nc.vector.tensor_copy if n0 + blocks < N // P else nc.scalar.copy
                 for n in range(n0, n0 + blocks, share):
+                    on_vector = n % 2 == 0 if share == 1 else n0 + blocks < N // P
+                    copy = nc.vector.tensor_copy if on_vector else nc.scalar.copy
                     copy(staged[:, n:n + share, :], results[i, n // share][:])
                 queue = nc.scalar if i + 1 == len(PIECES) and n0 else nc.sync
                 queue.dma_start(rows[:, n0:n0 + blocks, :], staged[:, n0:n0 + blocks, :])
@@ -423,11 +425,11 @@ def tile_list_site_phasing_kernel(tc, tab_words, tab_scales, offs, pos1, pos2, p
             pick_upper(a, 2, 0, M)
             for i, (c0, c1) in enumerate(PIECES if a == 1 else [(0, M)]):
                 pick_lower(a, 3, c0, c1)
-                pick_hearth(a, 3, c0, c1)
-                square_lower(a, 3, c0, c1)
                 pick_upper(a, 3, c0, c1)
-                half_product(a, 3, c0, c1)
+                square_lower(a, 3, c0, c1)
+                pick_hearth(a, 3, c0, c1)
                 scale_upper(a, 3, c0, c1)
+                half_product(a, 3, c0, c1)
                 if a == 1:
                     if i:
                         quantize_z(1, *PIECES[i - 1])

@@ -66,10 +66,10 @@ def tile_list_site_phasing_kernel(tc, tab_words, tab_scales, offs, pos1, pos2, p
             words = tab_words[a].rearrange("p t i -> p (t i)").bitcast(I32)
             nc.sync.dma_start(tile[:].bitcast(I32)[:, cols], words[:, cols])
 
-        def load_w1(dst, b, c0, c1):
+        def load_w1(dst, b, c0, c1, queue=nc.sync):
             rows = w1[b * KP:(b + 1) * KP, c0:c1]
             raw = dst.rearrange("p (j c) -> p j c", j=PACK)
-            nc.sync.dma_start(raw, rows.rearrange("(p j) c -> p j c", j=PACK))
+            queue.dma_start(raw, rows.rearrange("(p j) c -> p j c", j=PACK))
             return raw
 
         def load_planes(queues, planes, scales, first=0):
@@ -129,7 +129,7 @@ def tile_list_site_phasing_kernel(tc, tab_words, tab_scales, offs, pos1, pos2, p
         w2_codes = keep.tile([P, 2 * H], U8, name="w2_codes", align_bytes=64)
         in_slice_order(w2_codes[:].bitcast(U16), w2_raw[:].bitcast(U16))
         early = shared.tile([P, PACK * KP], F32, name="w1_early0", align_bytes=64, offset=AT_W1_EARLY[0])
-        w1_raw = {(0, 0): load_w1(early[:], 0, 0, KP)}
+        w1_raw = {(0, 0): load_w1(early[:], 0, 0, KP, nc.scalar)}
         gain_t = shared.tile([P, 2, PACK], F32, name="gain_t", align_bytes=64, offset=AT_GAIN)
         nc.sync.dma_start(gain_t[:], gain.rearrange("(a p t) -> p a t", p=P, t=PACK))
         table[1] = new_table(1)

@@ -43,6 +43,7 @@ AT_W3_PLANES = 47 * KB
 AT_W2_PLANE = (47 * KB + 512, 2 * KB)
 AT_W1_PLANE = 48 * KB
 AT_W3_CODES = 48 * KB + 512
+AT_SPREAD = 62 * KB
 
 
 def tile_list_site_phasing_kernel(tc, tab_words, tab_scales, offs, pos1, pos2, pos3, w1, w2_words,
@@ -96,10 +97,6 @@ def tile_list_site_phasing_kernel(tc, tab_words, tab_scales, offs, pos1, pos2, p
         load_planes((nc.gpsimd, nc.gpsimd, nc.scalar, nc.scalar), table_planes, tab_scales, FIRST_PLANE)
         load_planes([nc.gpsimd] * QUADRANTS, w2_plane_raw, w2_scales)
 
-        warm = keep.tile([P, 2], F32, name="warm")
-        nc.vector.memset(warm[:], 0.0)
-        nc.scalar.activation(warm[:, 1:2], warm[:, 0:1], ACT.Sigmoid)
-
         def in_slice_order(dst, src):
             nc.vector.tensor_copy(dst.rearrange("p (a t m) -> p a t m", m=P, t=PACK),
                                   src.rearrange("p (a m t) -> p a t m", m=P, t=PACK))
@@ -107,9 +104,6 @@ def tile_list_site_phasing_kernel(tc, tab_words, tab_scales, offs, pos1, pos2, p
         def round_w1(copy, rounded, raw, m0, m1, first=0, slices=slice(0, PACK)):
             src = raw[:, :, PACK * (m0 - first):PACK * (m1 - first)].rearrange("p j (m t) -> p m j t", t=PACK)
             copy(rounded[:].rearrange("p t m j -> p m j t")[:, m0:m1, :, :], src[:, :, :, slices])
-
-        def new_rounded():
-            return work.tile([P, PACK, P, PACK], BF16, name="w1_rounded", align_bytes=64, bufs=2)
 
         w1_mx = {}
 
@@ -156,21 +150,17 @@ def tile_list_site_phasing_kernel(tc, tab_words, tab_scales, offs, pos1, pos2, p
             return keep.tile([P, 2, PACK], F32, name=name)
 
         sign, signed_bias, factor, half = per_row("sign"), per_row("signed_bias"), per_row("factor"), per_row("half")
-        root, root2, minus_root = per_row("root"), per_row("root2"), per_row("minus_root")
+        root = per_row("root")
         nc.gpsimd.memset(half[:], 0.5)
         nc.vector.tensor_scalar(sign[:], gain_t[:], 0.0, 2.0, ALU.is_ge, ALU.mult)
         nc.vector.tensor_scalar(sign[:], sign[:], -1.0, None, ALU.add)
         nc.vector.tensor_tensor(factor[:], gain_t[:], sign[:], ALU.mult)
-        nc.vector.tensor_scalar(factor[:, :, 1::2], factor[:, :, 1::2], 2.0, None, ALU.mult)
         nc.gpsimd.tensor_tensor(root[:], factor[:], half[:], ALU.pow)
-        nc.gpsimd.tensor_scalar(root2[:], root[:], 2.0, 0.0, ALU.mult, ALU.add)
-        nc.gpsimd.tensor_scalar(minus_root[:], root[:], -1.0, 0.0, ALU.mult, ALU.add)
-        minus_half_factor = per_row("minus_half_factor")
-        nc.gpsimd.tensor_scalar(minus_half_factor[:], factor[:], -0.5, 0.0, ALU.mult, ALU.add)
         spread = {}
         for a in range(2):
-            for t in range(0, PACK, 2):
-                spread[a, t] = keep.tile([P, M], F32, name="spread%d%d" % (a, t))
+            for t in range(PACK if a == 0 else 2):
+                spread[a, t] = shared.tile([P, M], F32, name="spread%d%d" % (a, t), align_bytes=64,
+                                           offset=AT_SPREAD + 2 * KB * (PACK * a + t))
                 nc.scalar.copy(spread[a, t][:], factor[:, a, t:t + 1].to_broadcast([P, M]))
 
         sums = {}
@@ -250,11 +240,11 @@ def tile_list_site_phasing_kernel(tc, tab_words, tab_scales, offs, pos1, pos2, p
                 if t >= 2:
                     first_stage_pass(0, t, u, W2_PASS)
 
-        window, lower, square, hearth, upper = {}, {}, {}, {}, {}
+        window, lower, square, upper = {}, {}, {}, {}
         first_term, second_term = {}, {}
 
-        def new_term(name, at):
-            return shared.tile([P, PACK, M], F32, name=name, align_bytes=64, offset=at)
+        def new_term(name):
+            return keep.tile([P, PACK, M], F32, name=name, align_bytes=64)
 
         def entries(c0, c1):
             return slice(c0 // LANES, c1 // LANES)
@@ -269,71 +259,36 @@ def tile_list_site_phasing_kernel(tc, tab_words, tab_scales, offs, pos1, pos2, p
                 for u in range(2):
                     first_stage_pass(a, t, u, b)
 
-        def leave(a, t, u, on_vector=False):
-            if u == 0:
-                window[a, t] = work.tile([P, S], F32, name="window%d" % t, bufs=2)
-            dst = window[a, t][:, u * BANK:(u + 1) * BANK]
-            if on_vector:
-                nc.vector.tensor_scalar(dst, sums[a, t, u][:], sign[:, a, t:t + 1], signed_bias[:, a, t:t + 1],
-                                        ALU.mult, ALU.add)
-            else:
-                nc.scalar.activation(dst, sums[a, t, u][:], ACT.Identity if t % 2 else ACT.Tanh,
+        def leave(a, t):
+            window[a, t] = work.tile([P, S], F32, name="window%d" % t, bufs=2)
+            for u in range(2):
+                nc.scalar.activation(window[a, t][:, u * BANK:(u + 1) * BANK], sums[a, t, u][:], ACT.Tanh,
                                      scale=sign[:, a, t:t + 1], bias=signed_bias[:, a, t:t + 1])
-
-        def sigmoid(dst, a, t, places):
-            nc.scalar.activation(dst, window[a, t][:].indirect(places), ACT.Sigmoid, scale=2.0)
 
         def pick_lower(a, t, c0, c1):
             if c0 == 0:
-                lower[a, t] = temp("lower", t)
-            if t % 2:
-                sigmoid(lower[a, t][:, c0:c1], a, t, p1[:, entries(c0, c1)])
-            else:
-                nc.vector.tensor_copy(lower[a, t][:, c0:c1], window[a, t][:].indirect(p1[:, entries(c0, c1)]))
+                lower[a, t] = work.tile([P, M], F32, name="lower%d" % t)
+                square[a, t] = temp("square", t)
+            nc.scalar.activation(lower[a, t][:, c0:c1], window[a, t][:].indirect(p1[:, entries(c0, c1)]), ACT.Copy)
 
         def square_lower(a, t, c0, c1):
-            if c0 == 0:
-                square[a, t] = temp("square", t)
-            if t % 2:
-                nc.scalar.activation(square[a, t][:, c0:c1], lower[a, t][:, c0:c1], ACT.Square,
-                                     scale=root2[:, a, t:t + 1], bias=minus_root[:, a, t:t + 1])
-            elif t == 2:
-                nc.vector.scalar_tensor_tensor(square[a, t][:, c0:c1], lower[a, t][:, c0:c1], factor[:, a, t:t + 1],
-                                               lower[a, t][:, c0:c1], ALU.mult, ALU.mult)
-            else:
-                nc.scalar.activation(square[a, t][:, c0:c1], lower[a, t][:, c0:c1], ACT.Square,
-                                     scale=root[:, a, t:t + 1])
+            nc.scalar.activation(square[a, t][:, c0:c1], lower[a, t][:, c0:c1], ACT.Square, scale=root[:, a, t:t + 1])
 
         def pick_hearth(a, t, c0, c1):
-            if t % 2:
-                if c0 == 0:
-                    hearth[a, t] = temp("hearth", t)
-                sigmoid(hearth[a, t][:, c0:c1], a, t, p2[:, entries(c0, c1)])
-            else:
-                nc.vector.tensor_tensor(first_term[a][:, t, c0:c1], window[a, t][:].indirect(p2[:, entries(c0, c1)]),
-                                        square[a, t][:, c0:c1], ALU.mult)
+            nc.vector.tensor_tensor(first_term[a][:, t, c0:c1], window[a, t][:].indirect(p2[:, entries(c0, c1)]),
+                                    square[a, t][:, c0:c1], ALU.mult)
 
-        def half_product(a, t, c0, c1):
-            nc.vector.scalar_tensor_tensor(first_term[a][:, t, c0:c1], hearth[a, t][:, c0:c1], 0.5,
-                                           square[a, t][:, c0:c1], ALU.subtract, ALU.mult)
+        def pick_upper(a, t):
+            nc.vector.tensor_tensor(second_term[a][:, t, :], window[a, t][:].indirect(p3[:]), spread[a, t][:], ALU.mult)
 
-        def pick_upper(a, t, c0, c1):
-            if t % 2:
-                if c0 == 0:
-                    upper[a, t] = temp("upper", t)
-                sigmoid(upper[a, t][:, c0:c1], a, t, p3[:, entries(c0, c1)])
-            else:
-                nc.vector.tensor_tensor(second_term[a][:, t, c0:c1],
-                                        window[a, t][:].indirect(p3[:, entries(c0, c1)]),
-                                        spread[a, t][:, c0:c1], ALU.mult)
+        def copy_upper(a, t, c0, c1):
+            if c0 == 0:
+                upper[a, t] = temp("upper", t)
+            nc.scalar.activation(upper[a, t][:, c0:c1], window[a, t][:].indirect(p3[:, entries(c0, c1)]), ACT.Copy)
 
         def scale_upper(a, t, c0, c1):
-            if (a, t) == (1, 3):
-                nc.scalar.activation(second_term[a][:, t, c0:c1], upper[a, t][:, c0:c1], ACT.Identity,
-                                     scale=factor[:, a, t:t + 1], bias=minus_half_factor[:, a, t:t + 1])
-                return
-            nc.vector.tensor_scalar(second_term[a][:, t, c0:c1], upper[a, t][:, c0:c1], 0.5, factor[:, a, t:t + 1],
-                                    ALU.subtract, ALU.mult)
+            nc.vector.tensor_scalar(second_term[a][:, t, c0:c1], upper[a, t][:, c0:c1], factor[:, a, t:t + 1], None,
+                                    ALU.mult)
 
         woven = [keep.tile([P, M, PACK], BF16, name="woven%d" % a, align_bytes=64) for a in range(2)]
         z_codes = [keep.tile([P, M], U32, name="z_codes%d" % a, align_bytes=64) for a in range(2)]
@@ -366,12 +321,15 @@ def tile_list_site_phasing_kernel(tc, tab_words, tab_scales, offs, pos1, pos2, p
         def store(i):
             c0, c1 = PIECES[i]
             share = BLOCKS_IN_BANK[i]
-            staged = keep.tile([P, N // P, c1 - c0], F32, name="staged%d" % i)
+            if i == 0:
+                staged = work.tile([P, N // P, c1 - c0], F32, name="lower%d" % (PACK - 1))
+            else:
+                staged = keep.tile([P, N // P, c1 - c0], F32, name="staged%d" % i)
             rows = out[:, c0:c1].rearrange("(n p) m -> p n m", p=P)
             blocks = max(share, 2)
             for n0 in range(0, N // P, blocks):
                 for n in range(n0, n0 + blocks, share):
-                    on_vector = n % 2 == 0 if share == 1 else n0 + blocks < N // P
+                    on_vector = share == 1 and n % 2 == 0
                     copy = nc.vector.tensor_copy if on_vector else nc.scalar.copy
                     copy(staged[:, n:n + share, :], results[i, n // share][:])
                 queue = nc.scalar if i + 1 == len(PIECES) and n0 else nc.sync
@@ -380,65 +338,48 @@ def tile_list_site_phasing_kernel(tc, tab_words, tab_scales, offs, pos1, pos2, p
         rounded = shared.tile([P, PACK, P, PACK], BF16, name="w1_rounded10", align_bytes=64, offset=AT_W1_EARLY[1])
         round_w1(nc.vector.tensor_copy, rounded, late_raw[0], 0, P // 2)
         order_w2_plane(1)
-        leave(0, 0, 0)
-        leave(0, 0, 1)
-        leave(0, 1, 0, True)
-        leave(0, 1, 1, True)
         for a in range(2):
-            leave(a, 2, 0)
-            leave(a, 2, 1)
-            pick_lower(a, 0, 0, M)
-            pick_lower(a, 1, 0, M)
-            pick_lower(a, 2, 0, M)
-            square_lower(a, 0, 0, M)
-            square_lower(a, 1, 0, M)
-            pick_hearth(a, 1, 0, M)
-            if a == 0:
-                round_w1(nc.vector.tensor_copy, rounded, late_raw[1], P // 2, P, P // 2)
-            else:
-                weave(0, 0, M)
-            second_term[a] = new_term("second_term%d" % a, AT_W1_LATE[0])
-            pick_upper(a, 0, 0, M)
-            if a == 0:
-                quantize_w1(1, 0, rounded[:])
-                rounded = new_rounded()
-                round_w1(nc.vector.tensor_copy, rounded, w1_raw[1, 1], 0, P)
-            else:
-                quantize_z(0, 0, M)
-            first_term[a] = new_term("first_term%d" % a, AT_W1_LATE[1])
-            pick_hearth(a, 0, 0, M)
-            if a == 0:
-                quantize_w1(1, 1, rounded[:])
-            square_lower(a, 2, 0, M)
-            leave(a, 3, 0)
-            leave(a, 3, 1)
-            pick_upper(a, 1, 0, M)
-            if a == 0:
-                for t in range(PACK):
-                    multiply(1, t)
-            else:
-                for i in range(len(PIECES)):
-                    second_stage_pass(0, i)
-            half_product(a, 1, 0, M)
-            scale_upper(a, 1, 0, M)
-            pick_hearth(a, 2, 0, M)
-            pick_upper(a, 2, 0, M)
-            for i, (c0, c1) in enumerate(PIECES if a == 1 else [(0, M)]):
-                pick_lower(a, 3, c0, c1)
-                pick_upper(a, 3, c0, c1)
-                square_lower(a, 3, c0, c1)
-                pick_hearth(a, 3, c0, c1)
-                scale_upper(a, 3, c0, c1)
-                half_product(a, 3, c0, c1)
-                if a == 1:
-                    if i:
-                        quantize_z(1, *PIECES[i - 1])
-                        second_stage_pass(1, i - 1)
-                    weave(1, c0, c1)
-            if a == 0:
-                for t in range(2):
-                    leave(1, t, 0)
-                    leave(1, t, 1)
+            first_term[a], second_term[a] = new_term("first_term%d" % a), new_term("second_term%d" % a)
+            for t in range(PACK):
+                leave(a, t)
+                if (a, t) == (1, PACK - 1):
+                    break
+                if (a, t) in spread:
+                    pick_upper(a, t)
+                pick_lower(a, t, 0, M)
+                if (a, t) not in spread:
+                    copy_upper(a, t, 0, M)
+                square_lower(a, t, 0, M)
+                if (a, t) == (0, 0):
+                    round_w1(nc.vector.tensor_copy, rounded, late_raw[1], P // 2, P, P // 2)
+                if (a, t) == (0, 1):
+                    rounded = shared.tile([P, PACK, P, PACK], BF16, name="w1_rounded11", align_bytes=64,
+                                          offset=AT_SPREAD)
+                    round_w1(nc.vector.tensor_copy, rounded, w1_raw[1, 1], 0, P)
+                if (a, t) == (1, 0):
+                    weave(0, 0, M)
+                pick_hearth(a, t, 0, M)
+                if a == 0 and t < 2:
+                    quantize_w1(1, t, rounded[:])
+                if (a, t) == (1, 0):
+                    quantize_z(0, 0, M)
+                if (a, t) not in spread:
+                    scale_upper(a, t, 0, M)
+                if a == 0 and t >= 1:
+                    for done in range(t + 1) if t == 1 else [t]:
+                        multiply(1, done)
+        for i in range(len(PIECES)):
+            second_stage_pass(0, i)
+        for i, (c0, c1) in enumerate(PIECES):
+            pick_lower(1, PACK - 1, c0, c1)
+            copy_upper(1, PACK - 1, c0, c1)
+            square_lower(1, PACK - 1, c0, c1)
+            scale_upper(1, PACK - 1, c0, c1)
+            pick_hearth(1, PACK - 1, c0, c1)
+            if i:
+                quantize_z(1, *PIECES[i - 1])
+                second_stage_pass(1, i - 1)
+            weave(1, c0, c1)
         quantize_z(1, *PIECES[-1])
         second_stage_pass(1, len(PIECES) - 1)
         for i in range(len(PIECES)):

@@ -33,10 +33,10 @@ AT_PICKED_PLANES = 0
 AT_TABLE_PLANES = 16 * KB
 FIRST_PLANE = 4
 FIRST_COLUMNS = 1280
-PLANES_TILE = 6 * KB + 256
+PLANES_TILE = 6 * KB + 512
 AT_BIAS, AT_GAIN = 18 * KB, 38 * KB + 576
-AT_ROUNDED = 18 * KB + 64
-AT_W1_EARLY = (30 * KB + 512, 22 * KB + 64)
+AT_ROUNDED = 18 * KB + 256
+AT_W1_EARLY = (30 * KB + 512, 22 * KB + 256)
 AT_W2_RAW = 38 * KB
 AT_W1_LATE = (39 * KB, 52 * KB + 512)
 AT_W3_PLANES = 47 * KB
@@ -61,7 +61,7 @@ def tile_list_site_phasing_kernel(tc, tab_words, tab_scales, offs, pos1, pos2, p
             return tile
 
         def new_table(a):
-            return shared.tile([P, T], U32, name="table%d" % a, align_bytes=64, offset=AT_TABLE[a])
+            return shared.tile([P, T], U32, name="table%d" % a, align_bytes=256, offset=AT_TABLE[a])
 
         def load_table(tile, a, cols):
             words = tab_words[a].rearrange("p t i -> p (t i)").bitcast(I32)
@@ -338,6 +338,7 @@ def tile_list_site_phasing_kernel(tc, tab_words, tab_scales, offs, pos1, pos2, p
         rounded = shared.tile([P, PACK, P, PACK], BF16, name="w1_rounded10", align_bytes=64, offset=AT_W1_EARLY[1])
         round_w1(nc.vector.tensor_copy, rounded, late_raw[0], 0, P // 2)
         order_w2_plane(1)
+        round_w1(nc.vector.tensor_copy, rounded, late_raw[1], P // 2, P, P // 2)
         for a in range(2):
             first_term[a], second_term[a] = new_term("first_term%d" % a), new_term("second_term%d" % a)
             for t in range(PACK):
@@ -350,8 +351,6 @@ def tile_list_site_phasing_kernel(tc, tab_words, tab_scales, offs, pos1, pos2, p
                 if (a, t) not in spread:
                     copy_upper(a, t, 0, M)
                 square_lower(a, t, 0, M)
-                if (a, t) == (0, 0):
-                    round_w1(nc.vector.tensor_copy, rounded, late_raw[1], P // 2, P, P // 2)
                 if (a, t) == (0, 1):
                     rounded = shared.tile([P, PACK, P, PACK], BF16, name="w1_rounded11", align_bytes=64,
                                           offset=AT_SPREAD)

@@ -267,8 +267,10 @@ def tile_list_site_phasing_kernel(tc, tab_words, tab_scales, offs, pos1, pos2, p
 
         def pick_lower(a, t, c0, c1):
             if c0 == 0:
-                lower[a, t] = work.tile([P, M], F32, name="lower%d" % t)
                 square[a, t] = temp("square", t)
+            if c0 == 0 or (c1 - c0 < M and c0 == M // 2):
+                name = "lower%d" % t if c0 or c1 == M else "upper2"
+                lower[a, t] = work.tile([P, M], F32, name=name, bufs=1, align_bytes=64)
             nc.scalar.activation(lower[a, t][:, c0:c1], window[a, t][:].indirect(p1[:, entries(c0, c1)]), ACT.Copy)
 
         def square_lower(a, t, c0, c1):
@@ -282,8 +284,9 @@ def tile_list_site_phasing_kernel(tc, tab_words, tab_scales, offs, pos1, pos2, p
             nc.vector.tensor_tensor(second_term[a][:, t, :], window[a, t][:].indirect(p3[:]), spread[a, t][:], ALU.mult)
 
         def copy_upper(a, t, c0, c1):
-            if c0 == 0:
-                upper[a, t] = temp("upper", t)
+            if c0 == 0 or t < PACK - 1:
+                name = "lower%d" % t if (t, c0) == (PACK - 2, 0) else "upper%d" % t
+                upper[a, t] = work.tile([P, M], F32, name=name, bufs=1, align_bytes=64)
             nc.scalar.activation(upper[a, t][:, c0:c1], window[a, t][:].indirect(p3[:, entries(c0, c1)]), ACT.Copy)
 
         def scale_upper(a, t, c0, c1):
@@ -322,7 +325,7 @@ def tile_list_site_phasing_kernel(tc, tab_words, tab_scales, offs, pos1, pos2, p
             c0, c1 = PIECES[i]
             share = BLOCKS_IN_BANK[i]
             if i == 0:
-                staged = work.tile([P, N // P, c1 - c0], F32, name="lower%d" % (PACK - 1))
+                staged = work.tile([P, N // P, c1 - c0], F32, name="lower%d" % (PACK - 1), bufs=1, align_bytes=64)
             else:
                 staged = keep.tile([P, N // P, c1 - c0], F32, name="staged%d" % i)
             rows = out[:, c0:c1].rearrange("(n p) m -> p n m", p=P)
@@ -348,8 +351,6 @@ def tile_list_site_phasing_kernel(tc, tab_words, tab_scales, offs, pos1, pos2, p
                 if (a, t) in spread:
                     pick_upper(a, t)
                 pick_lower(a, t, 0, M)
-                if (a, t) not in spread:
-                    copy_upper(a, t, 0, M)
                 square_lower(a, t, 0, M)
                 if (a, t) == (0, 1):
                     rounded = shared.tile([P, PACK, P, PACK], BF16, name="w1_rounded11", align_bytes=64,
@@ -362,8 +363,6 @@ def tile_list_site_phasing_kernel(tc, tab_words, tab_scales, offs, pos1, pos2, p
                     quantize_w1(1, t, rounded[:])
                 if (a, t) == (1, 0):
                     quantize_z(0, 0, M)
-                if (a, t) not in spread:
-                    scale_upper(a, t, 0, M)
                 if a == 0 and t >= 1:
                     for done in range(t + 1) if t == 1 else [t]:
                         multiply(1, done)
@@ -372,8 +371,12 @@ def tile_list_site_phasing_kernel(tc, tab_words, tab_scales, offs, pos1, pos2, p
         for i, (c0, c1) in enumerate(PIECES):
             pick_lower(1, PACK - 1, c0, c1)
             copy_upper(1, PACK - 1, c0, c1)
+            if c0 % (M // 2) == 0:
+                copy_upper(1, 2, c0, c0 + M // 2)
             square_lower(1, PACK - 1, c0, c1)
             scale_upper(1, PACK - 1, c0, c1)
+            if c0 % (M // 2) == 0:
+                scale_upper(1, 2, c0, c0 + M // 2)
             pick_hearth(1, PACK - 1, c0, c1)
             if i:
                 quantize_z(1, *PIECES[i - 1])

@@ -94,7 +94,7 @@ def tile_list_site_phasing_kernel(tc, tab_words, tab_scales, offs, pos1, pos2, p
         p1 = load_list(pos1, "p1")
         p2 = load_list(pos2, "p2")
         p3 = load_list(pos3, "p3")
-        load_planes((nc.gpsimd, nc.gpsimd, nc.scalar, nc.scalar), table_planes, tab_scales, FIRST_PLANE)
+        load_planes((nc.scalar, nc.scalar, nc.gpsimd, nc.gpsimd), table_planes, tab_scales, FIRST_PLANE)
         load_planes([nc.gpsimd] * QUADRANTS, w2_plane_raw, w2_scales)
 
         def in_slice_order(dst, src):

from contextlib import ExitStack

import concourse.mybir as mybir

K1, K2, H, N, T, S, M = 1024, 512, 1024, 512, 4096, 1024, 512
FLOPS = 2 * (K1 + K2) * H * S + 2 * H * N * M

F32 = mybir.dt.float32
BF16 = mybir.dt.bfloat16
I32 = mybir.dt.int32
U32 = mybir.dt.uint32
U16 = mybir.dt.uint16
U8 = mybir.dt.uint8
FP8X4 = mybir.dt.float8_e4m3fn_x4
FP4X4 = mybir.dt.float4_e2m1fn_x4
ACT = mybir.ActivationFunctionType
ALU = mybir.AluOpType

P = 128
PACK = 4
KP = P * PACK
BANK = 512
QUADRANTS = 4
LANES = 16
W2_PASS = 2
PIECES = ((0, 128), (128, 256), (256, 384), (384, 512))
BLOCKS_IN_BANK = (4, 4, 2, 1)


KB = 1024
AT_TABLE = (0, 39 * KB, 2 * KB)
AT_PICKED_PLANES = 0
AT_TABLE_PLANES = 16 * KB
FIRST_PLANE = 4
FIRST_COLUMNS = 1280
PLANES_TILE = 6 * KB + 512
AT_BIAS, AT_GAIN = 18 * KB, 38 * KB + 576
AT_ROUNDED = 18 * KB + 256
AT_W1_EARLY = (30 * KB + 512, 22 * KB + 256)
AT_W2_RAW = 38 * KB
AT_W1_LATE = (39 * KB, 52 * KB + 512)
AT_W3_PLANES = 47 * KB
AT_W2_PLANE = (47 * KB + 512, 2 * KB)
AT_W1_PLANE = 48 * KB
AT_W3_CODES = 48 * KB + 512
AT_SPREAD = 62 * KB


def tile_list_site_phasing_kernel(tc, tab_words, tab_scales, offs, pos1, pos2, pos3, w1, w2_words,
                                                w2_scales, bias, gain, w3_words, w3_scales, out):
    nc = tc.nc
    with ExitStack() as ctx:
        keep = ctx.enter_context(tc.tile_pool(name="keep", bufs=1))
        shared = ctx.enter_context(tc.tile_pool(name="shared", bufs=1))
        work = ctx.enter_context(tc.tile_pool(name="work", bufs=1))
        psum = ctx.enter_context(tc.psum_pool(name="psum", bufs=1))

        def load_list(src, name):
            tile = keep.tile(list(src.shape), U16, name=name)
            nc.sync.dma_start(tile[:], src)
            return tile

        def new_table(a):
            return shared.tile([P, T], U32, name="table%d" % a, align_bytes=256, offset=AT_TABLE[a])

        def load_table(tile, a, cols):
            words = tab_words[a].rearrange("p t i -> p (t i)").bitcast(I32)
            nc.sync.dma_start(tile[:].bitcast(I32)[:, cols], words[:, cols])

        def load_w1(dst, b, c0, c1, queue=nc.sync):
            rows = w1[b * KP:(b + 1) * KP, c0:c1]
            raw = dst.rearrange("p (j c) -> p j c", j=PACK)
            queue.dma_start(raw, rows.rearrange("(p j) c -> p j c", j=PACK))
            return raw

        def load_planes(queues, planes, scales, first=0):
            rows = 4 * scales.shape[0]
            for q, queue in enumerate(queues):
                queue.dma_start(planes[32 * q + first:32 * q + first + rows, :].bitcast(I32),
                                scales[:, 4 * q:4 * q + 4, :].bitcast(I32))

        table_planes = shared.tile([P, PLANES_TILE], U8, name="table_planes", align_bytes=64,
                                   offset=AT_TABLE_PLANES)[:, 0:T]
        w2_plane_raw = keep.tile([P, H], U8, name="w2_plane_raw", align_bytes=64)
        picked_plane2 = keep.tile([P, S], U8, name="picked_plane2", align_bytes=64)
        for plane in (table_planes, w2_plane_raw[:], picked_plane2[:]):
            nc.vector.memset(plane.bitcast(I32), 0)
        offs_t = load_list(offs, "offs_t")
        w2_raw = shared.tile([P, 2 * H], U8, name="w2_raw", align_bytes=64, offset=AT_W2_RAW)
        table = {0: new_table(0)}
        load_table(table[0], 0, slice(0, FIRST_COLUMNS))
        nc.sync.dma_start(w2_raw[:].bitcast(I32), w2_words[0].bitcast(I32))
        load_table(table[0], 0, slice(FIRST_COLUMNS, T))
        p1 = load_list(pos1, "p1")
        p2 = load_list(pos2, "p2")
        p3 = load_list(pos3, "p3")
        load_planes((nc.scalar, nc.scalar, nc.gpsimd, nc.gpsimd), table_planes, tab_scales, FIRST_PLANE)
        load_planes([nc.gpsimd] * QUADRANTS, w2_plane_raw, w2_scales)

        def in_slice_order(dst, src):
            nc.vector.tensor_copy(dst.rearrange("p (a t m) -> p a t m", m=P, t=PACK),
                                  src.rearrange("p (a m t) -> p a t m", m=P, t=PACK))

        def round_w1(copy, rounded, raw, m0, m1, first=0, slices=slice(0, PACK)):
            src = raw[:, :, PACK * (m0 - first):PACK * (m1 - first)].rearrange("p j (m t) -> p m j t", t=PACK)
            copy(rounded[:].rearrange("p t m j -> p m j t")[:, m0:m1, :, :], src[:, :, :, slices])

        w1_mx = {}

        def quantize_w1(a, b, piece, first=0, at=None):
            count = piece.shape[1]
            codes = keep.tile([P, count * P], U32, name="w1_codes%d%d%d" % (a, b, first), align_bytes=64)
            name = "w1_plane%d%d%d" % (a, b, first)
            if at is None:
                plane = keep.tile([P, count * P], U8, name=name, align_bytes=64)
            else:
                plane = shared.tile([P, count * P], U8, name=name, align_bytes=64, offset=at)
            nc.vector.quantize_mx(out=codes[:].bitcast(FP8X4), scales=plane[:],
                                  in_=piece.rearrange("p t m j -> p (t m j)"))
            for t in range(count):
                w1_mx[a, b, first + t] = codes[:, t * P:(t + 1) * P], plane[:, t * P:(t + 1) * P]

        w2_codes = keep.tile([P, 2 * H], U8, name="w2_codes", align_bytes=64)
        in_slice_order(w2_codes[:].bitcast(U16), w2_raw[:].bitcast(U16))
        early = shared.tile([P, PACK * KP], F32, name="w1_early0", align_bytes=64, offset=AT_W1_EARLY[0])
        w1_raw = {(0, 0): load_w1(early[:], 0, 0, KP, nc.scalar)}
        gain_t = shared.tile([P, 2, PACK], F32, name="gain_t", align_bytes=64, offset=AT_GAIN)
        nc.sync.dma_start(gain_t[:], gain.rearrange("(a p t) -> p a t", p=P, t=PACK))
        table[1] = new_table(1)
        load_table(table[1], 1, slice(0, T))
        picked = {0: keep.tile([P, S], U32, name="picked_codes0", align_bytes=64)}
        nc.vector.tensor_copy(picked[0][:], table[0][:].indirect(offs_t[:]))
        picked_planes = shared.tile([P, S], U8, name="picked_planes", align_bytes=64, offset=AT_PICKED_PLANES)
        nc.vector.tensor_copy(picked_planes[:], table_planes.indirect(offs_t[:]))
        down = FIRST_PLANE + 4 * W2_PASS
        for q in range(QUADRANTS):
            nc.scalar.dma_start(picked_plane2[32 * q:32 * q + 4, :].bitcast(I32),
                                picked_planes[32 * q + down:32 * q + down + 4, :].bitcast(I32))
        table[W2_PASS] = new_table(W2_PASS)
        load_table(table[W2_PASS], W2_PASS, slice(0, T))
        early = shared.tile([P, PACK * KP], F32, name="w1_early1", align_bytes=64, offset=AT_W1_EARLY[1])
        last_raw = [load_w1(early[:, h * 2 * KP:(h + 1) * 2 * KP], 1, h * KP // 2, (h + 1) * KP // 2) for h in range(2)]
        bias_t = shared.tile([P, 2, PACK], F32, name="bias_t", align_bytes=64, offset=AT_BIAS)
        nc.sync.dma_start(bias_t[:], bias.rearrange("(a p t) -> p a t", p=P, t=PACK))
        rounded = shared.tile([P, PACK, P, PACK], BF16, name="w1_rounded00", align_bytes=64, offset=AT_ROUNDED)
        round_w1(nc.vector.tensor_copy, rounded, w1_raw[0, 0], 0, P)
        quantize_w1(0, 0, rounded[:, 0:2])

        def per_row(name):
            return keep.tile([P, 2, PACK], F32, name=name)

        sign, signed_bias, factor, half = per_row("sign"), per_row("signed_bias"), per_row("factor"), per_row("half")
        root = per_row("root")
        nc.gpsimd.memset(half[:], 0.5)
        nc.vector.tensor_scalar(sign[:], gain_t[:], 0.0, 2.0, ALU.is_ge, ALU.mult)
        nc.vector.tensor_scalar(sign[:], sign[:], -1.0, None, ALU.add)
        nc.vector.tensor_tensor(factor[:], gain_t[:], sign[:], ALU.mult)
        nc.gpsimd.tensor_tensor(root[:], factor[:], half[:], ALU.pow)
        spread = {}
        for a in range(2):
            for t in range(PACK if a == 0 else 2):
                spread[a, t] = shared.tile([P, M], F32, name="spread%d%d" % (a, t), align_bytes=64,
                                           offset=AT_SPREAD + 2 * KB * (PACK * a + t))
                nc.scalar.copy(spread[a, t][:], factor[:, a, t:t + 1].to_broadcast([P, M]))

        sums = {}

        def open_sums(a, t, u):
            sums[a, t, u] = psum.tile([P, BANK], F32, name="bank%d" % (2 * t + u))

        def pass_order(a, t, u):
            if a == 1:
                return W2_PASS, 0, 1
            return (0, W2_PASS, 1) if t < 2 else (0, 1, W2_PASS)

        def first_stage_pass(a, t, u, b):
            cols = slice(u * BANK, (u + 1) * BANK)
            if b == W2_PASS:
                c0 = a * KP + t * P
                lhs, lhs_plane = w2_codes[:, 2 * c0:2 * (c0 + P)].bitcast(FP4X4), w2_plane[a][:, t * P:(t + 1) * P]
                rhs_plane = picked_plane2[:, cols]
            else:
                w_codes, lhs_plane = w1_mx[a, b, t]
                lhs = w_codes.bitcast(FP8X4)
                rhs_plane = picked_planes[FIRST_PLANE + 4 * b:P, cols]
            nc.tensor.matmul_mx(out=sums[a, t, u][:], lhsT=lhs, lhsT_scale=lhs_plane,
                                rhs=picked[b][:, cols].bitcast(FP8X4), rhs_scale=rhs_plane,
                                start=b == pass_order(a, t, u)[0], stop=b == pass_order(a, t, u)[-1])

        for t in range(PACK):
            for u in range(2):
                open_sums(0, t, u)
        for t in range(2):
            for u in range(2):
                first_stage_pass(0, t, u, 0)

        def gather_half(b, u):
            nc.vector.tensor_copy(picked[b][:, u * BANK:(u + 1) * BANK],
                                  table[b][:].indirect(offs_t[:, u * BANK // LANES:(u + 1) * BANK // LANES]))

        picked[1] = keep.tile([P, S], U32, name="picked_codes1", align_bytes=64)
        picked[W2_PASS] = keep.tile([P, S], U32, name="picked_codes2", align_bytes=64)
        nc.vector.tensor_copy(picked[1][:], table[1][:].indirect(offs_t[:]))
        w2_plane = {}

        def order_w2_plane(a):
            w2_plane[a] = shared.tile([P, KP], U8, name="w2_plane%d" % a, align_bytes=64, offset=AT_W2_PLANE[a])
            in_slice_order(w2_plane[a][:], w2_plane_raw[:, a * KP:(a + 1) * KP])

        order_w2_plane(0)
        quantize_w1(0, 0, rounded[:, 2:PACK], 2, AT_W1_PLANE)
        for t in range(2, PACK):
            for u in range(2):
                first_stage_pass(0, t, u, 0)
        late = shared.tile([P, PACK * KP], F32, name="w1_late0", align_bytes=64, offset=AT_W1_LATE[0])
        late_raw = [load_w1(late[:, h * 2 * KP:(h + 1) * 2 * KP], 0, KP + h * KP // 2, KP + (h + 1) * KP // 2)
                    for h in range(2)]
        late = shared.tile([P, PACK * KP], F32, name="w1_late1", align_bytes=64, offset=AT_W1_LATE[1])
        w1_raw[1, 1] = load_w1(late[:], 1, KP, 2 * KP)
        w3_codes = shared.tile([P, 2, N], U32, name="w3_codes", align_bytes=64, offset=AT_W3_CODES)
        nc.sync.dma_start(w3_codes[:].bitcast(I32), w3_words.rearrange("a p c i -> p a (c i)").bitcast(I32))
        w3_planes = shared.tile([P, N], U8, name="w3_planes", align_bytes=64, offset=AT_W3_PLANES)
        nc.vector.memset(w3_planes[:].bitcast(I32), 0)
        load_planes([nc.sync] * QUADRANTS, w3_planes, w3_scales)
        for u in range(2):
            gather_half(W2_PASS, u)
            for t in range(2):
                first_stage_pass(0, t, u, W2_PASS)
        pairs = [keep.tile([P, 2, P, PACK], BF16, name="w1_rounded_pair%d" % i, align_bytes=64) for i in range(2)]
        round_w1(nc.scalar.copy, pairs[0], last_raw[0], 0, P // 2, 0, slice(0, 2))
        round_w1(nc.scalar.copy, pairs[1], last_raw[0], 0, P // 2, 0, slice(2, PACK))
        round_w1(nc.vector.tensor_copy, pairs[0], last_raw[1], P // 2, P, P // 2, slice(0, 2))
        round_w1(nc.scalar.copy, pairs[1], last_raw[1], P // 2, P, P // 2, slice(2, PACK))
        nc.vector.tensor_tensor(signed_bias[:], bias_t[:], sign[:], ALU.mult)
        quantize_w1(0, 1, pairs[0][:])
        quantize_w1(0, 1, pairs[1][:], 2)
        for t in range(PACK):
            for u in range(2):
                first_stage_pass(0, t, u, 1)
                if t >= 2:
                    first_stage_pass(0, t, u, W2_PASS)

        window, lower, square, upper = {}, {}, {}, {}
        first_term, second_term = {}, {}

        def new_term(name):
            return keep.tile([P, PACK, M], F32, name=name, align_bytes=64)

        def entries(c0, c1):
            return slice(c0 // LANES, c1 // LANES)

        def temp(name, t):
            return work.tile([P, M], F32, name="%s%d" % (name, t), bufs=2)

        def multiply(a, t):
            for u in range(2):
                open_sums(a, t, u)
            for b in pass_order(a, t, 0):
                for u in range(2):
                    first_stage_pass(a, t, u, b)

        def leave(a, t):
            window[a, t] = work.tile([P, S], F32, name="window%d" % t, bufs=2)
            for u in range(2):
                nc.scalar.activation(window[a, t][:, u * BANK:(u + 1) * BANK], sums[a, t, u][:], ACT.Tanh,
                                     scale=sign[:, a, t:t + 1], bias=signed_bias[:, a, t:t + 1])

        def pick_lower(a, t, c0, c1):
            if c0 == 0:
                square[a, t] = temp("square", t)
            if c0 == 0 or (c1 - c0 < M and c0 == M // 2):
                name = "lower%d" % t if c0 or c1 == M else "upper2"
                lower[a, t] = work.tile([P, M], F32, name=name, bufs=1, align_bytes=64)
            nc.scalar.activation(lower[a, t][:, c0:c1], window[a, t][:].indirect(p1[:, entries(c0, c1)]), ACT.Copy)

        def square_lower(a, t, c0, c1):
            nc.scalar.activation(square[a, t][:, c0:c1], lower[a, t][:, c0:c1], ACT.Square, scale=root[:, a, t:t + 1])

        def pick_hearth(a, t, c0, c1):
            nc.vector.tensor_tensor(first_term[a][:, t, c0:c1], window[a, t][:].indirect(p2[:, entries(c0, c1)]),
                                    square[a, t][:, c0:c1], ALU.mult)

        def pick_upper(a, t):
            nc.vector.tensor_tensor(second_term[a][:, t, :], window[a, t][:].indirect(p3[:]), spread[a, t][:], ALU.mult)

        def copy_upper(a, t, c0, c1):
            if c0 == 0 or t < PACK - 1:
                name = "lower%d" % t if (t, c0) == (PACK - 2, 0) else "upper%d" % t
                upper[a, t] = work.tile([P, M], F32, name=name, bufs=1, align_bytes=64)
            nc.scalar.activation(upper[a, t][:, c0:c1], window[a, t][:].indirect(p3[:, entries(c0, c1)]), ACT.Copy)

        def scale_upper(a, t, c0, c1):
            nc.vector.tensor_scalar(second_term[a][:, t, c0:c1], upper[a, t][:, c0:c1], factor[:, a, t:t + 1], None,
                                    ALU.mult)

        woven = [keep.tile([P, M, PACK], BF16, name="woven%d" % a, align_bytes=64) for a in range(2)]
        z_codes = [keep.tile([P, M], U32, name="z_codes%d" % a, align_bytes=64) for a in range(2)]
        z_plane = [keep.tile([P, M], U8, name="z_plane%d" % a, align_bytes=64) for a in range(2)]
        results = {}

        def weave(a, c0, c1):
            nc.vector.tensor_tensor(woven[a][:, c0:c1, :].rearrange("p (c i) t -> p c t i", i=4),
                                    first_term[a][:, :, c0:c1].rearrange("p t (c i) -> p c t i", i=4),
                                    second_term[a][:, :, c0:c1].rearrange("p t (c i) -> p c t i", i=4), ALU.add)

        def quantize_z(a, c0, c1):
            nc.vector.quantize_mx(out=z_codes[a][:, c0:c1].bitcast(FP8X4), scales=z_plane[a][:, c0:c1],
                                  in_=woven[a][:, c0:c1, :].rearrange("p m t -> p (m t)"))

        def second_stage_pass(a, i):
            c0, c1 = PIECES[i]
            share = BLOCKS_IN_BANK[i]
            first_bank = sum(N // P // other for other in BLOCKS_IN_BANK[:i])
            for n in range(N // P):
                k, side = divmod(n, share)
                if a == 0 and side == 0:
                    results[i, k] = psum.tile([P, share, c1 - c0], F32, name="bank%d" % (first_bank + k))
                nc.tensor.matmul_mx(out=results[i, k][:, side, :],
                                    lhsT=w3_codes[:, a, n * P:(n + 1) * P].bitcast(FP8X4),
                                    lhsT_scale=w3_planes[4 * a:P, n * P:(n + 1) * P],
                                    rhs=z_codes[a][:, c0:c1].bitcast(FP8X4), rhs_scale=z_plane[a][:, c0:c1],
                                    start=a == 0 and side == 0, stop=a == 1 and side == share - 1)

        def store(i):
            c0, c1 = PIECES[i]
            share = BLOCKS_IN_BANK[i]
            if i == 0:
                staged = work.tile([P, N // P, c1 - c0], F32, name="lower%d" % (PACK - 1), bufs=1, align_bytes=64)
            else:
                staged = keep.tile([P, N // P, c1 - c0], F32, name="staged%d" % i)
            rows = out[:, c0:c1].rearrange("(n p) m -> p n m", p=P)
            blocks = max(share, 2)
            for n0 in range(0, N // P, blocks):
                for n in range(n0, n0 + blocks, share):
                    on_vector = share == 1 and n % 2 == 0
                    copy = nc.vector.tensor_copy if on_vector else nc.scalar.copy
                    copy(staged[:, n:n + share, :], results[i, n // share][:])
                queue = nc.scalar if i + 1 == len(PIECES) and n0 else nc.sync
                queue.dma_start(rows[:, n0:n0 + blocks, :], staged[:, n0:n0 + blocks, :])

        rounded = shared.tile([P, PACK, P, PACK], BF16, name="w1_rounded10", align_bytes=64, offset=AT_W1_EARLY[1])
        round_w1(nc.vector.tensor_copy, rounded, late_raw[0], 0, P // 2)
        order_w2_plane(1)
        round_w1(nc.vector.tensor_copy, rounded, late_raw[1], P // 2, P, P // 2)
        for a in range(2):
            first_term[a], second_term[a] = new_term("first_term%d" % a), new_term("second_term%d" % a)
            for t in range(PACK):
                leave(a, t)
                if (a, t) == (1, PACK - 1):
                    break
                if (a, t) in spread:
                    pick_upper(a, t)
                pick_lower(a, t, 0, M)
                square_lower(a, t, 0, M)
                if (a, t) == (0, 1):
                    rounded = shared.tile([P, PACK, P, PACK], BF16, name="w1_rounded11", align_bytes=64,
                                          offset=AT_SPREAD)
                    round_w1(nc.vector.tensor_copy, rounded, w1_raw[1, 1], 0, P)
                if (a, t) == (1, 0):
                    weave(0, 0, M)
                pick_hearth(a, t, 0, M)
                if a == 0 and t < 2:
                    quantize_w1(1, t, rounded[:])
                if (a, t) == (1, 0):
                    quantize_z(0, 0, M)
                if a == 0 and t >= 1:
                    for done in range(t + 1) if t == 1 else [t]:
                        multiply(1, done)
        for i in range(len(PIECES)):
            second_stage_pass(0, i)
        for i, (c0, c1) in enumerate(PIECES):
            pick_lower(1, PACK - 1, c0, c1)
            copy_upper(1, PACK - 1, c0, c1)
            if c0 % (M // 2) == 0:
                copy_upper(1, 2, c0, c0 + M // 2)
            square_lower(1, PACK - 1, c0, c1)
            scale_upper(1, PACK - 1, c0, c1)
            if c0 % (M // 2) == 0:
                scale_upper(1, 2, c0, c0 + M // 2)
            pick_hearth(1, PACK - 1, c0, c1)
            if i:
                quantize_z(1, *PIECES[i - 1])
                second_stage_pass(1, i - 1)
            weave(1, c0, c1)
        quantize_z(1, *PIECES[-1])
        second_stage_pass(1, len(PIECES) - 1)
        for i in range(len(PIECES)):
            store(i)
